import numpy as np, ml_dtypes
CORES = [10,34,74,98]
N = 4
BF = ml_dtypes.bfloat16
W, L, B, V, S = 4096, 256, 2, 5, 3
def parts(rng):
    x = rng.integers(0, 256, (N, 8, 16, W))
    pool = rng.integers(0, W, (N, 8, 1, B, L, 6)); q = np.take_along_axis(pool, rng.integers(0, 6, (N, 8, 16, B, L, 2)), 5)
    q[..., 1] = np.where(rng.random((N, 8, 16, B, L)) < 0.5, q[..., 1], rng.integers(0, W, (N, 8, 16, B, L)))
    h = rng.integers(0, W, (N, 8, 16, L)); g = rng.integers(0, W, (N, 8, 16, L)); z = rng.integers(0, 256, (N, 8, 16, L))
    t = rng.choice(np.array([750, 900, 1050, 1200]), (N, 8, 1, 1)) + rng.integers(0, 300, (N, 8, 16, 1))
    return x, q, h, g, z, t
def pack(x, q, h, g, z, t):
    c = lambda a, n: np.ascontiguousarray(np.reshape(a, (N, 128, n))).astype(np.int32)
    return {"xt": c(x, W).astype(np.float32).astype(BF), "qs": c(q, 2 * B * L), "hn": c(h, L), "gt": c(g, L), "zs": c(z, L), "th": c(t, 1)}
def setup_inputs(rng):
    return pack(*parts(rng))
def setup_inputs_spread(rng):
    x, q, h, g, z, t = parts(rng); lg = W.bit_length() - 1
    x = np.minimum((np.exp2(8 * rng.random((N, 8, 1, W))) * rng.random((N, 8, 16, W))).astype(np.int64), 255)
    uneven = lambda *s: np.minimum(np.exp2(lg * rng.random(s)).astype(np.int64), W) - 1
    m = rng.random(q.shape) < 0.6; q = np.where(m, uneven(*q.shape), q); h = uneven(*h.shape); g = np.where(rng.random(g.shape) < 0.5, uneven(*g.shape), g)
    z = np.minimum((np.exp2(8 * rng.random((N, 8, 1, L))) * rng.random((N, 8, 16, L))).astype(np.int64), 255)
    t = np.where(rng.random((N, 8, 16, 1)) < 0.5, rng.integers(0, 4081, (N, 8, 16, 1)), rng.integers(200, 1200, (N, 8, 16, 1)))
    return pack(x, q, h, g, z, t)
def setup_inputs_ends(rng):
    two = lambda *s: rng.integers(0, 2, s)
    kind = rng.integers(0, 3, (N, 8, 1, W)); x = 255 * np.where(kind == 2, two(N, 8, 16, W), kind)
    odd = (np.arange(8) & 1)[None, :, None]; x[..., 0] = 255 * odd; x[..., W - 1] = 255 - 255 * odd
    q = (W - 1) * two(N, 8, 16, B, L, 2); h = (W - 1) * two(N, 8, 16, L); g = (W - 1) * two(N, 8, 16, L)
    kind = rng.integers(0, 3, (N, 8, 1, L)); z = 255 * np.where(kind == 2, two(N, 8, 16, L), kind); z[..., 0] = 0; z[..., L - 1] = 255
    t = 4080 * two(N, 8, 16, 1); t[:, 0::2, 0] = 0; t[:, 1::2, 0] = 4080; t[:, :, 2] = 4080; t[:, :, 15] = 4080
    for l in (0, 5, L - 1):
        for k in (2, 15):
            h[:, :, k, l] = W - 1; g[:, :, k, l] = 0; q[:, :, k, :, l] = 0
    return pack(x, q, h, g, z, t)
def setup_inputs_corners(rng):
    x, q, h, g, z, t = parts(rng); off = int(rng.integers(0, 6))
    for r in range(N):
        for a in range(8):
            o = rng.permutation(16); p = (r + a + off) % 6; e = np.zeros(16, np.int64)
            if p == 0: e[:] = 4080
            if p == 2: e[o[1:]] = 4080
            if p == 3: e[o[0]] = 4080
            if p == 4: e[0] = 4080; e[15] = 4080
            if p == 5: e = rng.choice(np.array([0, 1000, 1365, 4080]), 16)
            t[r, a, :, 0] = e
    q[:, :, :, :, 0::4] = 0; h[..., 0::4] = 0; g[..., 0::4] = 0
    q[:, :, :, :, 1::4] = rng.integers(0, W, (N, 8, 1, 1, len(range(1, L, 4)), 1))
    h[..., 2::4] = q[:, :, :, 0, 2::4, 0]; g[..., 2::4] = q[:, :, :, 0, 2::4, 1]
    z[..., 0:2] = 0; z[..., L - 2:] = 255
    return pack(x, q, h, g, z, t)
def setup_inputs_ties(rng):
    x, q, h, g, z, t = parts(rng)
    x = rng.integers(0, 253, (N, 8, 16, 1)) + rng.integers(0, 4, (N, 8, 16, W)) * (rng.random((N, 8, 16, W)) < 0.25)
    t = rng.integers(0, 10, (N, 8, 16, 1))
    return pack(x, q, h, g, z, t)
def setup_inputs_high(rng):
    x, q, h, g, z, t = parts(rng); near = lambda *s: rng.integers(W - 32, W, s)
    gap = rng.choice(np.array([130, 180, 252]), (N, 8, 1, 1))
    x = gap * rng.integers(0, 2, (N, 8, 1, W)) + rng.integers(0, 4, (N, 8, 16, W)) * (rng.random((N, 8, 16, W)) < 0.25)
    t = np.where(rng.random((N, 8, 16, 1)) < 0.25, rng.integers(0, 40, (N, 8, 16, 1)), 16 * gap + rng.integers(-12, 13, (N, 8, 16, 1)))
    d = rng.choice(np.array([3, 5]), (N, 8, 1, L)); one = np.arange(16)[:, None] == rng.integers(0, 16, (N, 8, 1, L))
    z = np.where(rng.random((N, 8, 1, L)) < 0.75, 255 - d * one, rng.integers(250, 256, (N, 8, 16, L)))
    tail = np.where(d == 5, W - 3, W - 5)[:, :, :, None]; name = np.where(d == 5, W - 21, W - 19)[:, :, :, None]
    q[..., 1] = np.where(rng.random((N, 8, 16, B, L)) < 0.75, tail, near(N, 8, 16, B, L))
    q[..., 0] = np.where(rng.random((N, 8, 16, B, L)) < 0.5, name, near(N, 8, 16, B, L))
    ab = np.array([[W - 5, W - 19], [W - 3, W - 21], [W - 19, W - 5], [W - 21, W - 3]])[rng.integers(0, 4, (N, 8, 16, L))]
    m = rng.random((N, 8, 16, L)) < 0.5; h = np.where(m, ab[..., 0], near(N, 8, 16, L)); g = np.where(m, ab[..., 1], near(N, 8, 16, L))
    return pack(x, q, h, g, z, t)
def check_inputs(d):
    bad = []
    for k, lo, hi in (("xt", 0, 255), ("qs", 0, W - 1), ("hn", 0, W - 1), ("gt", 0, W - 1), ("zs", 0, 255), ("th", 0, 4080)):
        v = np.asarray(d[k]).astype(np.float32)
        if not (np.min(v) >= lo and np.max(v) <= hi): bad.append("range of " + k)
        elif np.any(v != np.floor(v)): bad.append("whole numbers in " + k)
    return bad
def rec(x, a, b):
    ix = ((a * b >> 5) + a + 37 * b) & (W - 1)
    return np.take_along_axis(x, ix.reshape(N, 8, 1, 16 * L), 3).reshape(N, 8, 16, 16, L)
def reference(xt, qs, hn, gt, zs, th):
    x0 = xt.astype(np.float32).astype(np.int32).reshape(N, 8, 16, W); q = qs.astype(np.int64).reshape(N, 8, 16, B, L, 2)
    h = hn.astype(np.int64).reshape(N, 8, 16, L); g = gt.astype(np.int64).reshape(N, 8, 16, L); z = zs.astype(np.int64).reshape(N, 8, 16, L)
    lim = th.astype(np.int64).reshape(N, 8, 16, 1); cnt = np.zeros((N, 8, 1, L), np.int64); row = np.arange(16); prev = None
    for v in range(V):
        u = np.add.reduce(z, axis=2)[:, :, None]
        cal = u & (B - 1); rf = np.take_along_axis(q, cal[:, :, :, None, :, None], 3)[:, :, :, 0]
        R = rf[..., 0]; F = rf[..., 1]; x = rec(x0, h, g)
        usek = np.zeros((N, 8, 16, L), bool); usej = np.zeros((N, 8, 16, L), bool); mate = np.zeros((N, 8, 16, L), np.int64); top = np.full((N, 8, 16, L), -1, np.int64)
        for s in range(S):
            j = (row + 5 * s + v) & 15
            y = rec(x0, R[:, :, j], F[:, :, j]); dist = np.add.reduce(np.abs(x - y), axis=2)
            m = (dist < lim + cnt) & ~usek & ~usej[:, :, j]
            top = np.maximum(top, np.max(np.where(m[:, :, None], y, -1), axis=3))
            usek = usek | m; usej[:, :, j] = usej[:, :, j] | m; mate = np.where(m, j[None, None, :, None], mate)
            hit = np.any(m, axis=2)[:, :, None]; low = np.argmax(m, axis=2)[:, :, None]
            old = np.take_along_axis(R[:, :, j], low, 2); new = np.take_along_axis(h, low, 2)
            R = np.where(hit & (R == old), new, R); F = np.where(hit & (F == old), new, F)
        fj = np.take_along_axis(F, mate, 2); g = np.where(usek, ((fj * u >> 5) + fj) & (W - 1), g)
        if v > 0:
            Rb = np.roll(R, -1, axis=0); Fb = np.roll(F, -1, axis=0); ub = np.roll(usej, -1, axis=0)
            for b in range(B):
                put = (prev == b) & ~ub
                q[:, :, :, b, :, 0] = np.where(put, Rb, q[:, :, :, b, :, 0]); q[:, :, :, b, :, 1] = np.where(put, Fb, q[:, :, :, b, :, 1])
        cnt = np.add.reduce(usek.astype(np.int64), axis=2)[:, :, None]; z = np.where(cnt > 0, (z + top) >> 1, z); prev = cal
        if v < V - 1:
            h = np.roll(h, 1, axis=0); g = np.roll(g, 1, axis=0); z = np.roll(z, 1, axis=0); cnt = np.roll(cnt, 1, axis=0)
    return {"yq": q.reshape(N, 128, 2 * B * L).astype(np.float32), "yg": g.reshape(N, 128, L).astype(np.float32), "yz": z.reshape(N, 128, L).astype(np.float32)}

@@ -1,0 +1,577 @@
+import numpy as np
+from concourse.mybir import AluOpType as ALU, ActivationFunctionType as ACT
+
+NR, NV, NS = 4, 5, 3
+F32, BF, I32, U16, F16 = "float32", "bfloat16", "int32", "uint16", "float16"
+SB = {
+    "XT": (4112, BF), "HN": (256, I32), "GT": (256, I32), "ZS": (256, I32), "QS": (1024, I32), "TH": (4, I32),
+    "THF": (4, F32), "HRF": (4 * 768, F16), "GIN": (5 * 256, F16), "GOUT": (4 * 256, F16), "GL": (256, F32),
+    "ZI": (5 * 512, BF), "ZO": (4 * 512, BF), "ZF": (256, F32), "BK": (5 * 512, F16), "BO": (5 * 512, F16),
+    "W": (1024, F32), "X": (4096, BF), "D": (4096, BF), "AB": (4096, BF),
+    "OX": (256, U16), "OY": (256, U16), "OM": (256, U16), "OC": (5 * 32, U16),
+    "IA": (256, I32), "IB": (256, I32), "IC": (256, I32), "IZ": (256, I32), "IT": (32, I32),
+    "TM": (768, F32), "M": (768, BF), "F2": (512, F16), "EQ": (512, BF), "TT": (512, F32),
+    "FT": (768, F32), "GF": (256, F32), "ZN": (256, BF), "U": (256, F32), "RFI": (512, F16), "EB": (5 * 512, BF),
+    "V": (144, I32), "VB": (128, I32), "VP": (4, I32), "PC": (4, F32), "VJ": (16, F32), "JT": (16, F32), "JW": (144, F32),
+    "B32": (128, F32), "PM": (8 * 128, F16), "C32": (3 * 128, F32), "C16": (5 * 128, F16), "CB": (10 * 128, BF),
+    "NK": (16 * 128, BF), "Z1": (144, BF), "Z2": (144, BF), "ZT": (144, F32), "T1": (128, F32), "T2": (128, F32),
+    "RS": (1024, BF), "ET": (512, BF), "C05": (256, BF), "C37": (256, BF),
+}
+SCRATCH = {k: ("sbuf", [128, n], d) for k, (n, d) in SB.items()}
+for _b in range(8):
+    SCRATCH["P%d" % _b] = ("psum", [128, 512], F32)
+ROT = [0, 1, 2, 3, 4, 5, 6, 11]
+BIG = 8192.0
+REG = {
+    2: dict(c=(0, 0), mP=(0, 1), old=(0, 2), dl=(0, 3), P2=(1, 0), lin=(1, 2), ft=(1, 0), P4=(2, 0), PB=(2, 2), ut=(2, 2),
+            u=(2, 3), pd=(3, 0), X1=(3, 0), X2=(3, 1), zn=(3, 2), mg=(3, 0), o2=(0, 2), d2=(1, 2)),
+    4: dict(c=(0, 0), mP=(0, 1), old=(0, 2), dl=(0, 3), P2=(0, 4), lin=(0, 6), ft=(0, 4), P4=(1, 0), PB=(1, 2), ut=(1, 2),
+            u=(1, 3), pd=(1, 4), X1=(1, 4), X2=(1, 5), zn=(1, 6), mg=(1, 4), o2=(0, 2), d2=(0, 6)),
+}
+
+PARAMS = dict(ns=2, modes=[[("a", 64), ("a", 32), ("d", 32)]] * 3, sch=64, seed=0, iters=1500,
+              x0=[("act", 32), ("dve", 32)] * 2, xs=[("act", 32)] * 4, ts=[("act", 32), ("dve", 32)] * 2,
+              t4=[("act", 32), ("dve", 32)] * 2, act16=True, early=True, lead=8000.0, dup=True)
+COST = dict(f=1.25, gc=1.56, pe=0.42, ov=50.0, hop=100.0, same=60.0, net=4000.0, iss=800.0, bw=200.0)
+
+
+def A(name, a, n, step=1, ind=None):
+    return (name, a, a + (n - 1) * step + 1, step, ind)
+
+
+def is_ap(x):
+    return isinstance(x, tuple)
+
+
+def width(ap):
+    return 16 * (ap[4][2] - ap[4][1]) if ap[4] else (ap[2] - ap[1] - 1) // ap[3] + 1
+
+
+def build(par):
+    ops = []
+    hist = {}
+    bank = {}
+    cur = [-1]
+    nst = par["ns"]
+    LN = 256 // nst
+
+    def add(eng, ins, reads, writes, sem=None, peer=0, nbytes=0):
+        i = len(ops)
+        deps, order = set(), set()
+        rd = [r for r in reads if is_ap(r)]
+        rd += [r[4] for r in rd + writes if r[4]]
+        for lst, w in ((rd, False), (writes, True)):
+            for ap in lst:
+                nm = ap[0]
+                if nm not in SB:
+                    if nm[0] != "P":
+                        continue
+                    st = bank.setdefault(nm, [None, [], []])
+                    if st[0] != eng:
+                        st[0], st[1], st[2] = eng, [], st[1]
+                    deps.update(st[2])
+                    if eng == "pe":
+                        order.update(st[1][-1:])
+                    if i not in st[1]:
+                        st[1].append(i)
+                    if eng == "pe":
+                        continue
+                h = hist.setdefault(nm, [])
+                keep = []
+                for e in h:
+                    hit = e[1] < ap[2] and ap[1] < e[2]
+                    if hit and (w or e[3]):
+                        deps.add(e[0])
+                    if not (w and ap[3] == 1 and ap[1] <= e[1] and e[2] <= ap[2]):
+                        keep.append(e)
+                keep.append((i, ap[1], ap[2], w))
+                hist[nm] = keep
+        deps.discard(i)
+        order.discard(i)
+        ops.append(dict(eng=eng, ins=ins, deps=deps, order=order - deps, sem=sem, peer=peer, nbytes=nbytes, st=cur[0]))
+
+    def tt(o, a, b, op): add("dve", [("tt", o, a, b, op)], [a, b], [o])
+    def ts(o, a, s1, op0, s2=None, op1=None): add("dve", [("ts", o, a, s1, s2, op0, op1)], [a, s1, s2], [o])
+    def cp(o, a): add("dve", [("cp", o, a)], [a], [o])
+    def ms(o, c): add("dve", [("ms", o, c)], [], [o])
+    def act(o, a, fn, bias=0.0, scale=1.0): add("act", [("act", o, a, fn, bias, scale)], [a, bias, scale], [o])
+    def gat(o, a, eng): add(eng, [("gat", o, a)], [a], [o])
+    def iota(o, pat, base, cm): add("pool", [("iota", o, pat, base, cm)], [], [o])
+
+    def mm(terms, first=True, last=True):
+        ins = [("mm", o, l, r, first and j == 0, last and j == len(terms) - 1) for j, (o, l, r) in enumerate(terms)]
+        add("pe", ins, [x for t in terms for x in t[1:]], [t[0] for t in terms])
+
+    def dma(o, a, sem, nbytes, eng="sp"): add(eng, [("dma", o, a)], [a], [o], sem=sem, nbytes=nbytes)
+    def send(o, a, sem, peer): add("pool", [("send", o, a)], [a], [o], sem=sem, peer=peer)
+
+    def to16(o, a, bias=0.0):
+        if par["act16"]:
+            act(o, a, ACT.Identity, bias=bias)
+        else:
+            ts(o, a, bias, ALU.add)
+
+    def index(off, tmp, a, b, lin, mid=None):
+        tt(tmp, a, b, ALU.mult)
+        if mid:
+            mid()
+        ts(tmp, tmp, 5, ALU.arith_shift_right)
+        tt(tmp, tmp, lin, ALU.add)
+        ts(tmp, tmp, 4095, ALU.bitwise_and)
+        if off:
+            cp(off, tmp)
+
+    for nm, src, n in (("ZS", "zs", 256), ("QS", "qs", 1024), ("HN", "hn", 256), ("GT", "gt", 256)):
+        dma(A(nm, 0, n), A(src, 0, n), "l" + src, 512 * n)
+    dma(A("XT", 0, 4096), A("xt", 0, 4096), "lxt", 1 << 20)
+    iota(A("V", 0, 144), [[1, 144]], 128, -1)
+    iota(A("VB", 0, 128), [[16, 8], [0, 16]], 15, -1)
+    iota(A("VP", 0, 1), [[0, 1]], 0, 1)
+    iota(A("VJ", 0, 16), [[16, 16]], 0, 0)
+    dma(A("TH", 0, 1), A("th", 0, 1), "lth", 512, eng="pool")
+    iota(A("RS", 0, 1024), [[0, 64], [256, 16]], 0, 0)
+    ts(A("VP", 0, 1), A("VP", 0, 1), 15, ALU.bitwise_and)
+    PC = A("PC", 0, 1)
+    cp(PC, A("VP", 0, 1))
+    ts(A("JT", 0, 16), A("VJ", 0, 16), PC, ALU.add)
+    ts(A("ZT", 0, 144), A("V", 0, 144), PC, ALU.add, 143.0, ALU.is_equal)
+    act(A("Z1", 0, 144), A("ZT", 0, 144), ACT.Copy)
+    tt(A("JW", 0, 143), A("ZT", 0, 143), A("ZT", 1, 143), ALU.add)
+    act(A("Z2", 0, 143), A("JW", 0, 143), ACT.Identity, scale=2.0 * LN)
+    V0, B32 = A("V", 0, 128), A("B32", 0, 128)
+    ts(A("VB", 0, 128), A("VB", 0, 128), 4, ALU.arith_shift_right)
+    ts(B32, A("VB", 0, 128), 0.0, ALU.is_equal)
+    ts(A("T1", 0, 128), V0, -8192.0, ALU.mult, 128 * 8192.0 + 4096.0, ALU.add)
+    ts(A("T2", 0, 128), V0, 128.0, ALU.is_ge)
+    tt(A("T1", 0, 128), A("T1", 0, 128), A("T2", 0, 128), ALU.mult)
+    CB = {k: A("CB", 128 * j, 128) for j, k in enumerate(("T", "I", "nI", "B", "nB256", "K0", "K5", "K10", "nK4", "B64"))}
+    tt(CB["T"], A("T1", 0, 128), B32, ALU.mult)
+    ts(A("V", 0, 144), A("V", 0, 144), 15, ALU.bitwise_and)
+    ts(A("JW", 0, 144), A("V", 0, 144), 0.0, ALU.is_equal)
+    PM = {r: A("PM", 128 * j, 128) for j, r in enumerate(ROT)}
+    I32m, P5w, nKB = A("C32", 0, 128), A("C32", 128, 128), A("C32", 256, 128)
+    I65, I101, nI, B16, nB16 = (A("C16", 128 * j, 128) for j in range(5))
+    tt(I32m, B32, A("JW", 0, 128), ALU.mult)
+    for o, a, c in ((I65, I32m, 65.0), (I101, I32m, 101.0), (B16, B32, 1.0), (nB16, B32, -1.0), (nI, I32m, -1.0)):
+        ts(o, a, c, ALU.mult)
+    for r in ROT:
+        tt(PM[r], B32, A("JW", r, 128), ALU.mult)
+    tt(P5w, B32, A("JW", 5, 128), ALU.mult)
+    tt(A("T2", 0, 128), B32, A("JW", 10, 128), ALU.mult)
+    for o, a, c in ((CB["I"], I32m, 1.0), (CB["nI"], I32m, -1.0), (CB["B"], B32, 1.0), (nKB, B32, -BIG),
+                    (CB["K0"], I32m, BIG), (CB["K5"], P5w, BIG), (CB["K10"], A("T2", 0, 128), BIG),
+                    (CB["nB256"], B32, -256.0), (CB["nK4"], I32m, -4096.0), (CB["B64"], B32, 64.0)):
+        act(o, a, ACT.Identity, scale=c)
+    NK = {r: A("NK", 128 * r, 128) for r in range(16)}
+    for r in (0, 5, 10, 15, 4, 9, 14, 3, 8, 13, 2, 7, 12):
+        tt(NK[r], nKB, A("JW", r, 128), ALU.mult)
+    ms(A("XT", 4096, 16), 0.0)
+    ms(A("ET", 0, 2 * LN), -2048.0)
+    ms(A("ET", 2 * LN, 2 * LN), BIG - 2048.0)
+    ms(A("C05", 0, 256), 0.5)
+    ms(A("C37", 0, 256), 3.75)
+    TH = A("THF", 0, 1)
+    cp(TH, A("TH", 0, 1))
+    KR = {0: CB["K0"], 5: CB["K5"], 10: CB["K10"]}
+    XW, XZ = ("XT", 0, 4096, 1), ("XT", 0, 4112, 1)
+
+    for s in range(nst):
+        l0 = s * LN
+        cp(A("ZI", 2 * l0, LN), A("ZS", l0, LN))
+        ms(A("ZI", 2 * l0 + LN, LN), 0.0)
+        ts(A("HRF", 3 * l0, LN), A("HN", l0, LN), -2048.0, ALU.add)
+        for b in range(2):
+            cp(A("W", 4 * l0 + 2 * LN * b, 2 * LN), A("QS", 512 * b + 2 * l0, 2 * LN))
+    ts(A("GIN", 0, 256), A("GT", 0, 256), -2048.0, ALU.add)
+    for d in range(1, NR):
+        for s in range(nst):
+            send(A("HRF", 768 * d + 3 * LN * s, LN), A("HRF", 3 * LN * s, LN), "h%d%d" % (d, s), d)
+
+    for t in range(NV):
+        for s in range(nst):
+            cur[0] = s
+            l0 = s * LN
+            c0 = 16 * l0
+
+            def pr(name, off=0, n=LN, step=1):
+                bk, col = REG[nst][name]
+                return A("P%d" % (8 // nst * s + bk), col * LN + off, n, step)
+
+            h0 = 768 * (t % NR) + 3 * l0
+            H, R, F = A("HRF", h0, LN), A("HRF", h0 + LN, LN), A("HRF", h0 + 2 * LN, LN)
+            HR, RF = A("HRF", h0, 2 * LN), A("HRF", h0 + LN, 2 * LN)
+            G = A("GIN", 256 * t + l0, LN)
+            z0 = 512 * t + 2 * l0
+            Z, CNT = A("ZI", z0, LN), A("ZI", z0 + LN, LN)
+            Ms = [A("M", 3 * l0 + LN * k, LN) for k in range(NS)]
+            TMs = [A("TM", 3 * l0 + LN * k, LN) for k in range(NS)]
+            IA, IB, IC, IZ = (A(n, l0, LN) for n in ("IA", "IB", "IC", "IZ"))
+            lin = pr("lin")
+            Wn = ("W", 4 * l0, 4 * l0 + 4 * LN, 1)
+            mm([(lin, I65, H), (lin, I101, G)])
+            index(A("OX", l0, LN), IB, H, G, lin)
+            a = 0
+            for eng, n in par["x0" if t == 0 else "xs"]:
+                gat(A("X", c0 + 16 * a, 16 * n), XW + (A("OX", l0 + a, n),), eng)
+                a += n
+            nt = LN // 8
+            ut, IT, OC = pr("ut", 0, nt), A("IT", nt * s, nt), A("OC", 32 * t + nt * s, nt)
+            mm([(ut, A("Z2", 14 - 2 * a, 128), A("ZI", z0 + a, nt, 8)) for a in range(8)])
+            tt(IT, ut, A("JT", 0, nt), ALU.add)
+            ts(IT, IT, 4 * LN - 1, ALU.bitwise_and)
+            cp(OC, IT)
+            to16(A("RFI", 2 * l0, 2 * LN), Wn + (OC,), -2048.0)
+            P4 = pr("P4", 0, 2 * LN)
+            for hf in range(2):
+                mm([(pr("P4", LN * hf), PM[t], A("RFI", 2 * l0 + hf, LN, 2))])
+            for k in range(NS):
+                to16(RF, P4)
+                mm([(lin, I65, R), (lin, I101, F)])
+                index(A("OY", l0, LN), IA, pr("P4"), F, lin)
+                if k == 0:
+                    U = A("U", l0, LN)
+                    mm([(pr("u"), CB["B"], Z)])
+                    act(U, pr("u"), ACT.Identity, bias=32.0)
+                    if t < NV - 1:
+                        act(A("EB", 512 * t + 2 * l0, 2 * LN), ("ET", 0, 4 * LN, 1, OC), ACT.Copy)
+                P2 = pr("P2", 0, 2 * LN)
+                e2, e4 = [(P2, PM[0], HR)], [(P4, PM[5 if k < NS - 1 else 0], RF)]
+                if par["early"]:
+                    mm(e2, last=False)
+                    mm(e4, last=False)
+                    e2, e4 = [], []
+                c = pr("c")
+                mm([(c, CB["nI"], CNT)] + [(c, KR[r], Ms[j]) for j in range(k) for r in (0, 5 * (k - j))], last=False)
+                a, done, extra = 0, 0, []
+                for mode, n in par["modes"][k]:
+                    y = XW + (A("OY", l0 + a, n),)
+                    x, d, ab = (A(nm, c0 + 16 * a, 16 * n) for nm in ("X", "D", "AB"))
+                    if mode == "d":
+                        act(d, y, ACT.Copy)
+                        pd = pr("pd", 0, 16 * n)
+                        mm([(pd, CB["nI"], x), (pd, CB["I"], d)])
+                        act(ab, pd, ACT.Abs)
+                    else:
+                        tt(d, y, x, ALU.subtract)
+                        if mode == "a":
+                            act(ab, d, ACT.Abs)
+                        else:
+                            ts(ab, d, -2.0, ALU.mult, 0.0, ALU.max)
+                            extra.append((a, n))
+                    a += n
+                    if a - done >= 64 or a == LN:
+                        for ea, en in extra:
+                            mm([(pr("c", ea, en), A("Z1", 15 - j, 128), A("D", c0 + 16 * ea + j, en, 16)) for j in range(16)],
+                               first=False, last=False)
+                        mm([(pr("c", done, a - done), A("Z1", 15 - j, 128), A("AB", c0 + 16 * done + j, a - done, 16))
+                            for j in range(16)], first=False, last=a == LN)
+                        done, extra = a, []
+                ts(Ms[k], c, TH, ALU.is_lt)
+                mm(e2 + [(pr("P2", LN * hf), CB["T"], Ms[k]) for hf in range(2)], first=not par["early"])
+                fH, fR = A("F2", 2 * l0, LN), A("F2", 2 * l0 + LN, LN)
+                ts(A("F2", 2 * l0, 2 * LN), P2, -4096.0, ALU.add, -2048.0, ALU.max)
+                mP, old, dl = pr("mP"), pr("old"), pr("dl")
+                if par["dup"]:
+                    mm([(pr("o2", 0, 2 * LN), KR[0], A("C37", 0, 2 * LN))] + [(pr("o2", LN * hf), B16, fR) for hf in range(2)])
+                    for hf in range(2):
+                        mm([(pr("d2", LN * hf), B16, fH), (pr("d2", LN * hf), nB16, fR)])
+                    mm([(mP, CB["I"], Ms[k])])
+                    EQ = A("EQ", 2 * l0, 2 * LN)
+                    tt(EQ, RF, pr("o2", 0, 2 * LN), ALU.is_equal)
+                    tt(A("TT", 2 * l0, 2 * LN), EQ, pr("d2", 0, 2 * LN), ALU.mult)
+                else:
+                    mm([(mP, CB["I"], Ms[k])])
+                    mm([(old, KR[0], A("C37", 0, LN)), (old, B16, fR)])
+                    mm([(dl, B16, fH), (dl, nB16, fR)])
+                    for hf, src in enumerate((R, F)):
+                        tt(A("EQ", 2 * l0 + LN * hf, LN), src, old, ALU.is_equal)
+                    for hf in range(2):
+                        tt(A("TT", 2 * l0 + LN * hf, LN), A("EQ", 2 * l0 + LN * hf, LN), dl, ALU.mult)
+                tt(TMs[k], IA, mP, ALU.mult)
+                mm(e4 + [(P4, P5w if k < NS - 1 else I32m, A("TT", 2 * l0, 2 * LN))], first=not par["early"])
+            zn, ZN, pz = pr("zn"), A("ZN", l0, LN), pr("old")
+            mm([(zn, CB["I"], Z)] + [(zn, CB["nB256"], m) for m in Ms])
+            act(ZN, zn, ACT.Relu)
+            to16(RF, P4)
+            for k, r in enumerate((6, 11, 0)):
+                o = pr("ft", LN * k)
+                mm([(o, KR[0], Ms[k]), (o, PM[r], F)])
+            o = pr("ft", 3 * LN)
+            mm([(o, PM[0], G)] + [(o, NK[0], m) for m in Ms])
+            act(A("FT", 3 * l0, 3 * LN), pr("ft", 0, 3 * LN), ACT.Relu, bias=2048.0 - BIG)
+            GF = A("GF", l0, LN)
+            act(GF, o, ACT.Relu, bias=2048.0)
+            FT = [A("FT", 3 * l0 + LN * k, LN) for k in range(NS)]
+            X1, X2 = pr("X1"), pr("X2")
+            C05 = A("C05", 0, LN)
+            mm([(X1, CB["nK4"], C05)] + [(X1, I32m, f) for f in FT])
+            mm([(X2, CB["nK4"], C05), (X2, CB["B64"], Z), (X2, I32m, GF)])
+            index(None, IC, U, X1, X2)
+            if t < NV - 1:
+                GO = A("GOUT", 256 * t + l0, LN)
+                ts(GO, IC, -2048.0, ALU.add)
+                send(A("GIN", 256 * (t + 1) + l0, LN), GO, "g%d%d" % (t, s), 1)
+            else:
+                GO = A("GL", l0, LN)
+                cp(GO, IC)
+                dma(A("yg", l0, LN), GO, "sg%d" % s, 512 * LN)
+            if t > 0:
+                for hf, src in enumerate((R, F)):
+                    o = pr("PB", hf, LN, 2)
+                    mm([(o, NK[16 - 5 * j - t], Ms[j]) for j in range(NS)] + [(o, PM[6 - t], src)])
+                BO, BK = A("BO", 512 * t + 2 * l0, 2 * LN), A("BK", 512 * t + 2 * l0, 2 * LN)
+                to16(BO, pr("PB", 0, 2 * LN))
+                send(BK, BO, "b%d%d" % (t, s), NR - 1)
+            mi = pr("mP")
+            mm([(mi, CB["nK4"], m) for m in Ms] + [(mi, I32m, m) for m in TMs])
+            if t < NV - 1:
+                mm([(pr("c"), CB["B"], m) for m in Ms])
+            ts(A("OM", l0, LN), mi, 4096.0, ALU.add)
+            if t < NV - 1:
+                act(A("ZO", z0 + LN, LN), pr("c"), ACT.Copy)
+            a = 0
+            for eng, n in par["t4" if t == NV - 1 else "ts"]:
+                gat(A("D", c0 + 16 * a, 16 * n), XZ + (A("OM", l0 + a, n),), eng)
+                a += n
+            for a in range(0, LN, par["sch"]):
+                o, i0, i1 = (A(nm, b + 16 * a, 16 * par["sch"]) for nm, b in (("AB", c0), ("RS", -16 * a), ("D", c0)))
+                add("dve", [("scan", o, i0, i1)], [i0, i1], [o])
+            mm([(pz, CB["I"], Z), (pz, CB["I"], ZN), (pz, CB["I"], A("AB", c0 + 15, LN, 16))])
+            ts(IZ, pz, 0.5, ALU.mult, -0.25, ALU.add)
+            if t < NV - 1:
+                cp(A("ZO", z0, LN), IZ)
+                send(A("ZI", z0 + 512, 2 * LN), A("ZO", z0, 2 * LN), "z%d%d" % (t, s), 1)
+            else:
+                cp(A("ZF", l0, LN), IZ)
+                dma(A("yz", l0, LN), A("ZF", l0, LN), "sz%d" % s, 512 * LN)
+            if t > 0:
+                EB, o0, o1 = A("EB", 512 * (t - 1) + 2 * l0, 2 * LN), pr("mg", 0, 2 * LN), pr("mg", 2 * LN, 2 * LN)
+                mm([(o0, CB["I"], EB), (o0, nI, BK)])
+                mm([(o1, CB["nI"], EB), (o1, KR[0], A("C05", 0, 2 * LN)), (o1, nI, BK)])
+                Wa = A("W", 4 * l0, 4 * LN)
+                tt(Wa, Wa, pr("mg", 0, 4 * LN), ALU.min)
+                act(Wa, Wa, ACT.Abs)
+                if t == NV - 1:
+                    for b in range(2):
+                        dma(A("yq", 512 * b + 2 * l0, 2 * LN), A("W", 4 * l0 + 2 * LN * b, 2 * LN), "sq%d%d" % (s, b), 1024 * LN)
+    return ops
+
+
+def size(ap):
+    return 2 if ap[0] in SB and SB[ap[0]][1] in (BF, U16, F16) else 4
+
+
+def cost(op, eng, C):
+    cy, i = 0.83 * C["f"], op["ins"][0]
+    k = i[0]
+    if k == "mm":
+        return sum(max(64, width(j[3])) * (4 if size(j[3]) == 4 else 1) for j in op["ins"]) * C["pe"] * C["f"] + 20, 0
+    if k == "dma":
+        return (100 if eng == "sp" else 1500), 2000
+    if k == "send":
+        return C["iss"], C["net"]
+    n = width(i[1])
+    if k == "iota":
+        return 130 + 2 * n * cy, 0
+    aps = [x for x in i[1:] if is_ap(x) and (x[4] or width(x) > 1 or n == 1)]
+    if any(x[4] for x in aps):
+        return (50 if eng == "dve" else 65) + C["gc"] * n * cy, 0
+    if eng == "act":
+        return C["ov"] + 15 + n * cy, 0
+    c = 0.5 if all(size(x) == 2 for x in aps) else 1.0
+    if k == "tt" and i[2][0] in SB and i[3][0] in SB:
+        c = 2.0
+    return C["ov"] + max(64, n * c) * cy, 0
+
+
+def place(n, seq, pred, dur, engs):
+    st = [0.0] * n
+    line = {e: [] for e in set(engs)}
+    for i in seq:
+        t = 0.0
+        for d, lag in pred[i]:
+            x = st[d] + dur[d] + lag
+            if x > t:
+                t = x
+        l = line[engs[i]]
+        lo, hi = 0, len(l)
+        while lo < hi:
+            mid = (lo + hi) // 2
+            if l[mid][1] <= t:
+                lo = mid + 1
+            else:
+                hi = mid
+        while lo < len(l) and l[lo][0] < t + dur[i]:
+            t = max(t, l[lo][1])
+            lo += 1
+        l.insert(lo, (t, t + dur[i]))
+        st[i] = t
+    return st
+
+
+def schedule(ops, par, C):
+    n = len(ops)
+    engs = [o["eng"] for o in ops]
+    dur, lat, cum = [0.0] * n, [0.0] * n, 0.0
+    for i, o in enumerate(ops):
+        dur[i], lat[i] = cost(o, engs[i], C)
+        if o["ins"][0][0] == "dma":
+            cum = (cum if o["st"] < 0 else 0.0) + o["nbytes"] / C["bw"]
+            lat[i] += cum
+    pred, succ = [[] for _ in range(n + 1)], [[] for _ in range(n + 1)]
+    last = None
+    for i, o in enumerate(ops):
+        e = [(d, lat[d] + (C["hop"] if ops[d]["sem"] or engs[d] != engs[i] else 0 if engs[i] == "pe" else C["same"])) for d in o["deps"]]
+        e += [(d, 0.0) for d in o["order"]]
+        if engs[i] == "sp" and o["st"] < 0:
+            e += [(last, 0.0)] if last is not None else []
+            last = i
+        for d, lag in e:
+            pred[i].append((d, lag))
+            succ[d].append((i, lag))
+        pred[n].append((i, lat[i]))
+        succ[i].append((n, lat[i]))
+    dur, engs = dur + [1.0], engs + ["end"]
+    rng = np.random.default_rng(par["seed"])
+    pr = [0.0] * (n + 1)
+    for i in range(n - 1, -1, -1):
+        pr[i] = dur[i] + max(pr[j] + lag for j, lag in succ[i])
+    key = [-pr[i] + (par["lead"] * max(ops[i]["st"], 0) if i < n else 0) for i in range(n + 1)]
+
+    def forth(key):
+        return place(n + 1, topo_order(n + 1, pred, succ, key), pred, dur, engs)
+
+    def again(st):
+        bk = place(n + 1, topo_order(n + 1, succ, pred, [-(st[i] + dur[i]) for i in range(n + 1)]), succ, dur, engs)
+        return forth([-(bk[i] + dur[i]) for i in range(n + 1)])
+
+    now = forth(key)
+    for _ in range(4):
+        now = again(now)
+    best = now
+    for _ in range(par["iters"]):
+        a = np.array(now)
+        near = np.abs(a - rng.random() * now[n]) < 20000.0
+        st = again(forth((a + near * rng.random(n + 1) * 3000.0 * rng.random()).tolist()))
+        if st[n] <= now[n] + 300.0 * rng.random():
+            now = st
+        if now[n] < best[n]:
+            best = now
+    order = {e: [] for e in ("pe", "dve", "act", "pool", "sp")}
+    for i in sorted(range(n), key=lambda i: (best[i], i)):
+        order[engs[i]].append(i)
+    return order, engs[:n], best
+
+
+def topo_order(n, pred, succ, key):
+    rank = sorted(range(n), key=lambda i: (key[i], i))
+    seq, done = [], [False] * n
+    for i in rank:
+        stack = [i]
+        while stack:
+            j = stack[-1]
+            if done[j]:
+                stack.pop()
+                continue
+            todo = [d for d, _ in pred[j] if not done[d]]
+            if todo:
+                stack.extend(sorted(todo, key=lambda d: -key[d]))
+            else:
+                done[j] = True
+                seq.append(j)
+                stack.pop()
+    return seq
+
+
+OPS = build(PARAMS)
+ORDER, ENGS, _T = schedule(OPS, PARAMS, COST)
+SEMAPHORES = ["pe", "dve", "act", "pool", "sent"] + [o["sem"] for o in OPS if o["sem"]]
+
+
+def rank_program(g, core, T, topo):
+    rank = T.rank_of(core)
+    if rank is None:
+        return
+    q = dict(pe=g.tensor, dve=g.vector, act=g.scalar, pool=g, sp=g.sync)
+
+    def ap(x):
+        if not is_ap(x):
+            return x
+        v = T[x[0]][:, x[1]:x[2]:x[3]] if x[3] > 1 else T[x[0]][:, x[1]:x[2]]
+        return v.indirect(ap(x[4])) if x[4] else v
+
+    def engines(o, src_rank):
+        return len(topo.engines(T.cores[src_rank % NR], T.cores[(src_rank + o["peer"]) % NR]))
+
+    needed = set()
+    for i, o in enumerate(OPS):
+        needed.update(d for d in o["deps"] if not (ENGS[d] == "pe" and ENGS[i] == "pe"))
+    mark, total = {}, {}
+    for e, l in ORDER.items():
+        for i in l:
+            o = OPS[i]
+            if o["sem"]:
+                n = engines(o, rank - o["peer"]) if o["peer"] else 16
+                mark[i] = (o["sem"], n)
+                total[o["sem"]] = n
+            elif i in needed:
+                total[e] = total.get(e, 0) + 1
+                mark[i] = (e, total[e])
+    sent = 0
+    for e, l in ORDER.items():
+        seen = {}
+        for i in l:
+            o = OPS[i]
+            want = {}
+            for d in o["deps"]:
+                if not (e == "pe" and ENGS[d] == "pe"):
+                    sm, n = mark[d]
+                    want[sm] = max(want.get(sm, 0), n)
+            for sm in sorted(want):
+                if seen.get(sm, 0) < want[sm]:
+                    q[e].wait_ge(T.sem[sm], want[sm])
+                    seen[sm] = want[sm]
+            for j in o["ins"]:
+                k, x = j[0], [ap(y) for y in j[1:]]
+                if k == "mm":
+                    r = g.tensor.matmul(*x)
+                elif k == "tt":
+                    r = g.vector.tensor_tensor(*x)
+                elif k == "ts":
+                    r = g.vector.tensor_scalar(*(x if x[5] is not None else x[:5]))
+                elif k == "cp" or (k == "gat" and e == "dve"):
+                    r = g.vector.tensor_copy(*x)
+                elif k == "gat":
+                    r = g.scalar.activation(x[0], x[1], ACT.Copy)
+                elif k == "ms":
+                    r = g.vector.memset(*x)
+                elif k == "scan":
+                    r = g.vector.tensor_tensor_scan(x[0], x[1], x[2], 0.0, ALU.min, ALU.max)
+                elif k == "act":
+                    kw = {}
+                    if j[4] != 0.0:
+                        kw["bias"] = x[3]
+                    if j[5] != 1.0:
+                        kw["scale"] = x[4]
+                    r = g.scalar.activation(x[0], x[1], x[2], **kw)
+                elif k == "iota":
+                    if SB[j[1][0]][1] == I32:
+                        r = g.iota(*x)
+                    else:
+                        r = g.iota(*x, allow_small_or_imprecise_dtypes=True)
+                elif k == "dma":
+                    if e == "pool":
+                        r = g.dma_start(x[0], T.th[:], allow_slow_non_contiguous=True)
+                    else:
+                        r = q[e].dma_start(x[0], x[1])
+                else:
+                    dst = T.cores[(rank + o["peer"]) % NR]
+                    rid, pid = topo.addr(dst)[:2]
+                    g.remote_dma(x[0], x[1], T.sem[o["sem"]], T.sem["sent"], pid, rid, topo.mask(core, dst))
+                    sent += engines(o, rank)
+                    r = None
+            if r is not None and i in mark:
+                r.then_inc(T.sem[mark[i][0]], 16 if o["sem"] else 1)
+    total["sent"] = sent
+    for sm in sorted(total):
+        g.wait_ge(T.sem[sm], total[sm])

@@ -9,8 +9,8 @@ SB = {
     "ZI": (5 * 512, BF), "ZO": (4 * 512, BF), "ZF": (256, F32), "BK": (5 * 512, F16), "BO": (5 * 512, F16),
     "W": (1024, F32), "X": (4096, BF), "D": (4096, BF), "AB": (4096, BF),
     "OX": (256, U16), "OY": (256, U16), "OM": (256, U16), "OC": (5 * 32, U16),
-    "IA": (256, I32), "IB": (256, I32), "IC": (256, I32), "IZ": (256, I32), "IT": (32, I32),
-    "TM": (768, F32), "M": (768, BF), "F2": (512, F16), "EQ": (512, BF), "TT": (512, F32),
+    "IB": (256, I32), "IC": (256, I32), "IZ": (256, I32), "IT": (32, I32),
+    "M": (768, BF), "F2": (512, F16), "E3": (768, I32), "TT": (2304, F32), "THS": (4, F32),
     "FT": (768, F32), "GF": (256, F32), "ZN": (256, BF), "U": (256, F32), "RFI": (512, F16), "EB": (5 * 512, BF),
     "V": (144, I32), "VB": (128, I32), "VP": (4, I32), "PC": (4, F32), "VJ": (16, F32), "JT": (16, F32), "JW": (144, F32),
     "B32": (128, F32), "PM": (8 * 128, F16), "C32": (3 * 128, F32), "C16": (5 * 128, F16), "CB": (10 * 128, BF),
@@ -24,15 +24,16 @@ ROT = [0, 1, 2, 3, 4, 5, 6, 11]
 BIG = 8192.0
 REG = {
     2: dict(c=(0, 0), mP=(0, 1), old=(0, 2), dl=(0, 3), P2=(1, 0), lin=(1, 2), ft=(1, 0), P4=(2, 0), PB=(2, 2), ut=(2, 2),
-            u=(2, 3), pd=(3, 0), X1=(3, 0), X2=(3, 1), zn=(3, 2), mg=(3, 0), o2=(0, 2), d2=(1, 2)),
+            u=(2, 3), pd=(3, 0), X1=(3, 0), X2=(3, 1), zn=(3, 2), mg=(3, 0), o2=(0, 2), d2=(1, 1)),
     4: dict(c=(0, 0), mP=(0, 1), old=(0, 2), dl=(0, 3), P2=(0, 4), lin=(0, 6), ft=(0, 4), P4=(1, 0), PB=(1, 2), ut=(1, 2),
-            u=(1, 3), pd=(1, 4), X1=(1, 4), X2=(1, 5), zn=(1, 6), mg=(1, 4), o2=(0, 2), d2=(0, 6)),
+            u=(1, 3), pd=(1, 4), X1=(1, 4), X2=(1, 5), zn=(1, 6), mg=(1, 4), o2=(0, 2), d2=(0, 5)),
 }
 
-PARAMS = dict(ns=2, modes=[[("a", 64), ("a", 32), ("d", 32)]] * 3, sch=64, seed=0, iters=1500,
-              x0=[("act", 32), ("dve", 32)] * 2, xs=[("act", 32)] * 4, ts=[("act", 32), ("dve", 32)] * 2,
-              t4=[("act", 32), ("dve", 32)] * 2, act16=True, early=True, lead=8000.0, dup=True)
-COST = dict(f=1.25, gc=1.56, pe=0.42, ov=50.0, hop=100.0, same=60.0, net=4000.0, iss=800.0, bw=200.0)
+PARAMS = dict(ns=2, modes=[[("a", 64), ("a", 32), ("d", 32)]] * 3, sch=64, seed=0, iters=300,
+              x0=[("act", 32), ("dve", 32)] * 2, xs=[("act", 64)] * 2, ts=[("act", 64), ("dve", 64)],
+              t4=[("act", 32), ("dve", 32)] * 2, act16=True, early=True, lead=8000.0, merge=True, sig=True, sweeps=5, win=22000.0, tries=1500, amp=7000.0, temp=600.0,
+              conv=())
+COST = dict(f=1.1, gc=1.56, pe=0.45, ov=60.0, hop=200.0, same=110.0, net=3000.0, iss=800.0, bw=200.0)
 
 
 def A(name, a, n, step=1, ind=None):
@@ -111,15 +112,21 @@ def build(par):
         else:
             ts(o, a, bias, ALU.add)
 
-    def index(off, tmp, a, b, lin, mid=None):
+    def conv(o, a, tag, bias=0.0):
+        if tag in par["conv"]:
+            act(o, a, ACT.Identity, bias=bias)
+        elif bias:
+            ts(o, a, bias, ALU.add)
+        else:
+            cp(o, a)
+
+    def index(off, tmp, a, b, lin):
         tt(tmp, a, b, ALU.mult)
-        if mid:
-            mid()
         ts(tmp, tmp, 5, ALU.arith_shift_right)
         tt(tmp, tmp, lin, ALU.add)
         ts(tmp, tmp, 4095, ALU.bitwise_and)
         if off:
-            cp(off, tmp)
+            conv(off, tmp, off[0])
 
     for nm, src, n in (("ZS", "zs", 256), ("QS", "qs", 1024), ("HN", "hn", 256), ("GT", "gt", 256)):
         dma(A(nm, 0, n), A(src, 0, n), "l" + src, 512 * n)
@@ -172,6 +179,9 @@ def build(par):
     ms(A("C37", 0, 256), 3.75)
     TH = A("THF", 0, 1)
     cp(TH, A("TH", 0, 1))
+    THS = A("THS", 0, 1)
+    if par["sig"]:
+        ts(THS, TH, 256.0, ALU.mult, -128.0, ALU.add)
     KR = {0: CB["K0"], 5: CB["K5"], 10: CB["K10"]}
     XW, XZ = ("XT", 0, 4096, 1), ("XT", 0, 4112, 1)
 
@@ -204,8 +214,9 @@ def build(par):
             z0 = 512 * t + 2 * l0
             Z, CNT = A("ZI", z0, LN), A("ZI", z0 + LN, LN)
             Ms = [A("M", 3 * l0 + LN * k, LN) for k in range(NS)]
-            TMs = [A("TM", 3 * l0 + LN * k, LN) for k in range(NS)]
-            IA, IB, IC, IZ = (A(n, l0, LN) for n in ("IA", "IB", "IC", "IZ"))
+            TMs = [A("TT", 9 * l0 + 3 * LN * k + 2 * LN, LN) for k in range(NS)]
+            IA = A("E3", 3 * l0 + 2 * LN, LN)
+            IB, IC, IZ = (A(n, l0, LN) for n in ("IB", "IC", "IZ"))
             lin = pr("lin")
             Wn = ("W", 4 * l0, 4 * l0 + 4 * LN, 1)
             mm([(lin, I65, H), (lin, I101, G)])
@@ -219,7 +230,7 @@ def build(par):
             mm([(ut, A("Z2", 14 - 2 * a, 128), A("ZI", z0 + a, nt, 8)) for a in range(8)])
             tt(IT, ut, A("JT", 0, nt), ALU.add)
             ts(IT, IT, 4 * LN - 1, ALU.bitwise_and)
-            cp(OC, IT)
+            conv(OC, IT, "OC")
             to16(A("RFI", 2 * l0, 2 * LN), Wn + (OC,), -2048.0)
             P4 = pr("P4", 0, 2 * LN)
             for hf in range(2):
@@ -266,29 +277,25 @@ def build(par):
                         mm([(pr("c", done, a - done), A("Z1", 15 - j, 128), A("AB", c0 + 16 * done + j, a - done, 16))
                             for j in range(16)], first=False, last=a == LN)
                         done, extra = a, []
-                ts(Ms[k], c, TH, ALU.is_lt)
+                if par["sig"]:
+                    act(Ms[k], c, ACT.Sigmoid, bias=THS, scale=-256.0)
+                else:
+                    ts(Ms[k], c, TH, ALU.is_lt)
                 mm(e2 + [(pr("P2", LN * hf), CB["T"], Ms[k]) for hf in range(2)], first=not par["early"])
                 fH, fR = A("F2", 2 * l0, LN), A("F2", 2 * l0 + LN, LN)
                 ts(A("F2", 2 * l0, 2 * LN), P2, -4096.0, ALU.add, -2048.0, ALU.max)
-                mP, old, dl = pr("mP"), pr("old"), pr("dl")
-                if par["dup"]:
-                    mm([(pr("o2", 0, 2 * LN), KR[0], A("C37", 0, 2 * LN))] + [(pr("o2", LN * hf), B16, fR) for hf in range(2)])
-                    for hf in range(2):
-                        mm([(pr("d2", LN * hf), B16, fH), (pr("d2", LN * hf), nB16, fR)])
-                    mm([(mP, CB["I"], Ms[k])])
-                    EQ = A("EQ", 2 * l0, 2 * LN)
-                    tt(EQ, RF, pr("o2", 0, 2 * LN), ALU.is_equal)
-                    tt(A("TT", 2 * l0, 2 * LN), EQ, pr("d2", 0, 2 * LN), ALU.mult)
+                mm([(pr("o2", 0, 2 * LN), KR[0], A("C37", 0, 2 * LN))] + [(pr("o2", LN * hf), B16, fR) for hf in range(2)])
+                for hf in range(2):
+                    mm([(pr("d2", LN * hf), B16, fH), (pr("d2", LN * hf), nB16, fR)])
+                mm([(pr("d2", 2 * LN), CB["I"], Ms[k])])
+                t0 = 9 * l0 + 3 * LN * k
+                tt(A("E3", 3 * l0, 2 * LN), RF, pr("o2", 0, 2 * LN), ALU.is_equal)
+                if par["merge"]:
+                    tt(A("TT", t0, 3 * LN), A("E3", 3 * l0, 3 * LN), pr("d2", 0, 3 * LN), ALU.mult)
                 else:
-                    mm([(mP, CB["I"], Ms[k])])
-                    mm([(old, KR[0], A("C37", 0, LN)), (old, B16, fR)])
-                    mm([(dl, B16, fH), (dl, nB16, fR)])
-                    for hf, src in enumerate((R, F)):
-                        tt(A("EQ", 2 * l0 + LN * hf, LN), src, old, ALU.is_equal)
-                    for hf in range(2):
-                        tt(A("TT", 2 * l0 + LN * hf, LN), A("EQ", 2 * l0 + LN * hf, LN), dl, ALU.mult)
-                tt(TMs[k], IA, mP, ALU.mult)
-                mm(e4 + [(P4, P5w if k < NS - 1 else I32m, A("TT", 2 * l0, 2 * LN))], first=not par["early"])
+                    tt(A("TT", t0, 2 * LN), A("E3", 3 * l0, 2 * LN), pr("d2", 0, 2 * LN), ALU.mult)
+                    tt(TMs[k], IA, pr("d2", 2 * LN), ALU.mult)
+                mm(e4 + [(P4, P5w if k < NS - 1 else I32m, A("TT", t0, 2 * LN))], first=not par["early"])
             zn, ZN, pz = pr("zn"), A("ZN", l0, LN), pr("old")
             mm([(zn, CB["I"], Z)] + [(zn, CB["nB256"], m) for m in Ms])
             act(ZN, zn, ACT.Relu)
@@ -309,7 +316,7 @@ def build(par):
             index(None, IC, U, X1, X2)
             if t < NV - 1:
                 GO = A("GOUT", 256 * t + l0, LN)
-                ts(GO, IC, -2048.0, ALU.add)
+                conv(GO, IC, "GO", -2048.0)
                 send(A("GIN", 256 * (t + 1) + l0, LN), GO, "g%d%d" % (t, s), 1)
             else:
                 GO = A("GL", l0, LN)
@@ -326,7 +333,7 @@ def build(par):
             mm([(mi, CB["nK4"], m) for m in Ms] + [(mi, I32m, m) for m in TMs])
             if t < NV - 1:
                 mm([(pr("c"), CB["B"], m) for m in Ms])
-            ts(A("OM", l0, LN), mi, 4096.0, ALU.add)
+            conv(A("OM", l0, LN), mi, "OM", 4096.0)
             if t < NV - 1:
                 act(A("ZO", z0 + LN, LN), pr("c"), ACT.Copy)
             a = 0
@@ -339,7 +346,7 @@ def build(par):
             mm([(pz, CB["I"], Z), (pz, CB["I"], ZN), (pz, CB["I"], A("AB", c0 + 15, LN, 16))])
             ts(IZ, pz, 0.5, ALU.mult, -0.25, ALU.add)
             if t < NV - 1:
-                cp(A("ZO", z0, LN), IZ)
+                conv(A("ZO", z0, LN), IZ, "ZO")
                 send(A("ZI", z0 + 512, 2 * LN), A("ZO", z0, 2 * LN), "z%d%d" % (t, s), 1)
             else:
                 cp(A("ZF", l0, LN), IZ)
@@ -457,6 +464,48 @@ def schedule(ops, par, C):
             now = st
         if now[n] < best[n]:
             best = now
+    for _ in range(par["sweeps"]):
+        t0 = 0.0
+        while t0 < best[n]:
+            bk = place(n + 1, topo_order(n + 1, succ, pred, [-(best[i] + dur[i]) for i in range(n + 1)]), succ, dur, engs)
+            ids = [i for i in range(n) if t0 - 3000.0 <= best[i] < t0 + par["win"]]
+            pos = {i: j for j, i in enumerate(ids)}
+            m = len(ids)
+            fixed = [best[i] < t0 for i in ids]
+            rel = [max([best[d] + dur[d] + lag for d, lag in pred[i] if d not in pos] + [best[i] if fixed[j] else t0])
+                   for j, i in enumerate(ids)]
+            sp = [[(pos[d], lag) for d, lag in pred[i] if d in pos] + [(m, rel[j])] for j, i in enumerate(ids)] + [[]]
+            sd, se = [dur[i] for i in ids] + [0.0], [engs[i] for i in ids] + ["start"]
+            edge, half = t0 + par["win"] - 2500.0, t0 + par["win"] / 2
+            tail = np.array([max([lag + dur[i] + bk[j] + dur[j] for j, lag in succ[i] if j not in pos]
+                                 + [bk[i] + dur[i] if best[i] > edge else -1e9]) if best[i] > half else -1e9 for i in ids] + [-1e9])
+            fx = np.array(fixed + [True])
+
+            def value(st):
+                v = np.sort(np.array(st) + tail)
+                return float(v[-1] + 0.5 * np.mean(np.maximum(v[-12:], v[-1] - 5000.0)))
+
+            cur = np.array([best[i] for i in ids] + [-1e9])
+            cv = value(place(m + 1, topo_order(m + 1, sp, None, cur.tolist()), sp, sd, se))
+            bv, top = cv, cur
+            for it in range(par["tries"]):
+                near = (np.abs(cur - t0 - rng.random() * par["win"]) < 5000.0 * rng.random()) & ~fx
+                key = cur + near * rng.random(m + 1) * par["amp"] * rng.random() - fx * 1e6
+                st = place(m + 1, topo_order(m + 1, sp, None, key.tolist()), sp, sd, se)
+                v = value(st)
+                if v <= cv + par["temp"] * (1.0 - it / par["tries"]) * rng.random():
+                    cv, cur = v, np.array(st[:m] + [-1e9])
+                    if cv < bv:
+                        bv, top = cv, cur
+            key = list(best)
+            for j, i in enumerate(ids):
+                key[i] = float(top[j])
+            st = forth(key)
+            st2 = again(st)
+            st = st2 if st2[n] < st[n] else st
+            if st[n] < best[n]:
+                best = st
+            t0 += par["win"] * (0.3 + 0.3 * rng.random())
     order = {e: [] for e in ("pe", "dve", "act", "pool", "sp")}
     for i in sorted(range(n), key=lambda i: (best[i], i)):
         order[engs[i]].append(i)

@@ -3,36 +3,36 @@ from concourse.mybir import AluOpType as ALU, ActivationFunctionType as ACT
 
 NR, NV, NS = 4, 5, 3
 F32, BF, I32, U16, F16 = "float32", "bfloat16", "int32", "uint16", "float16"
+M16 = ("P0", "P5", "P6", "P11", "P15", "P4", "Q15", "Q4", "La", "Lb", "nI", "B", "nB", "B2k")
+MBF = ("K0", "K5", "K10", "nK0", "nK6", "nK11", "K4", "nK4", "K1", "Ib", "nIb", "Bb", "nB256")
 SB = {
     "XT": (4112, BF), "HN": (256, I32), "GT": (256, I32), "ZS": (256, I32), "QS": (1024, I32), "TH": (4, I32),
-    "THF": (4, F32), "HRF": (4 * 768, F16), "GIN": (5 * 256, F16), "GOUT": (4 * 256, F16), "GL": (256, F32),
-    "ZI": (5 * 512, BF), "ZO": (4 * 512, BF), "ZF": (256, F32), "BK": (5 * 512, F16), "BO": (5 * 512, F16),
+    "HO": (5 * 272, F16), "HI": (4 * 256, F16), "THS": (8, F32), "GI": (5 * 512, F16), "GO": (5 * 768, F16), "GL": (256, F32),
+    "ZI": (5 * 256, F16), "ZO": (5 * 256, F16), "ZF": (256, F32), "BK": (5 * 512, F16), "BO": (5 * 512, F16),
     "W": (1024, F32), "X": (4096, BF), "D": (4096, BF), "AB": (4096, BF),
     "OX": (256, U16), "OY": (256, U16), "OM": (256, U16), "OC": (5 * 32, U16),
-    "IB": (256, I32), "IC": (256, I32), "IZ": (256, I32), "IT": (32, I32),
-    "M": (768, BF), "F2": (512, F16), "E3": (768, I32), "TT": (2304, F32), "THS": (4, F32),
-    "FT": (768, F32), "GF": (256, F32), "ZN": (256, BF), "U": (256, F32), "RFI": (512, F16), "EB": (5 * 512, BF),
-    "V": (144, I32), "VB": (128, I32), "VP": (4, I32), "PC": (4, F32), "VJ": (16, F32), "JT": (16, F32), "JW": (144, F32),
-    "B32": (128, F32), "PM": (8 * 128, F16), "C32": (3 * 128, F32), "C16": (5 * 128, F16), "CB": (10 * 128, BF),
-    "NK": (16 * 128, BF), "Z1": (144, BF), "Z2": (144, BF), "ZT": (144, F32), "T1": (128, F32), "T2": (128, F32),
-    "RS": (1024, BF), "ET": (512, BF), "C05": (256, BF), "C37": (256, BF),
+    "IA": (768, I32), "IB": (256, I32), "IC": (256, I32), "IT": (32, I32),
+    "M": (1024, BF), "F2": (512, F16), "E": (1024, F16), "SO": (1024, F16), "TM": (768, F32), "DE": (512, F32),
+    "FT": (1024, F16), "U": (256, F32), "RFI": (512, F16), "EB": (5 * 512, F16),
+    "V": (144, I32), "VB": (128, I32), "VP": (4, I32), "PC": (4, F32), "VJ": (16, F32), "JT": (16, F32), "JW": (144, F16),
+    "C16": (128 * len(M16), F16), "CB": (128 * len(MBF), BF), "C32": (128, F32), "T": (5 * 128, BF), "TS": (5 * 128, BF),
+    "ORD": (144, BF), "BI": (8, I32), "BT": (8, F32), "Z1": (144, BF), "Z2": (144, F16), "ZT": (144, F16),
+    "RS": (1024, BF), "ET": (512, BF), "ZO1": (512, BF), "CN": (128, F16),
 }
 SCRATCH = {k: ("sbuf", [128, n], d) for k, (n, d) in SB.items()}
 for _b in range(8):
     SCRATCH["P%d" % _b] = ("psum", [128, 512], F32)
-ROT = [0, 1, 2, 3, 4, 5, 6, 11]
 BIG = 8192.0
-REG = {
-    2: dict(c=(0, 0), mP=(0, 1), old=(0, 2), dl=(0, 3), P2=(1, 0), lin=(1, 2), ft=(1, 0), P4=(2, 0), PB=(2, 2), ut=(2, 2),
-            u=(2, 3), pd=(3, 0), X1=(3, 0), X2=(3, 1), zn=(3, 2), mg=(3, 0), o2=(0, 2), d2=(1, 1)),
-    4: dict(c=(0, 0), mP=(0, 1), old=(0, 2), dl=(0, 3), P2=(0, 4), lin=(0, 6), ft=(0, 4), P4=(1, 0), PB=(1, 2), ut=(1, 2),
-            u=(1, 3), pd=(1, 4), X1=(1, 4), X2=(1, 5), zn=(1, 6), mg=(1, 4), o2=(0, 2), d2=(0, 5)),
-}
+REG = dict(S=(0, 0), pe=(0, 0), lx=(0, 0), gc=(0, 1), X1=(0, 0),
+           c=(1, 0), D=(1, 1), ft=(1, 0), ut=(1, 0), u=(1, 1),
+           P2=(2, 0), lin=(2, 2), mc=(2, 3), PB=(2, 0), X2=(2, 2),
+           pd=(3, 0), mi=(3, 0), zn=(3, 1), pz=(3, 3), mg=(3, 0))
 
 PARAMS = dict(ns=2, modes=[[("a", 64), ("a", 32), ("d", 32)]] * 3, sch=64, seed=0, iters=300,
-              x0=[("act", 32), ("dve", 32)] * 2, xs=[("act", 64)] * 2, ts=[("act", 64), ("dve", 64)],
-              t4=[("act", 32), ("dve", 32)] * 2, act16=True, early=True, lead=8000.0, merge=True, sig=True, sweeps=5, win=22000.0, tries=1500, amp=7000.0, temp=600.0,
-              conv=())
+              x0=[("act", 32), ("dve", 32)] * 2, xs=[("act", 64)] * 2, ts=[("act", 64)] * 2,
+              t4=[("act", 32), ("dve", 32)] * 2, act=("U", "BO", "RFI", "EB", "ZN", "ZO", "GO", "OX", "OM", "ZF"), cpx=False, cpy=False, scan=True,
+              loads=("hn", "gt", "xt", "zs", "qs"),
+              lead=8000.0, sweeps=5, win=22000.0, tries=1500, amp=7000.0, temp=600.0)
 COST = dict(f=1.1, gc=1.56, pe=0.45, ov=60.0, hop=200.0, same=110.0, net=3000.0, iss=800.0, bw=200.0)
 
 
@@ -95,9 +95,11 @@ def build(par):
     def ts(o, a, s1, op0, s2=None, op1=None): add("dve", [("ts", o, a, s1, s2, op0, op1)], [a, s1, s2], [o])
     def cp(o, a): add("dve", [("cp", o, a)], [a], [o])
     def ms(o, c): add("dve", [("ms", o, c)], [], [o])
+    def scan(o, a, b, op0, op1): add("dve", [("scan", o, a, b, op0, op1)], [a, b], [o])
     def act(o, a, fn, bias=0.0, scale=1.0): add("act", [("act", o, a, fn, bias, scale)], [a, bias, scale], [o])
     def gat(o, a, eng): add(eng, [("gat", o, a)], [a], [o])
     def iota(o, pat, base, cm): add("pool", [("iota", o, pat, base, cm)], [], [o])
+    def sel(o, a, pat, op, fill, base, cm): add("pool", [("sel", o, a, pat, op, fill, base, cm)], [a], [o])
 
     def mm(terms, first=True, last=True):
         ins = [("mm", o, l, r, first and j == 0, last and j == len(terms) - 1) for j, (o, l, r) in enumerate(terms)]
@@ -106,37 +108,42 @@ def build(par):
     def dma(o, a, sem, nbytes, eng="sp"): add(eng, [("dma", o, a)], [a], [o], sem=sem, nbytes=nbytes)
     def send(o, a, sem, peer): add("pool", [("send", o, a)], [a], [o], sem=sem, peer=peer)
 
-    def to16(o, a, bias=0.0):
-        if par["act16"]:
-            act(o, a, ACT.Identity, bias=bias)
-        else:
-            ts(o, a, bias, ALU.add)
-
-    def conv(o, a, tag, bias=0.0):
-        if tag in par["conv"]:
-            act(o, a, ACT.Identity, bias=bias)
+    def conv(o, a, tag, bias=0.0, scale=1.0, relu=False):
+        if tag in par["act"]:
+            act(o, a, ACT.Relu if relu else ACT.Identity, bias=bias, scale=scale)
+        elif relu:
+            ts(o, a, bias, ALU.add, 0.0, ALU.max)
+        elif scale != 1.0:
+            ts(o, a, scale, ALU.mult, bias, ALU.add)
         elif bias:
             ts(o, a, bias, ALU.add)
         else:
             cp(o, a)
 
-    def index(off, tmp, a, b, lin):
+    def index(tmp, a, b, lin):
         tt(tmp, a, b, ALU.mult)
-        ts(tmp, tmp, 5, ALU.arith_shift_right)
         tt(tmp, tmp, lin, ALU.add)
-        ts(tmp, tmp, 4095, ALU.bitwise_and)
-        if off:
-            conv(off, tmp, off[0])
+        ts(tmp, tmp, 5, ALU.arith_shift_right, 4095, ALU.bitwise_and)
 
-    for nm, src, n in (("ZS", "zs", 256), ("QS", "qs", 1024), ("HN", "hn", 256), ("GT", "gt", 256)):
-        dma(A(nm, 0, n), A(src, 0, n), "l" + src, 512 * n)
-    dma(A("XT", 0, 4096), A("xt", 0, 4096), "lxt", 1 << 20)
+    for src in par["loads"]:
+        if src == "qs":
+            for s in range(nst):
+                for b in range(2):
+                    dma(A("QS", 2 * LN * (2 * s + b), 2 * LN), A("qs", 512 * b + 2 * LN * s, 2 * LN), "lq%d%d" % (s, b), 1024 * LN)
+        else:
+            n = 4096 if src == "xt" else 256
+            dma(A(src.upper(), 0, n), A(src, 0, n), "l" + src, 1 << (20 if src == "xt" else 17))
     iota(A("V", 0, 144), [[1, 144]], 128, -1)
     iota(A("VB", 0, 128), [[16, 8], [0, 16]], 15, -1)
     iota(A("VP", 0, 1), [[0, 1]], 0, 1)
     iota(A("VJ", 0, 16), [[16, 16]], 0, 0)
+    iota(A("BI", 0, 5), [[-1, 5]], 16, 1)
+    iota(A("ORD", 0, 144), [[0, 9], [1, 16]], 0, 0)
     dma(A("TH", 0, 1), A("th", 0, 1), "lth", 512, eng="pool")
     iota(A("RS", 0, 1024), [[0, 64], [256, 16]], 0, 0)
+    C = {k: A("C16", 128 * j, 128) for j, k in enumerate(M16)}
+    C.update({k: A("CB", 128 * j, 128) for j, k in enumerate(MBF)})
+    I32m = A("C32", 0, 128)
     ts(A("VP", 0, 1), A("VP", 0, 1), 15, ALU.bitwise_and)
     PC = A("PC", 0, 1)
     cp(PC, A("VP", 0, 1))
@@ -145,57 +152,62 @@ def build(par):
     act(A("Z1", 0, 144), A("ZT", 0, 144), ACT.Copy)
     tt(A("JW", 0, 143), A("ZT", 0, 143), A("ZT", 1, 143), ALU.add)
     act(A("Z2", 0, 143), A("JW", 0, 143), ACT.Identity, scale=2.0 * LN)
-    V0, B32 = A("V", 0, 128), A("B32", 0, 128)
-    ts(A("VB", 0, 128), A("VB", 0, 128), 4, ALU.arith_shift_right)
-    ts(B32, A("VB", 0, 128), 0.0, ALU.is_equal)
-    ts(A("T1", 0, 128), V0, -8192.0, ALU.mult, 128 * 8192.0 + 4096.0, ALU.add)
-    ts(A("T2", 0, 128), V0, 128.0, ALU.is_ge)
-    tt(A("T1", 0, 128), A("T1", 0, 128), A("T2", 0, 128), ALU.mult)
-    CB = {k: A("CB", 128 * j, 128) for j, k in enumerate(("T", "I", "nI", "B", "nB256", "K0", "K5", "K10", "nK4", "B64"))}
-    tt(CB["T"], A("T1", 0, 128), B32, ALU.mult)
     ts(A("V", 0, 144), A("V", 0, 144), 15, ALU.bitwise_and)
     ts(A("JW", 0, 144), A("V", 0, 144), 0.0, ALU.is_equal)
-    PM = {r: A("PM", 128 * j, 128) for j, r in enumerate(ROT)}
-    I32m, P5w, nKB = A("C32", 0, 128), A("C32", 128, 128), A("C32", 256, 128)
-    I65, I101, nI, B16, nB16 = (A("C16", 128 * j, 128) for j in range(5))
-    tt(I32m, B32, A("JW", 0, 128), ALU.mult)
-    for o, a, c in ((I65, I32m, 65.0), (I101, I32m, 101.0), (B16, B32, 1.0), (nB16, B32, -1.0), (nI, I32m, -1.0)):
-        ts(o, a, c, ALU.mult)
-    for r in ROT:
-        tt(PM[r], B32, A("JW", r, 128), ALU.mult)
-    tt(P5w, B32, A("JW", 5, 128), ALU.mult)
-    tt(A("T2", 0, 128), B32, A("JW", 10, 128), ALU.mult)
-    for o, a, c in ((CB["I"], I32m, 1.0), (CB["nI"], I32m, -1.0), (CB["B"], B32, 1.0), (nKB, B32, -BIG),
-                    (CB["K0"], I32m, BIG), (CB["K5"], P5w, BIG), (CB["K10"], A("T2", 0, 128), BIG),
-                    (CB["nB256"], B32, -256.0), (CB["nK4"], I32m, -4096.0), (CB["B64"], B32, 64.0)):
-        act(o, a, ACT.Identity, scale=c)
-    NK = {r: A("NK", 128 * r, 128) for r in range(16)}
-    for r in (0, 5, 10, 15, 4, 9, 14, 3, 8, 13, 2, 7, 12):
-        tt(NK[r], nKB, A("JW", r, 128), ALU.mult)
+    ts(A("VB", 0, 128), A("VB", 0, 128), 4, ALU.arith_shift_right)
+    PB1, PBK = A("P7", 0, 128), A("P7", 128, 128)
+    ts(PB1, A("VB", 0, 128), 0.0, ALU.is_equal)
+    ts(PBK, A("VB", 0, 128), 0.0, ALU.is_equal, -BIG, ALU.mult)
+    ts(C["B"], A("VB", 0, 128), 0.0, ALU.is_equal)
+    for k, r in (("P0", 0), ("P5", 5), ("P6", 6), ("P11", 11), ("P15", 15), ("P4", 4), ("K10", 10)):
+        tt(C[k], A("JW", r, 128), PB1, ALU.mult)
+    ts(A("BI", 0, 5), A("BI", 0, 5), 15, ALU.bitwise_and)
+    ts(A("BT", 0, 5), A("BI", 0, 5), -256.0, ALU.mult, -128.0, ALU.add)
+    for t in range(NV):
+        act(A("TS", 128 * t, 128), A("ORD", 16 - t, 128), ACT.Sigmoid, bias=A("BT", t, 1), scale=256.0)
+        tt(A("T", 128 * t, 128), A("TS", 128 * t, 128), PBK, ALU.mult)
+    for a, n in ((0, 1), (1, NV - 1)):
+        sel(A("T", 128 * a, 128 * n), A("T", 128 * a, 128 * n), [[0, n], [-1, 128]], ALU.not_equal, 4096.0, 0, 1)
+    for j, (k, a, c) in enumerate((
+            ("La", "P0", 2080.0), ("Lb", "P0", 3232.0), ("nI", "P0", -1.0), ("Ib", "P0", 1.0), ("nIb", "P0", -1.0),
+            ("nB", "B", -1.0), ("K0", "P0", BIG), ("K5", "P5", BIG), ("K10", "K10", BIG), ("nK0", "P0", -BIG),
+            ("nK6", "P6", -BIG), ("nK11", "P11", -BIG), ("K4", "P0", 4096.0), ("nK4", "P0", -4096.0), ("K1", "P0", 1024.0),
+            ("Bb", "B", 1.0), ("nB256", "B", -256.0), ("B2k", "B", 2048.0), ("Q15", "P15", 32.0), ("Q4", "P4", 32.0))):
+        if j % 2:
+            act(C[k], C[a], ACT.Identity, scale=c)
+        else:
+            ts(C[k], C[a], c, ALU.mult)
+    act(I32m, C["P0"], ACT.Copy)
     ms(A("XT", 4096, 16), 0.0)
     ms(A("ET", 0, 2 * LN), -2048.0)
     ms(A("ET", 2 * LN, 2 * LN), BIG - 2048.0)
-    ms(A("C05", 0, 256), 0.5)
-    ms(A("C37", 0, 256), 3.75)
-    TH = A("THF", 0, 1)
-    cp(TH, A("TH", 0, 1))
-    THS = A("THS", 0, 1)
-    if par["sig"]:
-        ts(THS, TH, 256.0, ALU.mult, -128.0, ALU.add)
-    KR = {0: CB["K0"], 5: CB["K5"], 10: CB["K10"]}
+    ms(A("ZO1", 0, 2 * LN), 0.0)
+    ms(A("ZO1", 2 * LN, 2 * LN), 1.0)
+    ms(A("CN", 0, LN), -1280.0)
+    ONE = A("ZO1", 2 * LN, LN)
+    KR = {0: C["K0"], 5: C["K5"], 10: C["K10"]}
     XW, XZ = ("XT", 0, 4096, 1), ("XT", 0, 4112, 1)
 
     for s in range(nst):
-        l0 = s * LN
-        cp(A("ZI", 2 * l0, LN), A("ZS", l0, LN))
-        ms(A("ZI", 2 * l0 + LN, LN), 0.0)
-        ts(A("HRF", 3 * l0, LN), A("HN", l0, LN), -2048.0, ALU.add)
-        for b in range(2):
-            cp(A("W", 4 * l0 + 2 * LN * b, 2 * LN), A("QS", 512 * b + 2 * l0, 2 * LN))
-    ts(A("GIN", 0, 256), A("GT", 0, 256), -2048.0, ALU.add)
-    for d in range(1, NR):
-        for s in range(nst):
-            send(A("HRF", 768 * d + 3 * LN * s, LN), A("HRF", 3 * LN * s, LN), "h%d%d" % (d, s), d)
+        ts(A("HO", LN * s, LN), A("HN", LN * s, LN), -2048.0, ALU.add)
+        ts(A("GI", 2 * LN * s + LN, LN), A("GT", LN * s, LN), -2048.0, ALU.add)
+        ms(A("GI", 2 * LN * s, LN), 0.0)
+        act(A("ZI", LN * s, LN), A("ZS", LN * s, LN), ACT.Identity, bias=1024.0)
+        ms(A("M", 4 * LN * s + 3 * LN, LN), 1.0)
+        if par["scan"]:
+            ms(A("E", 4 * LN * s, 4 * LN), 0.0)
+    ts(A("HO", 256, 1), A("TH", 0, 1), -2048.0, ALU.add)
+    ts(A("THS", 0, 1), A("TH", 0, 1), 256.0, ALU.mult, -128.0, ALU.add)
+
+    def turn_names(d):
+        mm([(A("P3", 0, 257), C["P15"], A("HO", 272 * (d - 1), 257))])
+        act(A("HO", 272 * d, 257), A("P3", 0, 257), ACT.Copy)
+        if d < NR:
+            send(A("HI", 256 * d, 256), A("HO", 272 * d, 256), "h%d" % d, d)
+
+    for d in range(1, NV):
+        turn_names(d)
+    ts(A("THS", 1, 4), A("HO", 272 + 256, 4, 272), 256.0, ALU.mult, 2048 * 256.0 - 128.0, ALU.add)
 
     for t in range(NV):
         for s in range(nst):
@@ -204,23 +216,23 @@ def build(par):
             c0 = 16 * l0
 
             def pr(name, off=0, n=LN, step=1):
-                bk, col = REG[nst][name]
+                bk, col = REG[name]
                 return A("P%d" % (8 // nst * s + bk), col * LN + off, n, step)
 
-            h0 = 768 * (t % NR) + 3 * l0
-            H, R, F = A("HRF", h0, LN), A("HRF", h0 + LN, LN), A("HRF", h0 + 2 * LN, LN)
-            HR, RF = A("HRF", h0, 2 * LN), A("HRF", h0 + LN, 2 * LN)
-            G = A("GIN", 256 * t + l0, LN)
-            z0 = 512 * t + 2 * l0
-            Z, CNT = A("ZI", z0, LN), A("ZI", z0 + LN, LN)
-            Ms = [A("M", 3 * l0 + LN * k, LN) for k in range(NS)]
-            TMs = [A("TT", 9 * l0 + 3 * LN * k + 2 * LN, LN) for k in range(NS)]
-            IA = A("E3", 3 * l0 + 2 * LN, LN)
-            IB, IC, IZ = (A(n, l0, LN) for n in ("IB", "IC", "IZ"))
-            lin = pr("lin")
-            Wn = ("W", 4 * l0, 4 * l0 + 4 * LN, 1)
-            mm([(lin, I65, H), (lin, I101, G)])
-            index(A("OX", l0, LN), IB, H, G, lin)
+            H = A("HI", 256 * t + l0, LN) if t % NR else A("HO", 272 * t + l0, LN)
+            CNT, G = A("GI", 512 * t + 2 * l0, LN), A("GI", 512 * t + 2 * l0 + LN, LN)
+            z0 = 256 * t + l0
+            Z = A("ZI", z0, LN)
+            Ms = [A("M", 4 * l0 + LN * k, LN) for k in range(NS)]
+            TMs = [A("TM", 3 * l0 + LN * k, LN) for k in range(NS)]
+            IAs = [A("IA", 3 * l0 + LN * k, LN) for k in range(NS)]
+            IB, IC = A("IB", l0, LN), A("IC", l0, LN)
+            Wn = ("QS" if t < 2 else "W", 4 * l0, 4 * l0 + 4 * LN, 1)
+            mm([(pr("lx"), C["La"], H), (pr("lx"), C["Lb"], G)])
+            if par["cpx"]:
+                mm([(pr("gc"), C["P0"], G)])
+            index(IB, H, pr("gc") if par["cpx"] else G, pr("lx"))
+            conv(A("OX", l0, LN), IB, "OX")
             a = 0
             for eng, n in par["x0" if t == 0 else "xs"]:
                 gat(A("X", c0 + 16 * a, 16 * n), XW + (A("OX", l0 + a, n),), eng)
@@ -228,40 +240,38 @@ def build(par):
             nt = LN // 8
             ut, IT, OC = pr("ut", 0, nt), A("IT", nt * s, nt), A("OC", 32 * t + nt * s, nt)
             mm([(ut, A("Z2", 14 - 2 * a, 128), A("ZI", z0 + a, nt, 8)) for a in range(8)])
+            mm([(pr("u"), C["B"], Z)])
             tt(IT, ut, A("JT", 0, nt), ALU.add)
             ts(IT, IT, 4 * LN - 1, ALU.bitwise_and)
             conv(OC, IT, "OC")
-            to16(A("RFI", 2 * l0, 2 * LN), Wn + (OC,), -2048.0)
-            P4 = pr("P4", 0, 2 * LN)
-            for hf in range(2):
-                mm([(pr("P4", LN * hf), PM[t], A("RFI", 2 * l0 + hf, LN, 2))])
+            U = A("U", l0, LN)
+            conv(U, pr("u"), "U", 32.0 - 16384.0)
+            RF, R, F = A("RFI", 2 * l0, 2 * LN), A("RFI", 2 * l0, LN, 2), A("RFI", 2 * l0 + 1, LN, 2)
+            conv(RF, Wn + (OC,), "RFI", -2048.0)
+            if t < NV - 1:
+                conv(A("EB", 512 * t + 2 * l0, 2 * LN), ("ET", 0, 4 * LN, 1, OC), "EB")
             for k in range(NS):
-                to16(RF, P4)
-                mm([(lin, I65, R), (lin, I101, F)])
-                index(A("OY", l0, LN), IA, pr("P4"), F, lin)
-                if k == 0:
-                    U = A("U", l0, LN)
-                    mm([(pr("u"), CB["B"], Z)])
-                    act(U, pr("u"), ACT.Identity, bias=32.0)
-                    if t < NV - 1:
-                        act(A("EB", 512 * t + 2 * l0, 2 * LN), ("ET", 0, 4 * LN, 1, OC), ACT.Copy)
+                lin, IA = pr("lin"), IAs[k]
+                if par["cpy"]:
+                    mm([(pr("mc"), C["P0"], R)])
+                mm([(lin, C["La"], R), (lin, C["Lb"], F)])
+                index(IA, F, pr("mc") if par["cpy"] else R, lin)
+                conv(A("OY", l0, LN), IA, "OY")
                 P2 = pr("P2", 0, 2 * LN)
-                e2, e4 = [(P2, PM[0], HR)], [(P4, PM[5 if k < NS - 1 else 0], RF)]
-                if par["early"]:
-                    mm(e2, last=False)
-                    mm(e4, last=False)
-                    e2, e4 = [], []
                 c = pr("c")
-                mm([(c, CB["nI"], CNT)] + [(c, KR[r], Ms[j]) for j in range(k) for r in (0, 5 * (k - j))], last=False)
-                a, done, extra = 0, 0, []
+                mm([(c, C["nI"], CNT)] + [(c, KR[r], Ms[j]) for j in range(k) for r in (0, 5 * (k - j))], last=False)
+                a, done, extra, nd = 0, 0, [], 0
                 for mode, n in par["modes"][k]:
                     y = XW + (A("OY", l0 + a, n),)
                     x, d, ab = (A(nm, c0 + 16 * a, 16 * n) for nm in ("X", "D", "AB"))
                     if mode == "d":
                         act(d, y, ACT.Copy)
-                        pd = pr("pd", 0, 16 * n)
-                        mm([(pd, CB["nI"], x), (pd, CB["I"], d)])
-                        act(ab, pd, ACT.Abs)
+                        for b in range(0, 16 * n, 512):
+                            pd, w = pr(("pd", "pe")[nd % 2], 0, min(512, 16 * n - b)), min(512, 16 * n - b)
+                            nd += 1
+                            mm([(pd, C["nIb"], A("X", x[1] + b, w))], last=False)
+                            mm([(pd, C["Ib"], A("D", x[1] + b, w))], first=False)
+                            act(A("AB", x[1] + b, w), pd, ACT.Abs)
                     else:
                         tt(d, y, x, ALU.subtract)
                         if mode == "a":
@@ -270,6 +280,8 @@ def build(par):
                             ts(ab, d, -2.0, ALU.mult, 0.0, ALU.max)
                             extra.append((a, n))
                     a += n
+                    while len(extra) > 1 and extra[-2][0] + extra[-2][1] == extra[-1][0]:
+                        extra[-2:] = [(extra[-2][0], extra[-2][1] + extra[-1][1])]
                     if a - done >= 64 or a == LN:
                         for ea, en in extra:
                             mm([(pr("c", ea, en), A("Z1", 15 - j, 128), A("D", c0 + 16 * ea + j, en, 16)) for j in range(16)],
@@ -277,88 +289,92 @@ def build(par):
                         mm([(pr("c", done, a - done), A("Z1", 15 - j, 128), A("AB", c0 + 16 * done + j, a - done, 16))
                             for j in range(16)], first=False, last=a == LN)
                         done, extra = a, []
-                if par["sig"]:
-                    act(Ms[k], c, ACT.Sigmoid, bias=THS, scale=-256.0)
-                else:
-                    ts(Ms[k], c, TH, ALU.is_lt)
-                mm(e2 + [(pr("P2", LN * hf), CB["T"], Ms[k]) for hf in range(2)], first=not par["early"])
+                M, Tt = Ms[k], A("T", 128 * t, 128)
+                act(M, c, ACT.Sigmoid, bias=A("THS", t, 1), scale=-256.0)
+                for hf, src in enumerate((H, R)):
+                    o = pr("P2", LN * hf)
+                    mm([(o, C["P0"], src), (o, Tt, M)])
+                mm([(pr("mc"), C["Ib"], M)])
                 fH, fR = A("F2", 2 * l0, LN), A("F2", 2 * l0 + LN, LN)
                 ts(A("F2", 2 * l0, 2 * LN), P2, -4096.0, ALU.add, -2048.0, ALU.max)
-                mm([(pr("o2", 0, 2 * LN), KR[0], A("C37", 0, 2 * LN))] + [(pr("o2", LN * hf), B16, fR) for hf in range(2)])
-                for hf in range(2):
-                    mm([(pr("d2", LN * hf), B16, fH), (pr("d2", LN * hf), nB16, fR)])
-                mm([(pr("d2", 2 * LN), CB["I"], Ms[k])])
-                t0 = 9 * l0 + 3 * LN * k
-                tt(A("E3", 3 * l0, 2 * LN), RF, pr("o2", 0, 2 * LN), ALU.is_equal)
-                if par["merge"]:
-                    tt(A("TT", t0, 3 * LN), A("E3", 3 * l0, 3 * LN), pr("d2", 0, 3 * LN), ALU.mult)
+                tt(TMs[k], IA, pr("mc"), ALU.mult)
+                rot = C["P5" if k < NS - 1 else "P0"]
+                mm([(pr("D", 0, 2 * LN), rot, RF)], last=False)
+                mm([(pr("D", hf, LN, 2), C["nB"], fR) for hf in range(2)], first=False)
+                if par["scan"]:
+                    mm([(pr("S", 1, 2 * LN, 2), rot, RF)])
+                    for hf in range(2):
+                        mm([(pr("S", 2 * hf, LN, 4), C["B"], fH), (pr("S", 2 * hf, LN, 4), C["nB"], fR)])
+                    ts(A("E", 4 * l0 + 1, 2 * LN, 2), pr("D", 0, 2 * LN), 30720.0, ALU.is_equal)
+                    scan(A("SO", 4 * l0, 4 * LN), A("E", 4 * l0, 4 * LN), pr("S", 0, 4 * LN), ALU.mult, ALU.add)
+                    RF, R, F = A("SO", 4 * l0 + 1, 2 * LN, 2), A("SO", 4 * l0 + 1, LN, 4), A("SO", 4 * l0 + 3, LN, 4)
                 else:
-                    tt(A("TT", t0, 2 * LN), A("E3", 3 * l0, 2 * LN), pr("d2", 0, 2 * LN), ALU.mult)
-                    tt(TMs[k], IA, pr("d2", 2 * LN), ALU.mult)
-                mm(e4 + [(P4, P5w if k < NS - 1 else I32m, A("TT", t0, 2 * LN))], first=not par["early"])
-            zn, ZN, pz = pr("zn"), A("ZN", l0, LN), pr("old")
-            mm([(zn, CB["I"], Z)] + [(zn, CB["nB256"], m) for m in Ms])
-            act(ZN, zn, ACT.Relu)
-            to16(RF, P4)
-            for k, r in enumerate((6, 11, 0)):
-                o = pr("ft", LN * k)
-                mm([(o, KR[0], Ms[k]), (o, PM[r], F)])
-            o = pr("ft", 3 * LN)
-            mm([(o, PM[0], G)] + [(o, NK[0], m) for m in Ms])
-            act(A("FT", 3 * l0, 3 * LN), pr("ft", 0, 3 * LN), ACT.Relu, bias=2048.0 - BIG)
-            GF = A("GF", l0, LN)
-            act(GF, o, ACT.Relu, bias=2048.0)
-            FT = [A("FT", 3 * l0 + LN * k, LN) for k in range(NS)]
-            X1, X2 = pr("X1"), pr("X2")
-            C05 = A("C05", 0, LN)
-            mm([(X1, CB["nK4"], C05)] + [(X1, I32m, f) for f in FT])
-            mm([(X2, CB["nK4"], C05), (X2, CB["B64"], Z), (X2, I32m, GF)])
-            index(None, IC, U, X1, X2)
-            if t < NV - 1:
-                GO = A("GOUT", 256 * t + l0, LN)
-                conv(GO, IC, "GO", -2048.0)
-                send(A("GIN", 256 * (t + 1) + l0, LN), GO, "g%d%d" % (t, s), 1)
-            else:
-                GO = A("GL", l0, LN)
-                cp(GO, IC)
-                dma(A("yg", l0, LN), GO, "sg%d" % s, 512 * LN)
-            if t > 0:
-                for hf, src in enumerate((R, F)):
-                    o = pr("PB", hf, LN, 2)
-                    mm([(o, NK[16 - 5 * j - t], Ms[j]) for j in range(NS)] + [(o, PM[6 - t], src)])
-                BO, BK = A("BO", 512 * t + 2 * l0, 2 * LN), A("BK", 512 * t + 2 * l0, 2 * LN)
-                to16(BO, pr("PB", 0, 2 * LN))
-                send(BK, BO, "b%d%d" % (t, s), NR - 1)
-            mi = pr("mP")
-            mm([(mi, CB["nK4"], m) for m in Ms] + [(mi, I32m, m) for m in TMs])
-            if t < NV - 1:
-                mm([(pr("c"), CB["B"], m) for m in Ms])
+                    mm([(pr("S", 0, 2 * LN), rot, RF)])
+                    for hf in range(2):
+                        mm([(pr("S", 2 * LN + hf, LN, 2), C["B"], fH), (pr("S", 2 * LN + hf, LN, 2), C["nB"], fR)])
+                    Eq, DE = A("E", 4 * l0, 2 * LN), A("DE", 2 * l0, 2 * LN)
+                    ts(Eq, pr("D", 0, 2 * LN), 30720.0, ALU.is_equal)
+                    tt(DE, Eq, pr("S", 2 * LN, 2 * LN), ALU.mult)
+                    RF, R, F = A("SO", 4 * l0, 2 * LN), A("SO", 4 * l0, LN, 2), A("SO", 4 * l0 + 1, LN, 2)
+                    tt(RF, DE, pr("S", 0, 2 * LN), ALU.add)
+            more = t < NV - 1
+            g0 = 768 * t + 3 * l0
+            zn, ZN, pz, mi = pr("zn"), A("GO", g0, LN), pr("pz"), pr("mi")
+            mm([(zn, C["P0"], Z)] + [(zn, C["nB256"], m) for m in Ms])
+            if more:
+                mm([(pr("zn", LN), C["K1"], ONE)] + [(pr("zn", LN), C["Bb"], m) for m in Ms])
+            mm([(mi, C["nK4"], m) for m in Ms] + [(mi, I32m, m) for m in TMs[:2]], last=False)
+            mm([(mi, I32m, TMs[2])], first=False)
             conv(A("OM", l0, LN), mi, "OM", 4096.0)
-            if t < NV - 1:
-                act(A("ZO", z0 + LN, LN), pr("c"), ACT.Copy)
+            nz = 2 * LN if more else LN
+            conv(A("GO", g0, nz), pr("zn", 0, nz), "ZN", -1024.0, relu=True)
             a = 0
-            for eng, n in par["t4" if t == NV - 1 else "ts"]:
+            for eng, n in par["ts" if more else "t4"]:
                 gat(A("D", c0 + 16 * a, 16 * n), XZ + (A("OM", l0 + a, n),), eng)
                 a += n
             for a in range(0, LN, par["sch"]):
-                o, i0, i1 = (A(nm, b + 16 * a, 16 * par["sch"]) for nm, b in (("AB", c0), ("RS", -16 * a), ("D", c0)))
-                add("dve", [("scan", o, i0, i1)], [i0, i1], [o])
-            mm([(pz, CB["I"], Z), (pz, CB["I"], ZN), (pz, CB["I"], A("AB", c0 + 15, LN, 16))])
-            ts(IZ, pz, 0.5, ALU.mult, -0.25, ALU.add)
-            if t < NV - 1:
-                conv(A("ZO", z0, LN), IZ, "ZO")
-                send(A("ZI", z0 + 512, 2 * LN), A("ZO", z0, 2 * LN), "z%d%d" % (t, s), 1)
+                scan(*(A(nm, b + 16 * a, 16 * par["sch"]) for nm, b in (("AB", c0), ("RS", -16 * a), ("D", c0))), ALU.min, ALU.max)
+            mm([(pz, C["P0"], Z), (pz, C["P0"], ZN)], last=False)
+            mm([(pz, C["Ib"], A("AB", c0 + 15, LN, 16))], first=False)
+            ZO = A("ZO", z0, LN)
+            conv(ZO, pz, "ZO", 511.75, 0.5)
+            if more:
+                send(A("ZI", z0 + 256, LN), ZO, "z%d%d" % (t, s), 1)
             else:
-                cp(A("ZF", l0, LN), IZ)
+                conv(A("ZF", l0, LN), ZO, "ZF", -1024.0)
                 dma(A("yz", l0, LN), A("ZF", l0, LN), "sz%d" % s, 512 * LN)
             if t > 0:
+                for hf, src in enumerate((R, F)):
+                    o = pr("PB", hf, LN, 2)
+                    mm([(o, C[nk], m) for nk, m in zip(("nK0", "nK11", "nK6"), Ms)] + [(o, C["P6"], src)])
+                BO, BK = A("BO", 512 * t + 2 * l0, 2 * LN), A("BK", 512 * t + 2 * l0, 2 * LN)
+                conv(BO, pr("PB", 0, 2 * LN), "BO")
+                send(BK, BO, "b%d%d" % (t, s), NR - 1)
+            o = pr("ft", 3 * LN)
+            mm([(pr("ft", 0, 4 * LN), C["K0"], A("M", 4 * l0, 4 * LN)), (o, C["P0"], G)] + [(o, C["nK0"], m) for m in Ms], last=False)
+            mm([(pr("ft", LN * k), C[r], F) for k, r in enumerate(("P6", "P11", "P0"))], first=False)
+            ts(A("FT", 4 * l0, 4 * LN), pr("ft", 0, 4 * LN), -BIG, ALU.add, -2048.0, ALU.max)
+            FT = [A("FT", 4 * l0 + LN * k, LN) for k in range(4)]
+            X1, X2 = pr("X1"), pr("X2")
+            mm([(X1, C["K4"], ONE)], last=False)
+            mm([(X1, C["P15" if more else "P4"], f) for f in FT[:3]], first=False)
+            mm([(X2, C["B2k"], Z), (X2, C["B2k"], A("CN", 0, LN))], last=False)
+            mm([(X2, C["Q15" if more else "Q4"], FT[3])], first=False)
+            index(IC, U, X1, X2)
+            if more:
+                conv(A("GO", g0 + 2 * LN, LN), IC, "GO", -2048.0)
+                send(A("GI", 512 * (t + 1) + 2 * l0, 2 * LN), A("GO", g0 + LN, 2 * LN), "g%d%d" % (t, s), 1)
+            else:
+                conv(A("GL", l0, LN), IC, "GO")
+                dma(A("yg", l0, LN), A("GL", l0, LN), "sg%d" % s, 512 * LN)
+            if t > 0:
                 EB, o0, o1 = A("EB", 512 * (t - 1) + 2 * l0, 2 * LN), pr("mg", 0, 2 * LN), pr("mg", 2 * LN, 2 * LN)
-                mm([(o0, CB["I"], EB), (o0, nI, BK)])
-                mm([(o1, CB["nI"], EB), (o1, KR[0], A("C05", 0, 2 * LN)), (o1, nI, BK)])
+                mm([(pr("mg", 0, 4 * LN), C["K4"], A("ZO1", 0, 4 * LN)), (o0, C["P0"], EB), (o1, C["nI"], EB)], last=False)
+                mm([(o0, C["nI"], BK), (o1, C["nI"], BK)], first=False)
                 Wa = A("W", 4 * l0, 4 * LN)
-                tt(Wa, Wa, pr("mg", 0, 4 * LN), ALU.min)
+                tt(Wa, A(Wn[0], 4 * l0, 4 * LN), pr("mg", 0, 4 * LN), ALU.min)
                 act(Wa, Wa, ACT.Abs)
-                if t == NV - 1:
+                if not more:
                     for b in range(2):
                         dma(A("yq", 512 * b + 2 * l0, 2 * LN), A("W", 4 * l0 + 2 * LN * b, 2 * LN), "sq%d%d" % (s, b), 1024 * LN)
     return ops
@@ -378,8 +394,8 @@ def cost(op, eng, C):
     if k == "send":
         return C["iss"], C["net"]
     n = width(i[1])
-    if k == "iota":
-        return 130 + 2 * n * cy, 0
+    if k in ("iota", "sel"):
+        return 150 + 2 * n * cy, 0
     aps = [x for x in i[1:] if is_ap(x) and (x[4] or width(x) > 1 or n == 1)]
     if any(x[4] for x in aps):
         return (50 if eng == "dve" else 65) + C["gc"] * n * cy, 0
@@ -595,7 +611,7 @@ def rank_program(g, core, T, topo):
                 elif k == "ms":
                     r = g.vector.memset(*x)
                 elif k == "scan":
-                    r = g.vector.tensor_tensor_scan(x[0], x[1], x[2], 0.0, ALU.min, ALU.max)
+                    r = g.vector.tensor_tensor_scan(x[0], x[1], x[2], 0.0, x[3], x[4])
                 elif k == "act":
                     kw = {}
                     if j[4] != 0.0:
@@ -608,6 +624,8 @@ def rank_program(g, core, T, topo):
                         r = g.iota(*x)
                     else:
                         r = g.iota(*x, allow_small_or_imprecise_dtypes=True)
+                elif k == "sel":
+                    r = g.affine_select(*x)
                 elif k == "dma":
                     if e == "pool":
                         r = g.dma_start(x[0], T.th[:], allow_slow_non_contiguous=True)

@@ -3,41 +3,47 @@ from concourse.mybir import AluOpType as ALU, ActivationFunctionType as ACT
 
 NR, NV, NS = 4, 5, 3
 F32, BF, I32, U16, F16 = "float32", "bfloat16", "int32", "uint16", "float16"
-M16 = ("P0", "P5", "P6", "P11", "P15", "P4", "Q15", "Q4", "La", "Lb", "nI", "B", "nB", "B2k")
-MBF = ("K0", "K5", "K10", "nK0", "nK6", "nK11", "K4", "nK4", "K1", "Ib", "nIb", "Bb", "nB256")
+M16 = ("P0", "P5", "P6", "P10", "P15", "P4", "Q0", "La", "Lb", "nI", "nX", "B", "nB", "B2k")
+MBF = ("KN", "KL", "nKN", "nKL", "K5", "K10", "nK0", "nK6", "nK11", "K4", "X4", "K1", "K16", "nK16", "KX", "Ib", "nIb", "Bb", "nB256")
 SB = {
-    "XT": (4112, BF), "HN": (256, I32), "GT": (256, I32), "ZS": (256, I32), "QS": (1024, I32), "TH": (4, I32),
-    "HO": (5 * 272, F16), "HI": (4 * 256, F16), "THS": (8, F32), "GI": (5 * 512, F16), "GO": (5 * 768, F16), "GL": (256, F32),
-    "ZI": (5 * 256, F16), "ZO": (5 * 256, F16), "ZF": (256, F32), "BK": (5 * 512, F16), "BO": (5 * 512, F16),
+    "XT": (8208, BF), "HN": (256, I32), "GT": (256, I32), "ZS": (256, I32), "QS": (1024, I32), "TH": (4, I32),
+    "HO": (5 * 272, F16), "HI": (4 * 256, F16), "THS": (8, F32), "GI": (5 * 768, F16), "GO": (5 * 1024, F16), "GL": (256, F32),
+    "ZF": (256, F32), "BK": (5 * 512, F16), "BO": (5 * 512, F16),
     "W": (1024, F32), "X": (4096, BF), "D": (4096, BF), "AB": (4096, BF),
     "OX": (256, U16), "OY": (256, U16), "OM": (256, U16), "OC": (5 * 32, U16),
     "IA": (768, I32), "IB": (256, I32), "IC": (256, I32), "IT": (32, I32),
-    "M": (1024, BF), "F2": (512, F16), "E": (1024, F16), "SO": (1024, F16), "TM": (768, F32), "DE": (512, F32),
-    "FT": (1024, F16), "U": (256, F32), "RFI": (512, F16), "EB": (5 * 512, F16),
-    "V": (144, I32), "VB": (128, I32), "VP": (4, I32), "PC": (4, F32), "VJ": (16, F32), "JT": (16, F32), "JW": (144, F16),
+    "M": (1024, BF), "F2": (512, F16), "E": (1024, BF), "SO": (1024, F16), "AC": (768, F32),
+    "FT": (1024, F16), "RFI": (512, F16), "EB": (5 * 512, F16),
+    "VP": (8, I32), "VR": (32, I32), "PC": (8, F32), "SC": (48, F32), "VJ": (16, F32), "JT": (16, F32), "TAB": (584, BF),
     "C16": (128 * len(M16), F16), "CB": (128 * len(MBF), BF), "C32": (128, F32), "T": (5 * 128, BF), "TS": (5 * 128, BF),
-    "ORD": (144, BF), "BI": (8, I32), "BT": (8, F32), "Z1": (144, BF), "Z2": (144, F16), "ZT": (144, F16),
-    "RS": (1024, BF), "ET": (512, BF), "ZO1": (512, BF), "CN": (128, F16),
+    "ORD": (144, BF), "BT": (8, F32), "Z1": (56, BF), "Z2": (144, F16),
+    "RS": (1024, BF), "ET": (512, BF), "ZO1": (512, BF), "RT": (512, BF), "CN": (128, F16),
 }
 SCRATCH = {k: ("sbuf", [128, n], d) for k, (n, d) in SB.items()}
 for _b in range(8):
     SCRATCH["P%d" % _b] = ("psum", [128, 512], F32)
 BIG = 8192.0
-REG = dict(S=(0, 0), pe=(0, 0), lx=(0, 0), gc=(0, 1), X1=(0, 0),
-           c=(1, 0), D=(1, 1), ft=(1, 0), ut=(1, 0), u=(1, 1),
-           P2=(2, 0), lin=(2, 2), mc=(2, 3), PB=(2, 0), X2=(2, 2),
-           pd=(3, 0), mi=(3, 0), zn=(3, 1), pz=(3, 3), mg=(3, 0))
+REG = dict(S=(0, 0), pe=(0, 0), lx=(0, 0), gc=(0, 1), u=(0, 0),
+           c=(1, 0), D=(1, 1), ft=(1, 0), ut=(1, 0),
+           P2=(2, 0), lin=(2, 2), rc=(2, 3), PB=(2, 0), X2=(2, 2),
+           pd=(3, 0), zn=(3, 1), pz=(3, 0), mc=(2, 3), mg=(3, 0))
 
-PARAMS = dict(ns=2, modes=[[("a", 64), ("a", 32), ("d", 32)]] * 3, sch=64, seed=0, iters=300,
-              x0=[("act", 32), ("dve", 32)] * 2, xs=[("act", 64)] * 2, ts=[("act", 64)] * 2,
-              t4=[("act", 32), ("dve", 32)] * 2, act=("U", "BO", "RFI", "EB", "ZN", "ZO", "GO", "OX", "OM", "ZF"), cpx=False, cpy=False, scan=True,
-              loads=("hn", "gt", "xt", "zs", "qs"),
-              lead=8000.0, sweeps=5, win=22000.0, tries=1500, amp=7000.0, temp=600.0)
-COST = dict(f=1.1, gc=1.56, pe=0.45, ov=60.0, hop=200.0, same=110.0, net=3000.0, iss=800.0, bw=200.0)
+PARAMS = dict(ns=2, modes=[[("a", 32, 32), ("d", 32), ("d", 32)]] * 3, sums=[(64, 0, 96)] * 3, sch=64,
+              cut=[[(0, 128)], [(64, 64), (0, 64)], [(64, 64), (0, 64)]],
+              x0=[("act", 32), ("dve", 32)] * 2, xs=[("dve", 32), ("act", 32)] * 2, ts=[("dve", 32), ("act", 32)] * 2,
+              t4=[("act", 32), ("dve", 32)] * 2, act=("BO", "RFI", "EB", "ZN", "ZO", "GO", "OX", "OM", "ZF"), cpx=True, cpy=False, one=False,
+              loads=(("zs", 0), ("hn", 0), ("gt", 0), ("qs", 0), ("xt", 0), ("hn", 1), ("gt", 1), ("zs", 1), ("qs", 1), ("xt", 1)),
+              seed=4, iters=60, lead=3500.0, sweeps=2, win=11000.0, tries=2000, amp=3000.0, temp=300.0, flip=0.3,
+              passes=2, span=150, moves=2000, idle=500, ten=8, reach=6)
+COST = dict(f=1.1, gc=1.56, pe=0.5, ov=60.0, hop=200.0, same=110.0, net=4000.0, iss=800.0, bw=200.0)
 
 
 def A(name, a, n, step=1, ind=None):
     return (name, a, a + (n - 1) * step + 1, step, ind)
+
+
+def part(ap, a, n):
+    return A(ap[0], ap[1] + a * ap[3], n, ap[3])
 
 
 def is_ap(x):
@@ -89,7 +95,8 @@ def build(par):
                 hist[nm] = keep
         deps.discard(i)
         order.discard(i)
-        ops.append(dict(eng=eng, ins=ins, deps=deps, order=order - deps, sem=sem, peer=peer, nbytes=nbytes, st=cur[0]))
+        ops.append(dict(eng=eng, ins=ins, deps=deps, order=order - deps, sem=sem, peer=peer, nbytes=nbytes, st=cur[0],
+                        free=ins[0][0] in ("gat", "cv") and all(x[0] in SB for x in rd + writes)))
 
     def tt(o, a, b, op): add("dve", [("tt", o, a, b, op)], [a, b], [o])
     def ts(o, a, s1, op0, s2=None, op1=None): add("dve", [("ts", o, a, s1, s2, op0, op1)], [a, s1, s2], [o])
@@ -102,112 +109,117 @@ def build(par):
     def sel(o, a, pat, op, fill, base, cm): add("pool", [("sel", o, a, pat, op, fill, base, cm)], [a], [o])
 
     def mm(terms, first=True, last=True):
-        ins = [("mm", o, l, r, first and j == 0, last and j == len(terms) - 1) for j, (o, l, r) in enumerate(terms)]
+        ins = [("mm", o, l, r, first and j == 0, last and o[5:] not in [x[0][5:] for x in terms[j + 1:]]) for j, (o, l, r) in enumerate(terms)]
         add("pe", ins, [x for t in terms for x in t[1:]], [t[0] for t in terms])
 
     def dma(o, a, sem, nbytes, eng="sp"): add(eng, [("dma", o, a)], [a], [o], sem=sem, nbytes=nbytes)
     def send(o, a, sem, peer): add("pool", [("send", o, a)], [a], [o], sem=sem, peer=peer)
 
     def conv(o, a, tag, bias=0.0, scale=1.0, relu=False):
-        if tag in par["act"]:
-            act(o, a, ACT.Relu if relu else ACT.Identity, bias=bias, scale=scale)
-        elif relu:
-            ts(o, a, bias, ALU.add, 0.0, ALU.max)
-        elif scale != 1.0:
-            ts(o, a, scale, ALU.mult, bias, ALU.add)
-        elif bias:
-            ts(o, a, bias, ALU.add)
-        else:
-            cp(o, a)
+        add("act" if tag in par["act"] else "dve", [("cv", o, a, bias, scale, relu)], [a], [o])
 
     def index(tmp, a, b, lin):
         tt(tmp, a, b, ALU.mult)
         tt(tmp, tmp, lin, ALU.add)
         ts(tmp, tmp, 5, ALU.arith_shift_right, 4095, ALU.bitwise_and)
 
-    for src in par["loads"]:
+    for src, s in par["loads"]:
         if src == "qs":
-            for s in range(nst):
-                for b in range(2):
-                    dma(A("QS", 2 * LN * (2 * s + b), 2 * LN), A("qs", 512 * b + 2 * LN * s, 2 * LN), "lq%d%d" % (s, b), 1024 * LN)
+            for b in range(2):
+                dma(A("QS", 2 * LN * (2 * s + b), 2 * LN), A("qs", 512 * b + 2 * LN * s, 2 * LN), "lq%d%d" % (s, b), 1024 * LN)
+        elif src == "xt":
+            dma(A("XT", 4096 * s, 4096), A("xt", 0, 4096), "lx%d" % s, 1 << 20)
+        elif s < 0:
+            dma(A(src.upper(), 0, 256), A(src, 0, 256), "l" + src, 512 * 256)
         else:
-            n = 4096 if src == "xt" else 256
-            dma(A(src.upper(), 0, n), A(src, 0, n), "l" + src, 1 << (20 if src == "xt" else 17))
-    iota(A("V", 0, 144), [[1, 144]], 128, -1)
-    iota(A("VB", 0, 128), [[16, 8], [0, 16]], 15, -1)
+            dma(A(src.upper(), LN * s, LN), A(src, LN * s, LN), "l%s%d" % (src, s), 512 * LN)
     iota(A("VP", 0, 1), [[0, 1]], 0, 1)
+    iota(A("VP", 1, 1), [[0, 1]], 0, 16)
+    iota(A("VR", 0, 16), [[-1, 16]], 16, 1)
+    iota(A("VR", 16, 16), [[-1, 16]], 16, 0)
+    COL, CG, CX = (A("TAB", 128 * j, 128) for j in range(3))
+    iota(COL, [[1, 128]], 0, 0)
+    iota(CG, [[16, 8], [0, 16]], 0, 0)
+    iota(CX, [[16, 128]], 0, 0)
+    iota(A("TAB", 384, 144), [[2, 72], [0, 2]], -14, 0)
+    iota(A("TAB", 528, 56), [[16, 56]], -384, 0)
     iota(A("VJ", 0, 16), [[16, 16]], 0, 0)
-    iota(A("BI", 0, 5), [[-1, 5]], 16, 1)
     iota(A("ORD", 0, 144), [[0, 9], [1, 16]], 0, 0)
-    dma(A("TH", 0, 1), A("th", 0, 1), "lth", 512, eng="pool")
+    dma(A("TH", 0, 1), A("th", 0, 1), "lth", 0, eng="pool")
     iota(A("RS", 0, 1024), [[0, 64], [256, 16]], 0, 0)
     C = {k: A("C16", 128 * j, 128) for j, k in enumerate(M16)}
     C.update({k: A("CB", 128 * j, 128) for j, k in enumerate(MBF)})
     I32m = A("C32", 0, 128)
-    ts(A("VP", 0, 1), A("VP", 0, 1), 15, ALU.bitwise_and)
-    PC = A("PC", 0, 1)
-    cp(PC, A("VP", 0, 1))
-    ts(A("JT", 0, 16), A("VJ", 0, 16), PC, ALU.add)
-    ts(A("ZT", 0, 144), A("V", 0, 144), PC, ALU.add, 143.0, ALU.is_equal)
-    act(A("Z1", 0, 144), A("ZT", 0, 144), ACT.Copy)
-    tt(A("JW", 0, 143), A("ZT", 0, 143), A("ZT", 1, 143), ALU.add)
-    act(A("Z2", 0, 143), A("JW", 0, 143), ACT.Identity, scale=2.0 * LN)
-    ts(A("V", 0, 144), A("V", 0, 144), 15, ALU.bitwise_and)
-    ts(A("JW", 0, 144), A("V", 0, 144), 0.0, ALU.is_equal)
-    ts(A("VB", 0, 128), A("VB", 0, 128), 4, ALU.arith_shift_right)
-    PB1, PBK = A("P7", 0, 128), A("P7", 128, 128)
-    ts(PB1, A("VB", 0, 128), 0.0, ALU.is_equal)
-    ts(PBK, A("VB", 0, 128), 0.0, ALU.is_equal, -BIG, ALU.mult)
-    ts(C["B"], A("VB", 0, 128), 0.0, ALU.is_equal)
-    for k, r in (("P0", 0), ("P5", 5), ("P6", 6), ("P11", 11), ("P15", 15), ("P4", 4), ("K10", 10)):
-        tt(C[k], A("JW", r, 128), PB1, ALU.mult)
-    ts(A("BI", 0, 5), A("BI", 0, 5), 15, ALU.bitwise_and)
-    ts(A("BT", 0, 5), A("BI", 0, 5), -256.0, ALU.mult, -128.0, ALU.add)
+    for j, (src, n, op) in enumerate(((0, 15, ALU.bitwise_and), (0, 112, ALU.bitwise_and), (0, 3, ALU.arith_shift_right),
+                                      (0, 7, ALU.bitwise_and), (1, 112, ALU.bitwise_and))):
+        ts(A("VP", 2 + j, 1), A("VP", src, 1), n, op)
+    cp(A("PC", 0, 5), A("VP", 2, 5))
+    K, G16, K8, G8, E16 = (A("PC", j, 1) for j in range(5))
+    ts(A("PC", 5, 1), K, 128.0, ALU.mult, G16, ALU.add)
+    ts(A("VR", 16, 16), A("VR", 16, 16), K8, ALU.add)
+    ts(A("VR", 0, 32), A("VR", 0, 32), 15, ALU.bitwise_and)
+    ts(A("SC", 0, 16), A("VR", 0, 16), G16, ALU.add)
+    ts(A("SC", 16, 16), A("VR", 16, 16), E16, ALU.add)
+    ts(A("SC", 32, 16), A("VR", 16, 16), 8.0, ALU.mult, G8, ALU.add)
+    ts(A("BT", 0, 5), A("VR", 16, 5), -256.0, ALU.mult)
+    ts(A("JT", 0, 16), A("VJ", 0, 16), K, ALU.add)
+
+    def where(o, tab, s, c):
+        ts(o, tab, s, ALU.is_equal, c, ALU.mult)
+
+    for k, j, c in (("P0", 0, 1.0), ("La", 0, 2080.0), ("Lb", 0, 3232.0), ("P5", 5, 1.0), ("P6", 6, 1.0), ("P10", 10, 1.0),
+                    ("P15", 15, 1.0), ("P4", 4, 1.0), ("K16", 16, 2 * BIG), ("nK6", 22, -BIG), ("nK11", 27, -BIG),
+                    ("KN", 31, BIG), ("KL", 20, BIG), ("K5", 37, BIG), ("K10", 42, BIG)):
+        where(C[k], COL, A("SC", j, 1), c)
+    where(C["nX"], CX, A("PC", 5, 1), -1.0)
+    where(C["B"], CG, G16, 1.0)
+    where(C["Bb"], CG, E16, 1.0)
+    where(A("Z2", 0, 144), A("TAB", 384, 144), G16, 2.0 * LN)
+    where(A("Z1", 0, 56), A("TAB", 528, 56), G16, 1.0)
+    PBK = A("P7", 0, 128)
+    where(PBK, CG, E16, -BIG)
+    tt(PBK, C["K16"], PBK, ALU.add)
     for t in range(NV):
         act(A("TS", 128 * t, 128), A("ORD", 16 - t, 128), ACT.Sigmoid, bias=A("BT", t, 1), scale=256.0)
         tt(A("T", 128 * t, 128), A("TS", 128 * t, 128), PBK, ALU.mult)
-    for a, n in ((0, 1), (1, NV - 1)):
-        sel(A("T", 128 * a, 128 * n), A("T", 128 * a, 128 * n), [[0, n], [-1, 128]], ALU.not_equal, 4096.0, 0, 1)
-    for j, (k, a, c) in enumerate((
-            ("La", "P0", 2080.0), ("Lb", "P0", 3232.0), ("nI", "P0", -1.0), ("Ib", "P0", 1.0), ("nIb", "P0", -1.0),
-            ("nB", "B", -1.0), ("K0", "P0", BIG), ("K5", "P5", BIG), ("K10", "K10", BIG), ("nK0", "P0", -BIG),
-            ("nK6", "P6", -BIG), ("nK11", "P11", -BIG), ("K4", "P0", 4096.0), ("nK4", "P0", -4096.0), ("K1", "P0", 1024.0),
-            ("Bb", "B", 1.0), ("nB256", "B", -256.0), ("B2k", "B", 2048.0), ("Q15", "P15", 32.0), ("Q4", "P4", 32.0))):
-        if j % 2:
-            act(C[k], C[a], ACT.Identity, scale=c)
-        else:
-            ts(C[k], C[a], c, ALU.mult)
+    for k, a, c in (("nI", "P0", -1.0), ("nB", "B", -1.0), ("nK0", "K16", -0.5), ("X4", "K16", 0.25), ("nK16", "K16", -1.0), ("nB256", "Bb", -256.0),
+                    ("B2k", "B", 2048.0), ("Q0", "P0", 32.0), ("nKN", "KN", -1.0), ("nKL", "KL", -1.0)):
+        act(C[k], C[a], ACT.Identity, scale=c)
     act(I32m, C["P0"], ACT.Copy)
-    ms(A("XT", 4096, 16), 0.0)
-    ms(A("ET", 0, 2 * LN), -2048.0)
-    ms(A("ET", 2 * LN, 2 * LN), BIG - 2048.0)
-    ms(A("ZO1", 0, 2 * LN), 0.0)
-    ms(A("ZO1", 2 * LN, 2 * LN), 1.0)
-    ms(A("CN", 0, LN), -1280.0)
-    ONE = A("ZO1", 2 * LN, LN)
-    KR = {0: C["K0"], 5: C["K5"], 10: C["K10"]}
-    XW, XZ = ("XT", 0, 4096, 1), ("XT", 0, 4112, 1)
+    iota(A("ZO1", 0, LN), [[0, LN]], 0, 0)
+    iota(A("ZO1", LN, 2 * LN), [[0, 2 * LN]], 1, 0)
+    iota(A("RT", 0, 4 * LN), [[0, LN], [8192, 2], [0, 2]], -2048, 0)
+    ms(A("CN", 0, LN), -1022.0)
+    ONE = A("ZO1", LN, LN)
+    for k, c in (("Ib", 1.0), ("nIb", -1.0), ("K4", 4096.0), ("K1", 1024.0), ("KX", -5120 * BIG)):
+        sel(C[k], A("ZO1", 0, 128), [[-1, 128]], ALU.not_equal, c, 0, 1)
+    for k in ("K5", "K10"):
+        sel(C[k], C[k], [[-1, 128]], ALU.not_equal, BIG, 0, 1)
+    iota(A("XT", 8192, 16), [[0, 16]], 0, 0)
+    iota(A("ET", 0, 4 * LN), [[8192, 2], [0, 2 * LN]], -2048, 0)
+    XW, XZ = ("XT", 0, 4096, 1), ("XT", 0, 8208, 1)
 
     for s in range(nst):
         ts(A("HO", LN * s, LN), A("HN", LN * s, LN), -2048.0, ALU.add)
-        ts(A("GI", 2 * LN * s + LN, LN), A("GT", LN * s, LN), -2048.0, ALU.add)
-        ms(A("GI", 2 * LN * s, LN), 0.0)
-        act(A("ZI", LN * s, LN), A("ZS", LN * s, LN), ACT.Identity, bias=1024.0)
-        ms(A("M", 4 * LN * s + 3 * LN, LN), 1.0)
-        if par["scan"]:
-            ms(A("E", 4 * LN * s, 4 * LN), 0.0)
+        ts(A("GI", 3 * LN * s + LN, LN), A("GT", LN * s, LN), -2048.0, ALU.add)
+        ms(A("GI", 3 * LN * s, LN), 0.0)
+        act(A("GI", 3 * LN * s + 2 * LN, LN), A("ZS", LN * s, LN), ACT.Identity, bias=1024.0)
+        iota(A("E", 4 * LN * s, 4 * LN), [[0, 4 * LN]], 0, 0)
     ts(A("HO", 256, 1), A("TH", 0, 1), -2048.0, ALU.add)
-    ts(A("THS", 0, 1), A("TH", 0, 1), 256.0, ALU.mult, -128.0, ALU.add)
 
-    def turn_names(d):
-        mm([(A("P3", 0, 257), C["P15"], A("HO", 272 * (d - 1), 257))])
-        act(A("HO", 272 * d, 257), A("P3", 0, 257), ACT.Copy)
+    def thresholds(a, n):
+        mm([(A("P3", 0, n), C["nX"], A("HO", 272 * a + 256, n, 272))])
+        ts(A("THS", a, n), A("P3", 0, n), -256.0, ALU.mult, 2048 * 256.0 - 128.0, ALU.add)
+
+    def turn_names(d, o):
+        mm([(o, C["P15"], A("HO", 272 * (d - 1), 257))])
+        act(A("HO", 272 * d, 257), o, ACT.Copy)
         if d < NR:
             send(A("HI", 256 * d, 256), A("HO", 272 * d, 256), "h%d" % d, d)
+        else:
+            thresholds(1, NV - 1)
 
-    for d in range(1, NV):
-        turn_names(d)
-    ts(A("THS", 1, 4), A("HO", 272 + 256, 4, 272), 256.0, ALU.mult, 2048 * 256.0 - 128.0, ALU.add)
+    thresholds(0, 1)
 
     for t in range(NV):
         for s in range(nst):
@@ -220,11 +232,11 @@ def build(par):
                 return A("P%d" % (8 // nst * s + bk), col * LN + off, n, step)
 
             H = A("HI", 256 * t + l0, LN) if t % NR else A("HO", 272 * t + l0, LN)
-            CNT, G = A("GI", 512 * t + 2 * l0, LN), A("GI", 512 * t + 2 * l0 + LN, LN)
-            z0 = 256 * t + l0
-            Z = A("ZI", z0, LN)
+            i0 = 768 * t + 3 * l0
+            CNT, G, Z = (A("GI", i0 + LN * j, LN) for j in range(3))
             Ms = [A("M", 4 * l0 + LN * k, LN) for k in range(NS)]
-            TMs = [A("TM", 3 * l0 + LN * k, LN) for k in range(NS)]
+            ACs = [A("AC", 3 * l0 + LN * k, LN) for k in range(NS)]
+            way = {k: par[k][s] if isinstance(par[k], dict) else par[k] for k in ("modes", "x0", "xs", "ts", "t4")}
             IAs = [A("IA", 3 * l0 + LN * k, LN) for k in range(NS)]
             IB, IC = A("IB", l0, LN), A("IC", l0, LN)
             Wn = ("QS" if t < 2 else "W", 4 * l0, 4 * l0 + 4 * LN, 1)
@@ -234,18 +246,15 @@ def build(par):
             index(IB, H, pr("gc") if par["cpx"] else G, pr("lx"))
             conv(A("OX", l0, LN), IB, "OX")
             a = 0
-            for eng, n in par["x0" if t == 0 else "xs"]:
+            for eng, n in way["x0" if t == 0 else "xs"]:
                 gat(A("X", c0 + 16 * a, 16 * n), XW + (A("OX", l0 + a, n),), eng)
                 a += n
             nt = LN // 8
             ut, IT, OC = pr("ut", 0, nt), A("IT", nt * s, nt), A("OC", 32 * t + nt * s, nt)
-            mm([(ut, A("Z2", 14 - 2 * a, 128), A("ZI", z0 + a, nt, 8)) for a in range(8)])
-            mm([(pr("u"), C["B"], Z)])
+            mm([(ut, A("Z2", 14 - 2 * a, 128), A("GI", Z[1] + a, nt, 8)) for a in range(8)])
             tt(IT, ut, A("JT", 0, nt), ALU.add)
             ts(IT, IT, 4 * LN - 1, ALU.bitwise_and)
             conv(OC, IT, "OC")
-            U = A("U", l0, LN)
-            conv(U, pr("u"), "U", 32.0 - 16384.0)
             RF, R, F = A("RFI", 2 * l0, 2 * LN), A("RFI", 2 * l0, LN, 2), A("RFI", 2 * l0 + 1, LN, 2)
             conv(RF, Wn + (OC,), "RFI", -2048.0)
             if t < NV - 1:
@@ -253,123 +262,109 @@ def build(par):
             for k in range(NS):
                 lin, IA = pr("lin"), IAs[k]
                 if par["cpy"]:
-                    mm([(pr("mc"), C["P0"], R)])
+                    mm([(pr("rc"), C["P0"], R)])
                 mm([(lin, C["La"], R), (lin, C["Lb"], F)])
-                index(IA, F, pr("mc") if par["cpy"] else R, lin)
-                conv(A("OY", l0, LN), IA, "OY")
+                for a, n in par["cut"][k]:
+                    index(part(IA, a, n), part(F, a, n), part(pr("rc") if par["cpy"] else R, a, n), part(lin, a, n))
+                    conv(A("OY", l0 + a, n), part(IA, a, n), "OY")
                 P2 = pr("P2", 0, 2 * LN)
                 c = pr("c")
-                mm([(c, C["nI"], CNT)] + [(c, KR[r], Ms[j]) for j in range(k) for r in (0, 5 * (k - j))], last=False)
-                a, done, extra, nd = 0, 0, [], 0
-                for mode, n in par["modes"][k]:
-                    y = XW + (A("OY", l0 + a, n),)
-                    x, d, ab = (A(nm, c0 + 16 * a, 16 * n) for nm in ("X", "D", "AB"))
+                mm([(c, C["nX"], CNT)] + [(c, C["K%d" % (5 * (k - j))], Ms[j]) for j in range(k)], last=False)
+                mc = pr("mc")
+                mm([(pr("P2"), C["P0"], H), (pr("P2", LN), C["P0"], R)], last=False)
+                mm([(mc, I32m, ACs[k - 1]), (mc, C["X4"], Ms[k - 1])] if k else [(mc, C["KN"], ONE)], first=False, last=False)
+                a, nd, sums = 0, 0, {}
+                for mode, *parts in way["modes"][k]:
+                    n = sum(parts)
                     if mode == "d":
-                        act(d, y, ACT.Copy)
-                        for b in range(0, 16 * n, 512):
-                            pd, w = pr(("pd", "pe")[nd % 2], 0, min(512, 16 * n - b)), min(512, 16 * n - b)
+                        act(A("D", c0 + 16 * a, 16 * n), XW + (A("OY", l0 + a, n),), ACT.Copy)
+                    for w in parts:
+                        x, d, ab = (A(nm, c0 + 16 * a, 16 * w) for nm in ("X", "D", "AB"))
+                        if mode == "d":
+                            pd = pr(("pd", "pe")[nd % 2], 0, 16 * w)
                             nd += 1
-                            mm([(pd, C["nIb"], A("X", x[1] + b, w))], last=False)
-                            mm([(pd, C["Ib"], A("D", x[1] + b, w))], first=False)
-                            act(A("AB", x[1] + b, w), pd, ACT.Abs)
-                    else:
-                        tt(d, y, x, ALU.subtract)
-                        if mode == "a":
-                            act(ab, d, ACT.Abs)
+                            mm([(pd, C["nIb"], x)], last=False)
+                            mm([(pd, C["Ib"], d)], first=False)
+                            act(ab, pd, ACT.Abs)
+                            sums[a] = w
                         else:
-                            ts(ab, d, -2.0, ALU.mult, 0.0, ALU.max)
-                            extra.append((a, n))
-                    a += n
-                    while len(extra) > 1 and extra[-2][0] + extra[-2][1] == extra[-1][0]:
-                        extra[-2:] = [(extra[-2][0], extra[-2][1] + extra[-1][1])]
-                    if a - done >= 64 or a == LN:
-                        for ea, en in extra:
-                            mm([(pr("c", ea, en), A("Z1", 15 - j, 128), A("D", c0 + 16 * ea + j, en, 16)) for j in range(16)],
-                               first=False, last=False)
-                        mm([(pr("c", done, a - done), A("Z1", 15 - j, 128), A("AB", c0 + 16 * done + j, a - done, 16))
-                            for j in range(16)], first=False, last=a == LN)
-                        done, extra = a, []
+                            tt(d, XW + (A("OY", l0 + a, w),), x, ALU.subtract)
+                        a += w
+                    if mode == "a":
+                        act(A("AB", c0 + 16 * (a - n), 16 * n), A("D", c0 + 16 * (a - n), 16 * n), ACT.Abs)
+                        sums[a - n] = n
+                for b, a in enumerate(par["sums"][k]):
+                    mm([(pr("c", a, sums[a]) + (32 * (j // 4),), A("Z1", 24 - 8 * (j % 4), 32), A("AB", c0 + 16 * a + j, sums[a], 16))
+                        for j in range(16)], first=False, last=b == len(sums) - 1)
                 M, Tt = Ms[k], A("T", 128 * t, 128)
                 act(M, c, ACT.Sigmoid, bias=A("THS", t, 1), scale=-256.0)
-                for hf, src in enumerate((H, R)):
-                    o = pr("P2", LN * hf)
-                    mm([(o, C["P0"], src), (o, Tt, M)])
-                mm([(pr("mc"), C["Ib"], M)])
+                mm([(pr("P2", LN * hf), Tt, M) for hf in range(2)] + [(mc, C["nK16"], M)], first=False)
                 fH, fR = A("F2", 2 * l0, LN), A("F2", 2 * l0 + LN, LN)
                 ts(A("F2", 2 * l0, 2 * LN), P2, -4096.0, ALU.add, -2048.0, ALU.max)
-                tt(TMs[k], IA, pr("mc"), ALU.mult)
+                tt(ACs[k] if k < NS - 1 else A("OM", l0, LN), IA, mc, ALU.max)
+                if t == s == 0 and k < 2:
+                    for d in (1, 2):
+                        turn_names(d + 2 * k, pr("pd", 0, 257))
                 rot = C["P5" if k < NS - 1 else "P0"]
                 mm([(pr("D", 0, 2 * LN), rot, RF)], last=False)
                 mm([(pr("D", hf, LN, 2), C["nB"], fR) for hf in range(2)], first=False)
-                if par["scan"]:
-                    mm([(pr("S", 1, 2 * LN, 2), rot, RF)])
-                    for hf in range(2):
-                        mm([(pr("S", 2 * hf, LN, 4), C["B"], fH), (pr("S", 2 * hf, LN, 4), C["nB"], fR)])
-                    ts(A("E", 4 * l0 + 1, 2 * LN, 2), pr("D", 0, 2 * LN), 30720.0, ALU.is_equal)
-                    scan(A("SO", 4 * l0, 4 * LN), A("E", 4 * l0, 4 * LN), pr("S", 0, 4 * LN), ALU.mult, ALU.add)
-                    RF, R, F = A("SO", 4 * l0 + 1, 2 * LN, 2), A("SO", 4 * l0 + 1, LN, 4), A("SO", 4 * l0 + 3, LN, 4)
-                else:
-                    mm([(pr("S", 0, 2 * LN), rot, RF)])
-                    for hf in range(2):
-                        mm([(pr("S", 2 * LN + hf, LN, 2), C["B"], fH), (pr("S", 2 * LN + hf, LN, 2), C["nB"], fR)])
-                    Eq, DE = A("E", 4 * l0, 2 * LN), A("DE", 2 * l0, 2 * LN)
-                    ts(Eq, pr("D", 0, 2 * LN), 30720.0, ALU.is_equal)
-                    tt(DE, Eq, pr("S", 2 * LN, 2 * LN), ALU.mult)
-                    RF, R, F = A("SO", 4 * l0, 2 * LN), A("SO", 4 * l0, LN, 2), A("SO", 4 * l0 + 1, LN, 2)
-                    tt(RF, DE, pr("S", 0, 2 * LN), ALU.add)
+                mm([(pr("S", 1, 2 * LN, 2), rot, RF)])
+                for hf in range(2):
+                    mm([(pr("S", 2 * hf, LN, 4), C["B"], fH), (pr("S", 2 * hf, LN, 4), C["nB"], fR)])
+                ts(A("E", 4 * l0 + 1, 2 * LN, 2), pr("D", 0, 2 * LN), 30720.0, ALU.is_equal)
+                scan(A("SO", 4 * l0, 4 * LN), A("E", 4 * l0, 4 * LN), pr("S", 0, 4 * LN), ALU.mult, ALU.add)
+                RF, R, F = A("SO", 4 * l0 + 1, 2 * LN, 2), A("SO", 4 * l0 + 1, LN, 4), A("SO", 4 * l0 + 3, LN, 4)
             more = t < NV - 1
-            g0 = 768 * t + 3 * l0
-            zn, ZN, pz, mi = pr("zn"), A("GO", g0, LN), pr("pz"), pr("mi")
+            g0 = 1024 * t + 4 * l0
+            zn, ZN, pz = pr("zn"), A("GO", g0, LN), pr("pz")
             mm([(zn, C["P0"], Z)] + [(zn, C["nB256"], m) for m in Ms])
             if more:
                 mm([(pr("zn", LN), C["K1"], ONE)] + [(pr("zn", LN), C["Bb"], m) for m in Ms])
-            mm([(mi, C["nK4"], m) for m in Ms] + [(mi, I32m, m) for m in TMs[:2]], last=False)
-            mm([(mi, I32m, TMs[2])], first=False)
-            conv(A("OM", l0, LN), mi, "OM", 4096.0)
             nz = 2 * LN if more else LN
             conv(A("GO", g0, nz), pr("zn", 0, nz), "ZN", -1024.0, relu=True)
             a = 0
-            for eng, n in par["ts" if more else "t4"]:
+            for eng, n in way["ts" if more else "t4"]:
                 gat(A("D", c0 + 16 * a, 16 * n), XZ + (A("OM", l0 + a, n),), eng)
                 a += n
             for a in range(0, LN, par["sch"]):
                 scan(*(A(nm, b + 16 * a, 16 * par["sch"]) for nm, b in (("AB", c0), ("RS", -16 * a), ("D", c0))), ALU.min, ALU.max)
             mm([(pz, C["P0"], Z), (pz, C["P0"], ZN)], last=False)
             mm([(pz, C["Ib"], A("AB", c0 + 15, LN, 16))], first=False)
-            ZO = A("ZO", z0, LN)
+            ZO = A("GO", g0 + 3 * LN, LN)
             conv(ZO, pz, "ZO", 511.75, 0.5)
-            if more:
-                send(A("ZI", z0 + 256, LN), ZO, "z%d%d" % (t, s), 1)
-            else:
+            if more and not par["one"]:
+                send(A("GI", Z[1] + 768, LN), ZO, "z%d%d" % (t, s), 1)
+            if not more:
                 conv(A("ZF", l0, LN), ZO, "ZF", -1024.0)
                 dma(A("yz", l0, LN), A("ZF", l0, LN), "sz%d" % s, 512 * LN)
             if t > 0:
-                for hf, src in enumerate((R, F)):
-                    o = pr("PB", hf, LN, 2)
-                    mm([(o, C[nk], m) for nk, m in zip(("nK0", "nK11", "nK6"), Ms)] + [(o, C["P6"], src)])
+                o = pr("PB", 0, 2 * LN)
+                mm([(pr("PB", hf, LN, 2), C[nk], m) for nk, m in zip(("nK0", "nK11", "nK6"), Ms) for hf in range(2)], last=False)
+                mm([(o, C["P6"], RF)], first=False)
                 BO, BK = A("BO", 512 * t + 2 * l0, 2 * LN), A("BK", 512 * t + 2 * l0, 2 * LN)
                 conv(BO, pr("PB", 0, 2 * LN), "BO")
                 send(BK, BO, "b%d%d" % (t, s), NR - 1)
-            o = pr("ft", 3 * LN)
-            mm([(pr("ft", 0, 4 * LN), C["K0"], A("M", 4 * l0, 4 * LN)), (o, C["P0"], G)] + [(o, C["nK0"], m) for m in Ms], last=False)
-            mm([(pr("ft", LN * k), C[r], F) for k, r in enumerate(("P6", "P11", "P0"))], first=False)
-            ts(A("FT", 4 * l0, 4 * LN), pr("ft", 0, 4 * LN), -BIG, ALU.add, -2048.0, ALU.max)
-            FT = [A("FT", 4 * l0 + LN * k, LN) for k in range(4)]
-            X1, X2 = pr("X1"), pr("X2")
-            mm([(X1, C["K4"], ONE)], last=False)
-            mm([(X1, C["P15" if more else "P4"], f) for f in FT[:3]], first=False)
-            mm([(X2, C["B2k"], Z), (X2, C["B2k"], A("CN", 0, LN))], last=False)
-            mm([(X2, C["Q15" if more else "Q4"], FT[3])], first=False)
-            index(IC, U, X1, X2)
+            ft = [pr("ft", k, LN, 4) for k in range(4)]
+            turn, kp, kn = (("P5", "P10", "P15"), C["KN"], C["nKN"]) if more else (("P10", "P15", "P4"), C["KL"], C["nKL"])
+            mm([(ft[0], C[turn[2]], G)] + [(ft[0], kn, m) for m in Ms]
+               + [(o, w, m) for o, x in zip(ft[1:], Ms) for w, m in ((kp, x), (C["nK0"], ONE))], last=False)
+            mm([(o, C[r], F) for o, r in zip(ft[1:], turn)], first=False)
+            scan(A("FT", 4 * l0, 4 * LN), A("RT", 0, 4 * LN), pr("ft", 0, 4 * LN), ALU.min, ALU.max)
+            U, X2 = pr("u"), pr("X2")
+            mm([(U, C["B"], Z), (U, C["B"], A("CN", 0, LN))])
+            mm([(X2, C["B2k"], Z), (X2, C["KX"], ONE)], last=False)
+            mm([(X2, C["Q0"], A("FT", 4 * l0, LN, 4))], first=False)
+            index(IC, A("FT", 4 * l0 + 3, LN, 4), U, X2)
             if more:
                 conv(A("GO", g0 + 2 * LN, LN), IC, "GO", -2048.0)
-                send(A("GI", 512 * (t + 1) + 2 * l0, 2 * LN), A("GO", g0 + LN, 2 * LN), "g%d%d" % (t, s), 1)
+                n = (2 + par["one"]) * LN
+                send(A("GI", i0 + 768, n), A("GO", g0 + LN, n), "g%d%d" % (t, s), 1)
             else:
                 conv(A("GL", l0, LN), IC, "GO")
                 dma(A("yg", l0, LN), A("GL", l0, LN), "sg%d" % s, 512 * LN)
             if t > 0:
                 EB, o0, o1 = A("EB", 512 * (t - 1) + 2 * l0, 2 * LN), pr("mg", 0, 2 * LN), pr("mg", 2 * LN, 2 * LN)
-                mm([(pr("mg", 0, 4 * LN), C["K4"], A("ZO1", 0, 4 * LN)), (o0, C["P0"], EB), (o1, C["nI"], EB)], last=False)
+                mm([(o1, C["K4"], A("ZO1", LN, 2 * LN)), (o0, C["P0"], EB), (o1, C["nI"], EB)], last=False)
                 mm([(o0, C["nI"], BK), (o1, C["nI"], BK)], first=False)
                 Wa = A("W", 4 * l0, 4 * LN)
                 tt(Wa, A(Wn[0], 4 * l0, 4 * LN), pr("mg", 0, 4 * LN), ALU.min)
@@ -388,7 +383,7 @@ def cost(op, eng, C):
     cy, i = 0.83 * C["f"], op["ins"][0]
     k = i[0]
     if k == "mm":
-        return sum(max(64, width(j[3])) * (4 if size(j[3]) == 4 else 1) for j in op["ins"]) * C["pe"] * C["f"] + 20, 0
+        return sum(max(min(64, width(j[2])), width(j[3])) * (4 if size(j[3]) == 4 else 1) for j in op["ins"]) * C["pe"] * C["f"] + 20, 0
     if k == "dma":
         return (100 if eng == "sp" else 1500), 2000
     if k == "send":
@@ -440,20 +435,25 @@ def schedule(ops, par, C):
         dur[i], lat[i] = cost(o, engs[i], C)
         if o["ins"][0][0] == "dma":
             cum = (cum if o["st"] < 0 else 0.0) + o["nbytes"] / C["bw"]
-            lat[i] += cum
-    pred, succ = [[] for _ in range(n + 1)], [[] for _ in range(n + 1)]
-    last = None
-    for i, o in enumerate(ops):
-        e = [(d, lat[d] + (C["hop"] if ops[d]["sem"] or engs[d] != engs[i] else 0 if engs[i] == "pe" else C["same"])) for d in o["deps"]]
-        e += [(d, 0.0) for d in o["order"]]
-        if engs[i] == "sp" and o["st"] < 0:
-            e += [(last, 0.0)] if last is not None else []
-            last = i
-        for d, lag in e:
-            pred[i].append((d, lag))
-            succ[d].append((i, lag))
-        pred[n].append((i, lat[i]))
-        succ[i].append((n, lat[i]))
+            lat[i] += cum if o["nbytes"] else 0.0
+    pred, succ = [], []
+
+    def edges():
+        pred[:], succ[:] = [[] for _ in range(n + 1)], [[] for _ in range(n + 1)]
+        last = None
+        for i, o in enumerate(ops):
+            e = [(d, lat[d] + (C["hop"] if ops[d]["sem"] or engs[d] != engs[i] else 0 if engs[i] == "pe" else C["same"])) for d in o["deps"]]
+            e += [(d, 0.0) for d in o["order"]]
+            if engs[i] == "sp" and o["st"] < 0:
+                e += [(last, 0.0)] if last is not None else []
+                last = i
+            for d, lag in e:
+                pred[i].append((d, lag))
+                succ[d].append((i, lag))
+            pred[n].append((i, lat[i]))
+            succ[i].append((n, lat[i]))
+
+    edges()
     dur, engs = dur + [1.0], engs + ["end"]
     rng = np.random.default_rng(par["seed"])
     pr = [0.0] * (n + 1)
@@ -503,29 +503,215 @@ def schedule(ops, par, C):
 
             cur = np.array([best[i] for i in ids] + [-1e9])
             cv = value(place(m + 1, topo_order(m + 1, sp, None, cur.tolist()), sp, sd, se))
-            bv, top = cv, cur
+            bv, top, tope = cv, cur, list(se)
+            free = [j for j, i in enumerate(ids) if ops[i]["free"] and not fixed[j]]
+
+            def flip(j):
+                se[j] = "act" if se[j] == "dve" else "dve"
+                sd[j] = cost(ops[ids[j]], se[j], C)[0]
+                for a, b in [(d, j) for d, _ in sp[j][:-1]] + [(j, pos[k]) for k, _ in succ[ids[j]] if k in pos]:
+                    if not ops[ids[a]]["sem"]:
+                        sp[b] = [(d, C["same" if se[a] == se[b] else "hop"] if d == a else lag) for d, lag in sp[b]]
+
             for it in range(par["tries"]):
-                near = (np.abs(cur - t0 - rng.random() * par["win"]) < 5000.0 * rng.random()) & ~fx
+                at = t0 + rng.random() * par["win"]
+                flips = []
+                if free and rng.random() < par["flip"]:
+                    flips = [free[int(rng.random() * len(free))]]
+                    at = cur[flips[0]]
+                    other = [j for j in free if se[j] != se[flips[0]] and abs(cur[j] - at) < 6000.0]
+                    if other and rng.random() < 0.5:
+                        flips.append(other[int(rng.random() * len(other))])
+                for j in flips:
+                    flip(j)
+                near = (np.abs(cur - at) < 5000.0 * rng.random()) & ~fx
                 key = cur + near * rng.random(m + 1) * par["amp"] * rng.random() - fx * 1e6
                 st = place(m + 1, topo_order(m + 1, sp, None, key.tolist()), sp, sd, se)
                 v = value(st)
                 if v <= cv + par["temp"] * (1.0 - it / par["tries"]) * rng.random():
                     cv, cur = v, np.array(st[:m] + [-1e9])
                     if cv < bv:
-                        bv, top = cv, cur
-            key = list(best)
+                        bv, top, tope = cv, cur, list(se)
+                else:
+                    for j in flips:
+                        flip(j)
+            key, was = list(best), (list(engs), list(dur))
             for j, i in enumerate(ids):
-                key[i] = float(top[j])
+                key[i], engs[i] = float(top[j]), tope[j]
+                dur[i] = cost(ops[i], engs[i], C)[0]
+            edges()
             st = forth(key)
             st2 = again(st)
             st = st2 if st2[n] < st[n] else st
             if st[n] < best[n]:
                 best = st
+            else:
+                engs[:], dur[:] = was
+                edges()
             t0 += par["win"] * (0.3 + 0.3 * rng.random())
+    best = polish(n + 1, [[(d, dur[d] + lag) for d, lag in p] for p in pred],
+                  [[(j, dur[i] + lag) for j, lag in p] for i, p in enumerate(succ)], dur, engs, best, par, rng)
     order = {e: [] for e in ("pe", "dve", "act", "pool", "sp")}
     for i in sorted(range(n), key=lambda i: (best[i], i)):
         order[engs[i]].append(i)
     return order, engs[:n], best
+
+
+def polish(n, pred, succ, dur, engs, start, par, rng):
+    order = sorted(range(n), key=lambda i: (start[i], i))
+    mp, ms, last = [-1] * n, [-1] * n, {}
+    for i in order:
+        if engs[i] in last:
+            mp[i], ms[last[engs[i]]] = last[engs[i]], i
+        last[engs[i]] = i
+    head, tail, jh, jt, pos = [0.0] * n, [0.0] * n, [0.0] * n, [0.0] * n, [0] * n
+
+    def heads(seq):
+        for i in seq:
+            t = 0.0
+            for d, w in pred[i]:
+                x = head[d] + w
+                if x > t:
+                    t = x
+            jh[i] = t
+            d = mp[i]
+            if d >= 0:
+                x = head[d] + dur[d]
+                if x > t:
+                    t = x
+            head[i] = t
+
+    def tails(seq):
+        for i in seq:
+            t = 0.0
+            for d, w in succ[i]:
+                x = tail[d] + w
+                if x > t:
+                    t = x
+            jt[i] = t
+            d = ms[i]
+            if d >= 0:
+                x = tail[d] + dur[i]
+                if x > t:
+                    t = x
+            tail[i] = t
+
+    def guess(seq, a, b):
+        t = head[a] + dur[a] if a >= 0 else 0.0
+        hs = []
+        for i in seq:
+            if jh[i] > t:
+                t = jh[i]
+            hs.append(t)
+            t += dur[i]
+        t, top = tail[b] if b >= 0 else 0.0, 0.0
+        for k in range(len(seq) - 1, -1, -1):
+            i = seq[k]
+            t += dur[i]
+            if jt[i] > t:
+                t = jt[i]
+            if t + hs[k] > top:
+                top = t + hs[k]
+        return top
+
+    def link(seq, p, q):
+        for i in seq:
+            mp[i] = p
+            if p >= 0:
+                ms[p] = i
+            p = i
+        ms[p] = q
+        if q >= 0:
+            mp[q] = p
+
+    def window(a, b):
+        win = order[a:b]
+        inside = set(win)
+        for k, i in enumerate(win):
+            pos[i] = k
+        mk = best = max(head[i] + tail[i] for i in win)
+        keep = (list(win), [mp[i] for i in win], [ms[i] for i in win])
+        tabu, idle, reach = {}, 0, par["reach"]
+        for it in range(par["moves"]):
+            lim = mk - 0.01
+            runs, seen = [], set()
+            for i in win:
+                if head[i] + tail[i] > lim and i not in seen:
+                    run, j = [i], ms[i]
+                    while j in inside and head[j] + tail[j] > lim and head[j] < head[run[-1]] + dur[run[-1]] + 0.01:
+                        run.append(j)
+                        seen.add(j)
+                        j = ms[j]
+                    if len(run) > 1:
+                        runs.append(run)
+            top = None
+            for run in runs:
+                k = len(run)
+                for x, y in sorted({(0, j) for j in range(1, min(k, reach))} | {(j, k - 1) for j in range(max(0, k - reach), k - 1)}):
+                    u, v = run[x], run[y]
+                    for late in ((0,) if y == x + 1 else (0, 1)):
+                        if late:
+                            if any(d == v or tail[d] > tail[v] for d, _ in succ[u]):
+                                continue
+                            seq = run[x + 1:y + 1] + [u]
+                            bad = any(tabu.get((w, u), -1) > it for w in seq)
+                        else:
+                            if any(d == u or head[d] >= head[u] + dur[u] for d, _ in pred[v]):
+                                continue
+                            seq = [v] + run[x:y]
+                            bad = any(tabu.get((v, w), -1) > it for w in seq)
+                        e = guess(seq, mp[u], ms[v])
+                        if bad and e >= best - 0.01:
+                            e += 1e6
+                        if top is None or e < top[0]:
+                            top = (e, late, u, v, seq)
+            if top is None:
+                break
+            _, late, u, v, seq = top
+            link(seq, mp[u], ms[v])
+            ten = it + par["ten"] + int(rng.random() * par["ten"])
+            lo, hi = pos[u], pos[v] + 1
+            seg = win[lo:hi]
+            if late:
+                tabu.update({(u, w): ten for w in seq[:-1]})
+                mark = {u}
+                for i in seg:
+                    if mp[i] in mark or any(d in mark for d, _ in pred[i]):
+                        mark.add(i)
+                seg = [i for i in seg if i not in mark] + [i for i in seg if i in mark]
+            else:
+                tabu.update({(w, v): ten for w in seq[1:]})
+                mark = {v}
+                for i in reversed(seg):
+                    if ms[i] in mark or any(d in mark for d, _ in succ[i]):
+                        mark.add(i)
+                seg = [i for i in seg if i in mark] + [i for i in seg if i not in mark]
+            win[lo:hi] = seg
+            for k in range(lo, hi):
+                pos[win[k]] = k
+            heads(win[lo:])
+            tails(win[hi - 1::-1])
+            mk = max(head[i] + tail[i] for i in win)
+            idle += 1
+            if mk < best - 0.01:
+                best, idle = mk, 0
+                keep = (list(win), [mp[i] for i in win], [ms[i] for i in win])
+            if idle > par["idle"]:
+                break
+        order[a:b] = keep[0]
+        for i, p, q in zip(*keep):
+            link([i], p, q)
+
+    for _ in range(par["passes"]):
+        a = 0
+        while a < n - 20:
+            heads(order)
+            order.sort(key=lambda i: head[i])
+            tails(order[::-1])
+            window(a, min(n, a + par["span"]))
+            a += int(par["span"] * (0.3 + 0.4 * rng.random()))
+    heads(order)
+    return head
 
 
 def topo_order(n, pred, succ, key):
@@ -562,7 +748,8 @@ def rank_program(g, core, T, topo):
     def ap(x):
         if not is_ap(x):
             return x
-        v = T[x[0]][:, x[1]:x[2]:x[3]] if x[3] > 1 else T[x[0]][:, x[1]:x[2]]
+        rows = slice(x[5], x[5] + 32) if len(x) > 5 else slice(0, 128)
+        v = T[x[0]][rows, x[1]:x[2]:x[3]] if x[3] > 1 else T[x[0]][rows, x[1]:x[2]]
         return v.indirect(ap(x[4])) if x[4] else v
 
     def engines(o, src_rank):
@@ -582,20 +769,23 @@ def rank_program(g, core, T, topo):
             elif i in needed:
                 total[e] = total.get(e, 0) + 1
                 mark[i] = (e, total[e])
+    seen, knew, waits = {e: {} for e in ORDER}, {}, {}
+    for i in sorted(range(len(OPS)), key=lambda i: (_T[i], i)):
+        e = ENGS[i]
+        waits[i] = []
+        for d in sorted(OPS[i]["deps"], key=lambda d: (-_T[d], -d)):
+            if not (e == "pe" and ENGS[d] == "pe") and seen[e].get(mark[d][0], 0) < mark[d][1]:
+                waits[i].append(mark[d])
+                for sm, n in knew[d].items():
+                    seen[e][sm] = max(seen[e].get(sm, 0), n)
+        if i in mark:
+            knew[i] = dict({} if OPS[i]["peer"] else seen[e], **{mark[i][0]: mark[i][1]})
     sent = 0
     for e, l in ORDER.items():
-        seen = {}
         for i in l:
             o = OPS[i]
-            want = {}
-            for d in o["deps"]:
-                if not (e == "pe" and ENGS[d] == "pe"):
-                    sm, n = mark[d]
-                    want[sm] = max(want.get(sm, 0), n)
-            for sm in sorted(want):
-                if seen.get(sm, 0) < want[sm]:
-                    q[e].wait_ge(T.sem[sm], want[sm])
-                    seen[sm] = want[sm]
+            for sm, n in waits[i]:
+                q[e].wait_ge(T.sem[sm], n)
             for j in o["ins"]:
                 k, x = j[0], [ap(y) for y in j[1:]]
                 if k == "mm":
@@ -608,6 +798,14 @@ def rank_program(g, core, T, topo):
                     r = g.vector.tensor_copy(*x)
                 elif k == "gat":
                     r = g.scalar.activation(x[0], x[1], ACT.Copy)
+                elif k == "cv" and e == "act":
+                    r = g.scalar.activation(x[0], x[1], ACT.Relu if x[4] else ACT.Identity, bias=x[2], scale=x[3])
+                elif k == "cv" and x[4]:
+                    r = g.vector.tensor_scalar(x[0], x[1], x[2], 0.0, ALU.add, ALU.max)
+                elif k == "cv" and x[2:4] == [0.0, 1.0]:
+                    r = g.vector.tensor_copy(x[0], x[1])
+                elif k == "cv":
+                    r = g.vector.tensor_scalar(x[0], x[1], x[3], x[2], ALU.mult, ALU.add)
                 elif k == "ms":
                     r = g.vector.memset(*x)
                 elif k == "scan":

@@ -3,38 +3,31 @@ from concourse.mybir import AluOpType as ALU, ActivationFunctionType as ACT
 
 NR, NV, NS = 4, 5, 3
 F32, BF, I32, U16, F16 = "float32", "bfloat16", "int32", "uint16", "float16"
-M16 = ("P0", "P5", "P6", "P10", "P15", "P4", "Q0", "La", "Lb", "nI", "nX", "B", "nB", "B2k")
-MBF = ("KN", "KL", "nKN", "nKL", "K5", "K10", "nK0", "nK6", "nK11", "K4", "X4", "K1", "K16", "nK16", "KX", "Ib", "nIb", "Bb", "nB256")
+M16 = ("P0", "P5", "P6", "P10", "P15", "P4", "La", "Lb", "nI", "nX", "B", "nB", "B2k",
+       "Da", "Db", "Dc", "nP15", "nP4", "Q15", "Q4")
+MBF = ("KN", "KL", "nKN", "nKL", "K5", "K10", "nK0", "nK6", "nK11", "X4", "K16", "nK16", "Ib", "nIb", "Bb",
+       "KB", "nKB", "KO", "nKO", "KE", "nKE", "c64", "cP", "cN", "c512", "cm16", "cm8")
 SB = {
     "XT": (8208, BF), "HN": (256, I32), "GT": (256, I32), "ZS": (256, I32), "QS": (1024, I32), "TH": (4, I32),
-    "HO": (5 * 272, F16), "HI": (4 * 256, F16), "THS": (8, F32), "GI": (5 * 768, F16), "GO": (5 * 1024, F16), "GL": (256, F32),
-    "ZF": (256, F32), "BK": (5 * 512, F16), "BO": (5 * 512, F16),
-    "W": (1024, F32), "X": (4096, BF), "D": (4096, BF), "AB": (4096, BF),
-    "OX": (256, U16), "OY": (256, U16), "OM": (256, U16), "OC": (5 * 32, U16),
-    "IA": (768, I32), "IB": (256, I32), "IC": (256, I32), "IT": (32, I32),
-    "M": (1024, BF), "F2": (512, F16), "E": (1024, BF), "SO": (1024, F16), "AC": (768, F32),
-    "FT": (1024, F16), "RFI": (512, F16), "EB": (5 * 512, F16),
-    "VP": (8, I32), "VR": (32, I32), "PC": (8, F32), "SC": (48, F32), "VJ": (16, F32), "JT": (16, F32), "TAB": (584, BF),
+    "HO": (5 * 272, F16), "HI": (4 * 256, F16), "THS": (16, F32), "GI": (5 * 768, F16), "OUT": (5 * 1536, F16),
+    "BK": (5 * 768, F16), "GL": (256, F32), "ZF": (256, F32), "W": (1024, F16), "WF": (1024, F32),
+    "X": (4096, BF), "D": (4096, BF), "AB": (4096, BF), "OX": (256, U16), "OY": (256, U16), "OM": (256, U16),
+    "IA": (512, I32), "IB": (256, I32), "IC": (512, I32), "M": (768, BF), "F2": (512, F16), "DD": (512, BF), "AC": (512, F32),
+    "PAR": (5 * 256, BF), "U": (512, F32),
+    "VP": (8, I32), "VR": (32, I32), "PC": (16, F32), "SC": (48, F32), "TAB": (440, BF),
     "C16": (128 * len(M16), F16), "CB": (128 * len(MBF), BF), "C32": (128, F32), "T": (5 * 128, BF), "TS": (5 * 128, BF),
-    "ORD": (144, BF), "BT": (8, F32), "Z1": (56, BF), "Z2": (144, F16),
-    "RS": (1024, BF), "ET": (512, BF), "ZO1": (512, BF), "RT": (512, BF), "CN": (128, F16),
+    "ORD": (144, BF), "BT": (8, F32), "Z1": (112, BF), "RS": (1024, BF), "ZO1": (384, BF), "CN": (128, F16),
 }
 SCRATCH = {k: ("sbuf", [128, n], d) for k, (n, d) in SB.items()}
 for _b in range(8):
     SCRATCH["P%d" % _b] = ("psum", [128, 512], F32)
-BIG = 8192.0
-REG = dict(S=(0, 0), pe=(0, 0), lx=(0, 0), gc=(0, 1), u=(0, 0),
-           c=(1, 0), D=(1, 1), ft=(1, 0), ut=(1, 0),
-           P2=(2, 0), lin=(2, 2), rc=(2, 3), PB=(2, 0), X2=(2, 2),
-           pd=(3, 0), zn=(3, 1), pz=(3, 0), mc=(2, 3), mg=(3, 0))
+BIG, HUGE = 8192.0, 2.0 ** 40
+REG = dict(c=(0, 0), D=(0, 0), u=(0, 2), lin=(0, 0), cu=(0, 0), ft=(0, 0), xa=(0, 0), par=(0, 0),
+           P2=(1, 0), mc=(1, 2), N=(1, 0), pd=(1, 0), pz=(1, 0), mg=(1, 0))
 
-PARAMS = dict(ns=2, modes=[[("a", 32, 32), ("d", 32), ("d", 32)]] * 3, sums=[(64, 0, 96)] * 3, sch=64,
-              cut=[[(0, 128)], [(64, 64), (0, 64)], [(64, 64), (0, 64)]],
-              x0=[("act", 32), ("dve", 32)] * 2, xs=[("dve", 32), ("act", 32)] * 2, ts=[("dve", 32), ("act", 32)] * 2,
-              t4=[("act", 32), ("dve", 32)] * 2, act=("BO", "RFI", "EB", "ZN", "ZO", "GO", "OX", "OM", "ZF"), cpx=True, cpy=False, one=False,
-              loads=(("zs", 0), ("hn", 0), ("gt", 0), ("qs", 0), ("xt", 0), ("hn", 1), ("gt", 1), ("zs", 1), ("qs", 1), ("xt", 1)),
-              seed=4, iters=60, lead=3500.0, sweeps=2, win=11000.0, tries=2000, amp=3000.0, temp=300.0, flip=0.3,
-              passes=2, span=150, moves=2000, idle=500, ten=8, reach=6)
+PARAMS = dict(lanes=(64, 64, 64, 64), modes=[[("a", 32), ("a", 32)]] * 3, xs=(32, 32), ts=(32, 32), sch=32, relu=False, pool=(),
+              dve=("GO",), lead=(0, 2500, 5000, 7500), seed=4, iters=100, flip=0.15, toll=0.5,
+              passes=12, span=200, moves=2000, idle=500, ten=8, reach=6)
 COST = dict(f=1.1, gc=1.56, pe=0.5, ov=60.0, hop=200.0, same=110.0, net=4000.0, iss=800.0, bw=200.0)
 
 
@@ -42,8 +35,8 @@ def A(name, a, n, step=1, ind=None):
     return (name, a, a + (n - 1) * step + 1, step, ind)
 
 
-def part(ap, a, n):
-    return A(ap[0], ap[1] + a * ap[3], n, ap[3])
+def part(ap, a, n, step=1):
+    return A(ap[0], ap[1] + a * ap[3], n, ap[3] * step)
 
 
 def is_ap(x):
@@ -59,14 +52,15 @@ def build(par):
     hist = {}
     bank = {}
     cur = [-1]
-    nst = par["ns"]
-    LN = 256 // nst
+    lanes = par["lanes"]
+    first_lane = [sum(lanes[:s]) for s in range(len(lanes))]
 
-    def add(eng, ins, reads, writes, sem=None, peer=0, nbytes=0):
+    def add(eng, ins, reads, writes, sem=None, peer=0, nbytes=0, free=False):
         i = len(ops)
         deps, order = set(), set()
         rd = [r for r in reads if is_ap(r)]
         rd += [r[4] for r in rd + writes if r[4]]
+        who = i if free else eng
         for lst, w in ((rd, False), (writes, True)):
             for ap in lst:
                 nm = ap[0]
@@ -74,8 +68,8 @@ def build(par):
                     if nm[0] != "P":
                         continue
                     st = bank.setdefault(nm, [None, [], []])
-                    if st[0] != eng:
-                        st[0], st[1], st[2] = eng, [], st[1]
+                    if st[0] != who:
+                        st[0], st[1], st[2] = who, [], st[1]
                     deps.update(st[2])
                     if eng == "pe":
                         order.update(st[1][-1:])
@@ -95,8 +89,7 @@ def build(par):
                 hist[nm] = keep
         deps.discard(i)
         order.discard(i)
-        ops.append(dict(eng=eng, ins=ins, deps=deps, order=order - deps, sem=sem, peer=peer, nbytes=nbytes, st=cur[0],
-                        free=ins[0][0] in ("gat", "cv") and all(x[0] in SB for x in rd + writes)))
+        ops.append(dict(eng=eng, ins=ins, deps=deps, order=order - deps, sem=sem, peer=peer, nbytes=nbytes, st=cur[0], free=free))
 
     def tt(o, a, b, op): add("dve", [("tt", o, a, b, op)], [a, b], [o])
     def ts(o, a, s1, op0, s2=None, op1=None): add("dve", [("ts", o, a, s1, s2, op0, op1)], [a, s1, s2], [o])
@@ -104,35 +97,53 @@ def build(par):
     def ms(o, c): add("dve", [("ms", o, c)], [], [o])
     def scan(o, a, b, op0, op1): add("dve", [("scan", o, a, b, op0, op1)], [a, b], [o])
     def act(o, a, fn, bias=0.0, scale=1.0): add("act", [("act", o, a, fn, bias, scale)], [a, bias, scale], [o])
-    def gat(o, a, eng): add(eng, [("gat", o, a)], [a], [o])
     def iota(o, pat, base, cm): add("pool", [("iota", o, pat, base, cm)], [], [o])
     def sel(o, a, pat, op, fill, base, cm): add("pool", [("sel", o, a, pat, op, fill, base, cm)], [a], [o])
-
-    def mm(terms, first=True, last=True):
-        ins = [("mm", o, l, r, first and j == 0, last and o[5:] not in [x[0][5:] for x in terms[j + 1:]]) for j, (o, l, r) in enumerate(terms)]
-        add("pe", ins, [x for t in terms for x in t[1:]], [t[0] for t in terms])
-
     def dma(o, a, sem, nbytes, eng="sp"): add(eng, [("dma", o, a)], [a], [o], sem=sem, nbytes=nbytes)
     def send(o, a, sem, peer): add("pool", [("send", o, a)], [a], [o], sem=sem, peer=peer)
 
-    def conv(o, a, tag, bias=0.0, scale=1.0, relu=False):
-        add("act" if tag in par["act"] else "dve", [("cv", o, a, bias, scale, relu)], [a], [o])
+    def mm(terms, first=False):
+        ins = [("mm", o, l, r, first and j == 0, False) for j, (o, l, r) in enumerate(terms)]
+        add("pe", ins, [x for t in terms for x in t[1:]], [t[0] for t in terms])
 
-    def index(tmp, a, b, lin):
-        tt(tmp, a, b, ALU.mult)
+    def either(tag, ins, reads, writes): add("dve" if tag in par["dve"] else "act", [ins], reads, writes, free=True)
+
+    def only(i, eng, *js):
+        ops[i]["link"] = js
+        for j in js:
+            ops[j]["only"] = (i, eng)
+
+    def conv(o, a, tag, bias=0.0, scale=1.0):
+        either(tag, ("cv", o, a, bias, scale), [a], [o])
+
+    def index(o, tmp, b, a, lin):
+        tt(tmp, b, a, ALU.mult)
         tt(tmp, tmp, lin, ALU.add)
         ts(tmp, tmp, 5, ALU.arith_shift_right, 4095, ALU.bitwise_and)
+        if o[0] in par["pool"]:
+            sel(o, tmp, [[0, width(o)]], ALU.is_ge, 0.0, 0, 0)
+        else:
+            conv(o, tmp, o[0])
 
-    for src, s in par["loads"]:
+    def drop(o, name, mask):
+        return [(o, C[name], mask), (o, C["n" + name], mask)]
+
+    def both(o): return [part(o, hf, width(o) // 2, 2) for hf in range(2)]
+
+    def load(src, s):
+        l0, n = (0, 0) if src == "xt" else (first_lane[s], lanes[s])
         if src == "qs":
             for b in range(2):
-                dma(A("QS", 2 * LN * (2 * s + b), 2 * LN), A("qs", 512 * b + 2 * LN * s, 2 * LN), "lq%d%d" % (s, b), 1024 * LN)
+                dma(A("QS", 4 * l0 + 2 * n * b, 2 * n), A("qs", 512 * b + 2 * l0, 2 * n), "lq%d%d" % (s, b), 1024 * n)
         elif src == "xt":
             dma(A("XT", 4096 * s, 4096), A("xt", 0, 4096), "lx%d" % s, 1 << 20)
-        elif s < 0:
-            dma(A(src.upper(), 0, 256), A(src, 0, 256), "l" + src, 512 * 256)
         else:
-            dma(A(src.upper(), LN * s, LN), A(src, LN * s, LN), "l%s%d" % (src, s), 512 * LN)
+            n = 256 - l0 if s else n
+            dma(A(src.upper(), l0, n), A(src, l0, n), "l%s%d" % (src, s), 512 * n)
+
+    for src, s in ([("zs", 0), ("hn", 0), ("gt", 0), ("qs", 0), ("xt", 0), ("zs", 1), ("hn", 1), ("gt", 1)]
+                   + [("qs", s) for s in range(1, len(lanes))] + [("xt", 1)]):
+        load(src, s)
     iota(A("VP", 0, 1), [[0, 1]], 0, 1)
     iota(A("VP", 1, 1), [[0, 1]], 0, 16)
     iota(A("VR", 0, 16), [[-1, 16]], 16, 1)
@@ -140,13 +151,12 @@ def build(par):
     COL, CG, CX = (A("TAB", 128 * j, 128) for j in range(3))
     iota(COL, [[1, 128]], 0, 0)
     iota(CG, [[16, 8], [0, 16]], 0, 0)
+    iota(A("ZO1", 0, 128), [[0, 128]], 0, 0)
+    ms(A("ZO1", 128, 128), 1.0)
     iota(CX, [[16, 128]], 0, 0)
-    iota(A("TAB", 384, 144), [[2, 72], [0, 2]], -14, 0)
-    iota(A("TAB", 528, 56), [[16, 56]], -384, 0)
-    iota(A("VJ", 0, 16), [[16, 16]], 0, 0)
+    iota(A("TAB", 384, 56), [[16, 56]], -384, 0)
     iota(A("ORD", 0, 144), [[0, 9], [1, 16]], 0, 0)
     dma(A("TH", 0, 1), A("th", 0, 1), "lth", 0, eng="pool")
-    iota(A("RS", 0, 1024), [[0, 64], [256, 16]], 0, 0)
     C = {k: A("C16", 128 * j, 128) for j, k in enumerate(M16)}
     C.update({k: A("CB", 128 * j, 128) for j, k in enumerate(MBF)})
     I32m = A("C32", 0, 128)
@@ -156,222 +166,216 @@ def build(par):
     cp(A("PC", 0, 5), A("VP", 2, 5))
     K, G16, K8, G8, E16 = (A("PC", j, 1) for j in range(5))
     ts(A("PC", 5, 1), K, 128.0, ALU.mult, G16, ALU.add)
+    ts(A("PC", 6, 1), A("PC", 5, 1), -1024.0, ALU.add)
+    ts(A("PC", 7, 1), K, 8.0, ALU.is_ge)
     ts(A("VR", 16, 16), A("VR", 16, 16), K8, ALU.add)
     ts(A("VR", 0, 32), A("VR", 0, 32), 15, ALU.bitwise_and)
     ts(A("SC", 0, 16), A("VR", 0, 16), G16, ALU.add)
     ts(A("SC", 16, 16), A("VR", 16, 16), E16, ALU.add)
     ts(A("SC", 32, 16), A("VR", 16, 16), 8.0, ALU.mult, G8, ALU.add)
     ts(A("BT", 0, 5), A("VR", 16, 5), -256.0, ALU.mult)
-    ts(A("JT", 0, 16), A("VJ", 0, 16), K, ALU.add)
 
     def where(o, tab, s, c):
         ts(o, tab, s, ALU.is_equal, c, ALU.mult)
 
+    where(C["B"], CG, G16, 1.0)
+    where(C["KO"], CG, A("PC", 5, 1), HUGE)
+    for k, c in (("cP", 2.0 ** 17), ("cN", -2.0 ** 17), ("c64", 64.0), ("c512", 512.0), ("cm16", -16.0), ("cm8", -8.0)):
+        ms(C[k], c)
     for k, j, c in (("P0", 0, 1.0), ("La", 0, 2080.0), ("Lb", 0, 3232.0), ("P5", 5, 1.0), ("P6", 6, 1.0), ("P10", 10, 1.0),
                     ("P15", 15, 1.0), ("P4", 4, 1.0), ("K16", 16, 2 * BIG), ("nK6", 22, -BIG), ("nK11", 27, -BIG),
-                    ("KN", 31, BIG), ("KL", 20, BIG), ("K5", 37, BIG), ("K10", 42, BIG)):
+                    ("KN", 31, HUGE), ("KL", 20, HUGE), ("K5", 37, BIG), ("K10", 42, BIG)):
         where(C[k], COL, A("SC", j, 1), c)
     where(C["nX"], CX, A("PC", 5, 1), -1.0)
-    where(C["B"], CG, G16, 1.0)
+    where(C["KE"], CG, A("PC", 6, 1), HUGE)
     where(C["Bb"], CG, E16, 1.0)
-    where(A("Z2", 0, 144), A("TAB", 384, 144), G16, 2.0 * LN)
-    where(A("Z1", 0, 56), A("TAB", 528, 56), G16, 1.0)
+    where(A("Z1", 0, 56), A("TAB", 384, 56), G16, 1.0)
+    where(A("Z1", 56, 56), A("TAB", 384, 56), G16, -1.0)
     PBK = A("P7", 0, 128)
     where(PBK, CG, E16, -BIG)
     tt(PBK, C["K16"], PBK, ALU.add)
     for t in range(NV):
         act(A("TS", 128 * t, 128), A("ORD", 16 - t, 128), ACT.Sigmoid, bias=A("BT", t, 1), scale=256.0)
         tt(A("T", 128 * t, 128), A("TS", 128 * t, 128), PBK, ALU.mult)
-    for k, a, c in (("nI", "P0", -1.0), ("nB", "B", -1.0), ("nK0", "K16", -0.5), ("X4", "K16", 0.25), ("nK16", "K16", -1.0), ("nB256", "Bb", -256.0),
-                    ("B2k", "B", 2048.0), ("Q0", "P0", 32.0), ("nKN", "KN", -1.0), ("nKL", "KL", -1.0)):
-        act(C[k], C[a], ACT.Identity, scale=c)
-    act(I32m, C["P0"], ACT.Copy)
-    iota(A("ZO1", 0, LN), [[0, LN]], 0, 0)
-    iota(A("ZO1", LN, 2 * LN), [[0, 2 * LN]], 1, 0)
-    iota(A("RT", 0, 4 * LN), [[0, LN], [8192, 2], [0, 2]], -2048, 0)
-    ms(A("CN", 0, LN), -1022.0)
-    ONE = A("ZO1", LN, LN)
-    for k, c in (("Ib", 1.0), ("nIb", -1.0), ("K4", 4096.0), ("K1", 1024.0), ("KX", -5120 * BIG)):
+    for k, a, c in (("nB", "B", -1.0), ("nKO", "KO", -1.0), ("nI", "P0", -1.0), ("nK0", "K16", -0.5), ("X4", "K16", 0.25),
+                    ("nK16", "K16", -1.0), ("B2k", "B", 2048.0), ("nKN", "KN", -1.0), ("nKL", "KL", -1.0), ("nKE", "KE", -1.0),
+                    ("nP15", "P15", -1.0), ("nP4", "P4", -1.0), ("Q15", "P15", 32.0), ("Q4", "P4", 32.0)):
+        conv(C[k], C[a], "const", 0.0, c)
+    conv(I32m, C["P0"], "const")
+    for k, a, b in (("Da", "P10", "P5"), ("Db", "P15", "P10"), ("Dc", "P4", "P15")):
+        tt(C[k], C[a], C[b], ALU.subtract)
+    ms(A("CN", 0, 128), -1086.0)
+    for k, c in (("Ib", 1.0), ("KB", HUGE), ("nKB", -HUGE), ("nIb", -1.0)):
         sel(C[k], A("ZO1", 0, 128), [[-1, 128]], ALU.not_equal, c, 0, 1)
     for k in ("K5", "K10"):
         sel(C[k], C[k], [[-1, 128]], ALU.not_equal, BIG, 0, 1)
     iota(A("XT", 8192, 16), [[0, 16]], 0, 0)
-    iota(A("ET", 0, 4 * LN), [[8192, 2], [0, 2 * LN]], -2048, 0)
+    iota(A("RS", 0, 16 * par["sch"]), [[0, par["sch"]], [256, 16]], 0, 0)
+    iota(A("U", 0, 512), [[0, 512]], 0, 0)
     XW, XZ = ("XT", 0, 4096, 1), ("XT", 0, 8208, 1)
 
-    for s in range(nst):
-        ts(A("HO", LN * s, LN), A("HN", LN * s, LN), -2048.0, ALU.add)
-        ts(A("GI", 3 * LN * s + LN, LN), A("GT", LN * s, LN), -2048.0, ALU.add)
-        ms(A("GI", 3 * LN * s, LN), 0.0)
-        act(A("GI", 3 * LN * s + 2 * LN, LN), A("ZS", LN * s, LN), ACT.Identity, bias=1024.0)
-        iota(A("E", 4 * LN * s, 4 * LN), [[0, 4 * LN]], 0, 0)
     ts(A("HO", 256, 1), A("TH", 0, 1), -2048.0, ALU.add)
+    for l0, n in zip(first_lane, lanes):
+        conv(A("HO", l0, n), A("HN", l0, n), "const", -2048.0)
+        conv(A("GI", 3 * l0, n), A("ZS", l0, n), "const", 1024.0)
+        conv(A("GI", 3 * l0 + n, n), A("GT", l0, n), "const", -2048.0)
+        conv(A("W", 4 * l0, 4 * n), A("QS", 4 * l0, 4 * n), "const", -2048.0)
 
-    def thresholds(a, n):
-        mm([(A("P3", 0, n), C["nX"], A("HO", 272 * a + 256, n, 272))])
-        ts(A("THS", a, n), A("P3", 0, n), -256.0, ALU.mult, 2048 * 256.0 - 128.0, ALU.add)
+    def thresholds(a, n, o):
+        mm([(o, C["nX"], A("HO", 272 * a + 256, n, 272))], True)
+        ts(A("THS", a, n), o, -256.0, ALU.mult, 2048 * 256.0 - 128.0, ALU.add)
+        ts(A("THS", 8 + a, n), o, -1.0, ALU.mult, 2048.0, ALU.add)
 
     def turn_names(d, o):
-        mm([(o, C["P15"], A("HO", 272 * (d - 1), 257))])
-        act(A("HO", 272 * d, 257), o, ACT.Copy)
+        mm([(o, C["P15"], A("HO", 272 * (d - 1), 257))], True)
+        conv(A("HO", 272 * d, 257), o, "turn")
         if d < NR:
             send(A("HI", 256 * d, 256), A("HO", 272 * d, 256), "h%d" % d, d)
         else:
-            thresholds(1, NV - 1)
+            thresholds(1, NV - 1, part(o, 0, NV - 1))
 
-    thresholds(0, 1)
+    thresholds(0, 1, A("P6", 0, 1))
 
     for t in range(NV):
-        for s in range(nst):
+        for s, (l0, LN) in enumerate(zip(first_lane, lanes)):
             cur[0] = s
-            l0 = s * LN
             c0 = 16 * l0
 
             def pr(name, off=0, n=LN, step=1):
                 bk, col = REG[name]
-                return A("P%d" % (8 // nst * s + bk), col * LN + off, n, step)
+                return A("P%d" % (2 * s + bk), col * LN + off, n, step)
 
+            def pieces(ws):
+                ws = [w * LN // sum(ws) for w in ws]
+                return [(sum(ws[:j]), w) for j, w in enumerate(ws)]
+
+            ONE = A("ZO1", 128, LN)
             H = A("HI", 256 * t + l0, LN) if t % NR else A("HO", 272 * t + l0, LN)
-            i0 = 768 * t + 3 * l0
-            CNT, G, Z = (A("GI", i0 + LN * j, LN) for j in range(3))
-            Ms = [A("M", 4 * l0 + LN * k, LN) for k in range(NS)]
-            ACs = [A("AC", 3 * l0 + LN * k, LN) for k in range(NS)]
-            way = {k: par[k][s] if isinstance(par[k], dict) else par[k] for k in ("modes", "x0", "xs", "ts", "t4")}
-            IAs = [A("IA", 3 * l0 + LN * k, LN) for k in range(NS)]
-            IB, IC = A("IB", l0, LN), A("IC", l0, LN)
-            Wn = ("QS" if t < 2 else "W", 4 * l0, 4 * l0 + 4 * LN, 1)
-            mm([(pr("lx"), C["La"], H), (pr("lx"), C["Lb"], G)])
-            if par["cpx"]:
-                mm([(pr("gc"), C["P0"], G)])
-            index(IB, H, pr("gc") if par["cpx"] else G, pr("lx"))
-            conv(A("OX", l0, LN), IB, "OX")
-            a = 0
-            for eng, n in way["x0" if t == 0 else "xs"]:
-                gat(A("X", c0 + 16 * a, 16 * n), XW + (A("OX", l0 + a, n),), eng)
-                a += n
-            nt = LN // 8
-            ut, IT, OC = pr("ut", 0, nt), A("IT", nt * s, nt), A("OC", 32 * t + nt * s, nt)
-            mm([(ut, A("Z2", 14 - 2 * a, 128), A("GI", Z[1] + a, nt, 8)) for a in range(8)])
-            tt(IT, ut, A("JT", 0, nt), ALU.add)
-            ts(IT, IT, 4 * LN - 1, ALU.bitwise_and)
-            conv(OC, IT, "OC")
-            RF, R, F = A("RFI", 2 * l0, 2 * LN), A("RFI", 2 * l0, LN, 2), A("RFI", 2 * l0 + 1, LN, 2)
-            conv(RF, Wn + (OC,), "RFI", -2048.0)
-            if t < NV - 1:
-                conv(A("EB", 512 * t + 2 * l0, 2 * LN), ("ET", 0, 4 * LN, 1, OC), "EB")
+            i0, o0 = 768 * t + 3 * l0, 1536 * t + 6 * l0
+            Z, G, CNT = (A("GI", i0 + LN * j, LN) for j in range(3))
+            ZO, GO, CO, USED = (A("OUT", o0 + LN * j, LN) for j in range(4))
+            RF = A("OUT", o0 + 4 * LN, 2 * LN)
+            R, F = both(RF)
+            Ms = [A("M", 3 * l0 + LN * k, LN) for k in range(NS)]
+            ACs = [A("AC", 2 * l0 + LN * k, LN) for k in range(NS - 1)]
+            IB, IC = A("IB", l0, LN), A("IC", 2 * l0, 2 * LN)
+            Q = [A("W", 4 * l0 + 2 * LN * b, 2 * LN) for b in range(2)]
+            PAR, U = A("PAR", 256 * t + l0, LN), A("U", 2 * l0, 2 * LN)
+            N, Dr = pr("N", 0, 2 * LN), pr("D", 0, 2 * LN)
+            mm([(pr("xa"), C["P0"], H), (pr("xa"), C["Lb"], ONE), (pr("xa", LN), C["La"], H)], True)
+            index(A("OX", l0, LN), IB, G, pr("xa"), pr("xa", LN))
+            for a, n in pieces(par["xs"]):
+                w = XW + (A("OX", l0 + a, n),)
+                either("x", ("gat", A("X", c0 + 16 * a, 16 * n), w), [w], [A("X", c0 + 16 * a, 16 * n)])
+            p = pr("par")
+            mm([(N, C["P0"], Q[0]), (N, C["nI"], Q[1])], True)
+            mm([(p, C["B"], Z), (p, C["cP"], ONE), (p, C["cN"], ONE), (p, C["nB"], Z)], True)
+            ts(PAR, p, 0.0, ALU.is_equal, A("PC", 7, 1), ALU.is_equal)
+            mm([x for o in both(N) for x in drop(o, "KO", PAR)] + [(N, C["P0"], Q[1])])
             for k in range(NS):
-                lin, IA = pr("lin"), IAs[k]
-                if par["cpy"]:
-                    mm([(pr("rc"), C["P0"], R)])
-                mm([(lin, C["La"], R), (lin, C["Lb"], F)])
-                for a, n in par["cut"][k]:
-                    index(part(IA, a, n), part(F, a, n), part(pr("rc") if par["cpy"] else R, a, n), part(lin, a, n))
-                    conv(A("OY", l0 + a, n), part(IA, a, n), "OY")
-                P2 = pr("P2", 0, 2 * LN)
-                c = pr("c")
-                mm([(c, C["nX"], CNT)] + [(c, C["K%d" % (5 * (k - j))], Ms[j]) for j in range(k)], last=False)
-                mc = pr("mc")
-                mm([(pr("P2"), C["P0"], H), (pr("P2", LN), C["P0"], R)], last=False)
-                mm([(mc, I32m, ACs[k - 1]), (mc, C["X4"], Ms[k - 1])] if k else [(mc, C["KN"], ONE)], first=False, last=False)
-                a, nd, sums = 0, 0, {}
-                for mode, *parts in way["modes"][k]:
-                    n = sum(parts)
-                    if mode == "d":
-                        act(A("D", c0 + 16 * a, 16 * n), XW + (A("OY", l0 + a, n),), ACT.Copy)
-                    for w in parts:
-                        x, d, ab = (A(nm, c0 + 16 * a, 16 * w) for nm in ("X", "D", "AB"))
-                        if mode == "d":
-                            pd = pr(("pd", "pe")[nd % 2], 0, 16 * w)
-                            nd += 1
-                            mm([(pd, C["nIb"], x)], last=False)
-                            mm([(pd, C["Ib"], d)], first=False)
-                            act(ab, pd, ACT.Abs)
-                            sums[a] = w
-                        else:
-                            tt(d, XW + (A("OY", l0 + a, w),), x, ALU.subtract)
-                        a += w
-                    if mode == "a":
-                        act(A("AB", c0 + 16 * (a - n), 16 * n), A("D", c0 + 16 * (a - n), 16 * n), ACT.Abs)
-                        sums[a - n] = n
-                for b, a in enumerate(par["sums"][k]):
-                    mm([(pr("c", a, sums[a]) + (32 * (j // 4),), A("Z1", 24 - 8 * (j % 4), 32), A("AB", c0 + 16 * a + j, sums[a], 16))
-                        for j in range(16)], first=False, last=b == len(sums) - 1)
+                lin, c, mc, P2, IA = pr("lin"), pr("c"), pr("mc"), pr("P2", 0, 2 * LN), A("IA", 2 * l0 + LN * (k % 2), LN)
+                conv(RF, N, "RF")
+                mm([(lin, C["La"], R), (lin, C["Lb"], F)], True)
+                index(A("OY", l0, LN), IA, F, both(N)[0], lin)
+                if t == s == 0 and k < 2:
+                    for d in (1, 2):
+                        turn_names(d + 2 * k, A("P1", 0, 257))
+                rot = C["P5" if k < NS - 1 else "P0"]
+                mm(([(c, C["nX"], CNT if t else A("ZO1", 0, LN))] if t or not k else [])
+                   + [(c, C["K%d" % (5 * (k - j))], Ms[j]) for j in range(k)], True)
+                ways = par["modes"][k]
+                for (mode, _), (a, n) in zip(ways, pieces([w for _, w in ways])):
+                    x, d, ab = (A(nm, c0 + 16 * a, 16 * n) for nm in ("X", "D", "AB"))
+                    y, pd = XW + (A("OY", l0 + a, n),), pr("pd", 0, 16 * n)
+                    if mode in "dD":
+                        add("act" if mode == "d" else "dve", [("gy", d, y, x)], [y, x], [d], free=True)
+                        i = len(ops) - 1
+                        mm([(pd, C["nIb"], x)], True)
+                        mm([(pd, C["Ib"], d)])
+                        only(i, "act", i + 1, i + 2)
+                        add("act", [("ab", ab, d, pd, i)], [d, pd], [ab])
+                    else:
+                        tt(d, y, x, ALU.subtract)
+                        add("act" if mode == "a" else "dve", [("nl", ab, d)], [d], [ab], free=par["relu"])
+                    for src, z in ([] if mode in "dD" else [(d, 56)]) + [(ab, 0)]:
+                        mm([(pr("c", a, n) + (32 * (j // 4),), A("Z1", z + 24 - 8 * (j % 4), 32), part(src, j, n, 16)) for j in range(16)])
+                    if mode in "ar":
+                        only(len(ops) - 3, "dve", len(ops) - 2)
+                mm([(pr("P2"), C["P0"], H), (pr("P2", LN), C["P0"], R)]
+                   + ([(mc, I32m, ACs[k - 1]), (mc, C["X4"], Ms[k - 1])] if k else [(mc, C["c64"], ONE)]), True)
                 M, Tt = Ms[k], A("T", 128 * t, 128)
-                act(M, c, ACT.Sigmoid, bias=A("THS", t, 1), scale=-256.0)
-                mm([(pr("P2", LN * hf), Tt, M) for hf in range(2)] + [(mc, C["nK16"], M)], first=False)
+                either("M", ("mt", M, c, A("THS", t, 1), A("THS", 8 + t, 1)), [c, A("THS", t, 1), A("THS", 8 + t, 1)], [M])
+                mm([(pr("P2", LN * hf), Tt, M) for hf in range(2)] + [(mc, C["nK16"], M)])
+                mm([(Dr, rot, RF)] + ([] if k else [(pr("u"), C["B"], Z)]), True)
                 fH, fR = A("F2", 2 * l0, LN), A("F2", 2 * l0 + LN, LN)
                 ts(A("F2", 2 * l0, 2 * LN), P2, -4096.0, ALU.add, -2048.0, ALU.max)
                 tt(ACs[k] if k < NS - 1 else A("OM", l0, LN), IA, mc, ALU.max)
-                if t == s == 0 and k < 2:
-                    for d in (1, 2):
-                        turn_names(d + 2 * k, pr("pd", 0, 257))
-                rot = C["P5" if k < NS - 1 else "P0"]
-                mm([(pr("D", 0, 2 * LN), rot, RF)], last=False)
-                mm([(pr("D", hf, LN, 2), C["nB"], fR) for hf in range(2)], first=False)
-                mm([(pr("S", 1, 2 * LN, 2), rot, RF)])
-                for hf in range(2):
-                    mm([(pr("S", 2 * hf, LN, 4), C["B"], fH), (pr("S", 2 * hf, LN, 4), C["nB"], fR)])
-                ts(A("E", 4 * l0 + 1, 2 * LN, 2), pr("D", 0, 2 * LN), 30720.0, ALU.is_equal)
-                scan(A("SO", 4 * l0, 4 * LN), A("E", 4 * l0, 4 * LN), pr("S", 0, 4 * LN), ALU.mult, ALU.add)
-                RF, R, F = A("SO", 4 * l0 + 1, 2 * LN, 2), A("SO", 4 * l0 + 1, LN, 4), A("SO", 4 * l0 + 3, LN, 4)
+                mm([(o, C["nB"], fR) for o in both(Dr)])
+                mm([(o, w, m) for w, m in ((C["B"], fH), (C["nB"], fR)) for o in both(N)], True)
+                DD = A("DD", 2 * l0, 2 * LN)
+                conv(DD, Dr, "DD", -30720.0)
+                if k == 0:
+                    conv(both(U)[1], pr("u"), "U", -16352.0)
+                if k == NS - 1:
+                    mm([(pr("cu"), C["Bb"], m) for m in Ms]
+                       + ([(pr("cu", LN), C[nk], m) for nk, m in zip(("nK0", "nK11", "nK6"), Ms)] if t else []), True)
+                mm(drop(N, "KB", DD) + [(N, rot, RF)])
+            conv(RF, N, "RF")
             more = t < NV - 1
-            g0 = 1024 * t + 4 * l0
-            zn, ZN, pz = pr("zn"), A("GO", g0, LN), pr("pz")
-            mm([(zn, C["P0"], Z)] + [(zn, C["nB256"], m) for m in Ms])
+            nz = 2 * LN if t else LN
+            conv(A("OUT", CO[1], nz), pr("cu", 0, nz), "CU")
+            if t > 0:
+                BK = A("BK", i0, 3 * LN)
+                send(BK, A("OUT", USED[1], 3 * LN), "b%d%d" % (t, s), NR - 1)
+            fs, fl = both(pr("ft", 0, 2 * LN))
+            kn, turn = ("KN", ("Q15", "nP15", "Db", "Da", "P5")) if more else ("KL", ("Q4", "nP4", "Dc", "Db", "P10"))
+            mm([(fl, C[turn[0]], G), (fl, C["c512"], ONE)] + [x for m in Ms for x in drop(fl, kn, m)]
+               + [(fl, C["B2k"], Z), (fl, C["B2k"], A("CN", 0, LN)), (fs, C["cm16"], ONE)], True)
+            mm([x for w, m in zip(turn[1:], Ms[::-1]) for x in [(fs, C[w], F)] + drop(fs, kn, m)] + [(fs, C[turn[4]], F)])
+            scan(IC, U, pr("ft", 0, 2 * LN), ALU.mult, ALU.add)
+            ts(IB, both(IC)[1], 5, ALU.arith_shift_right, 4095, ALU.bitwise_and)
             if more:
-                mm([(pr("zn", LN), C["K1"], ONE)] + [(pr("zn", LN), C["Bb"], m) for m in Ms])
-            nz = 2 * LN if more else LN
-            conv(A("GO", g0, nz), pr("zn", 0, nz), "ZN", -1024.0, relu=True)
-            a = 0
-            for eng, n in way["ts" if more else "t4"]:
-                gat(A("D", c0 + 16 * a, 16 * n), XZ + (A("OM", l0 + a, n),), eng)
-                a += n
+                conv(GO, IB, "GO", -2048.0)
+                send(A("GI", G[1] + 768, 2 * LN), A("OUT", GO[1], 2 * LN), "g%d%d" % (t, s), 1)
+            else:
+                conv(A("GL", l0, LN), IB, "GO")
+                dma(A("yg", l0, LN), A("GL", l0, LN), "sg%d" % s, 512 * LN)
+            for a, n in pieces(par["ts"]):
+                w = XZ + (A("OM", l0 + a, n),)
+                either("m", ("gat", A("D", c0 + 16 * a, 16 * n), w), [w], [A("D", c0 + 16 * a, 16 * n)])
             for a in range(0, LN, par["sch"]):
-                scan(*(A(nm, b + 16 * a, 16 * par["sch"]) for nm, b in (("AB", c0), ("RS", -16 * a), ("D", c0))), ALU.min, ALU.max)
-            mm([(pz, C["P0"], Z), (pz, C["P0"], ZN)], last=False)
-            mm([(pz, C["Ib"], A("AB", c0 + 15, LN, 16))], first=False)
-            ZO = A("GO", g0 + 3 * LN, LN)
+                n = 16 * min(par["sch"], LN - a)
+                scan(A("AB", c0 + 16 * a, n), A("RS", 0, n), A("D", c0 + 16 * a, n), ALU.min, ALU.max)
+            pz = pr("pz")
+            mm([(pz, C["P0"], Z), (pz, C["cm8"], ONE)] + drop(pz, "KB", CO) + [(pz, C["P0"], Z)], True)
+            mm([(pz, C["Ib"], A("AB", c0 + 15, LN, 16))])
             conv(ZO, pz, "ZO", 511.75, 0.5)
-            if more and not par["one"]:
+            if more:
                 send(A("GI", Z[1] + 768, LN), ZO, "z%d%d" % (t, s), 1)
-            if not more:
+            else:
                 conv(A("ZF", l0, LN), ZO, "ZF", -1024.0)
                 dma(A("yz", l0, LN), A("ZF", l0, LN), "sz%d" % s, 512 * LN)
             if t > 0:
-                o = pr("PB", 0, 2 * LN)
-                mm([(pr("PB", hf, LN, 2), C[nk], m) for nk, m in zip(("nK0", "nK11", "nK6"), Ms) for hf in range(2)], last=False)
-                mm([(o, C["P6"], RF)], first=False)
-                BO, BK = A("BO", 512 * t + 2 * l0, 2 * LN), A("BK", 512 * t + 2 * l0, 2 * LN)
-                conv(BO, pr("PB", 0, 2 * LN), "BO")
-                send(BK, BO, "b%d%d" % (t, s), NR - 1)
-            ft = [pr("ft", k, LN, 4) for k in range(4)]
-            turn, kp, kn = (("P5", "P10", "P15"), C["KN"], C["nKN"]) if more else (("P10", "P15", "P4"), C["KL"], C["nKL"])
-            mm([(ft[0], C[turn[2]], G)] + [(ft[0], kn, m) for m in Ms]
-               + [(o, w, m) for o, x in zip(ft[1:], Ms) for w, m in ((kp, x), (C["nK0"], ONE))], last=False)
-            mm([(o, C[r], F) for o, r in zip(ft[1:], turn)], first=False)
-            scan(A("FT", 4 * l0, 4 * LN), A("RT", 0, 4 * LN), pr("ft", 0, 4 * LN), ALU.min, ALU.max)
-            U, X2 = pr("u"), pr("X2")
-            mm([(U, C["B"], Z), (U, C["B"], A("CN", 0, LN))])
-            mm([(X2, C["B2k"], Z), (X2, C["KX"], ONE)], last=False)
-            mm([(X2, C["Q0"], A("FT", 4 * l0, LN, 4))], first=False)
-            index(IC, A("FT", 4 * l0 + 3, LN, 4), U, X2)
-            if more:
-                conv(A("GO", g0 + 2 * LN, LN), IC, "GO", -2048.0)
-                n = (2 + par["one"]) * LN
-                send(A("GI", i0 + 768, n), A("GO", g0 + LN, n), "g%d%d" % (t, s), 1)
-            else:
-                conv(A("GL", l0, LN), IC, "GO")
-                dma(A("yg", l0, LN), A("GL", l0, LN), "sg%d" % s, 512 * LN)
-            if t > 0:
-                EB, o0, o1 = A("EB", 512 * (t - 1) + 2 * l0, 2 * LN), pr("mg", 0, 2 * LN), pr("mg", 2 * LN, 2 * LN)
-                mm([(o1, C["K4"], A("ZO1", LN, 2 * LN)), (o0, C["P0"], EB), (o1, C["nI"], EB)], last=False)
-                mm([(o0, C["nI"], BK), (o1, C["nI"], BK)], first=False)
-                Wa = A("W", 4 * l0, 4 * LN)
-                tt(Wa, A(Wn[0], 4 * l0, 4 * LN), pr("mg", 0, 4 * LN), ALU.min)
-                act(Wa, Wa, ACT.Abs)
-                if not more:
+                before, mg = A("PAR", 256 * (t - 1) + l0, LN), [pr("mg", 2 * LN * b, 2 * LN) for b in range(2)]
+                mm([(o, C["nI"], q) for o, q in zip(mg, Q)], True)
+                for o, q, kp in zip(mg, Q, ("KO", "KE")):
+                    mm([(o, C["P6"], part(BK, LN, 2 * LN))]
+                       + [x for h in both(o) for x in drop(h, kp, before) + drop(h, "KB", part(BK, 0, LN))]
+                       + ([] if more else [(o, C["P0"], q)]))
+                if more:
+                    tt(A("W", 4 * l0, 4 * LN), A("W", 4 * l0, 4 * LN), pr("mg", 0, 4 * LN), ALU.add)
+                else:
+                    conv(A("WF", 4 * l0, 4 * LN), pr("mg", 0, 4 * LN), "W", 2048.0)
                     for b in range(2):
-                        dma(A("yq", 512 * b + 2 * l0, 2 * LN), A("W", 4 * l0 + 2 * LN * b, 2 * LN), "sq%d%d" % (s, b), 1024 * LN)
+                        dma(A("yq", 512 * b + 2 * l0, 2 * LN), A("WF", 4 * l0 + 2 * LN * b, 2 * LN), "sq%d%d" % (s, b), 1024 * LN)
+    closed = set()
+    for o in reversed(ops):
+        if o["eng"] == "pe":
+            for j in range(len(o["ins"]) - 1, -1, -1):
+                x = o["ins"][j]
+                rows = {(x[1][0], r) for r in x[1][5:] or (0, 32, 64, 96)}
+                o["ins"][j] = x[:5] + (not rows & closed,)
+                closed = closed - rows if x[4] else closed | rows
     return ops
 
 
@@ -427,12 +431,34 @@ def place(n, seq, pred, dur, engs):
     return st
 
 
+def topo_order(n, pred, key):
+    rank = sorted(range(n), key=lambda i: (key[i], i))
+    seq, done = [], [False] * n
+    for i in rank:
+        stack = [i]
+        while stack:
+            j = stack[-1]
+            if done[j]:
+                stack.pop()
+                continue
+            todo = [d for d, _ in pred[j] if not done[d]]
+            if todo:
+                stack.extend(sorted(todo, key=lambda d: -key[d]))
+            else:
+                done[j] = True
+                seq.append(j)
+                stack.pop()
+    return seq
+
+
 def schedule(ops, par, C):
     n = len(ops)
     engs = [o["eng"] for o in ops]
     dur, lat, cum = [0.0] * n, [0.0] * n, 0.0
     for i, o in enumerate(ops):
         dur[i], lat[i] = cost(o, engs[i], C)
+        if "only" in o and engs[o["only"][0]] != o["only"][1]:
+            dur[i] = 0.0
         if o["ins"][0][0] == "dma":
             cum = (cum if o["st"] < 0 else 0.0) + o["nbytes"] / C["bw"]
             lat[i] += cum if o["nbytes"] else 0.0
@@ -459,13 +485,16 @@ def schedule(ops, par, C):
     pr = [0.0] * (n + 1)
     for i in range(n - 1, -1, -1):
         pr[i] = dur[i] + max(pr[j] + lag for j, lag in succ[i])
-    key = [-pr[i] + (par["lead"] * max(ops[i]["st"], 0) if i < n else 0) for i in range(n + 1)]
+    key = [-pr[i] + (par["lead"][max(ops[i]["st"], 0)] if i < n else 0) for i in range(n + 1)]
 
     def forth(key):
-        return place(n + 1, topo_order(n + 1, pred, succ, key), pred, dur, engs)
+        return place(n + 1, topo_order(n + 1, pred, key), pred, dur, engs)
+
+    def back(st):
+        return place(n + 1, topo_order(n + 1, succ, [-(st[i] + dur[i]) for i in range(n + 1)]), succ, dur, engs)
 
     def again(st):
-        bk = place(n + 1, topo_order(n + 1, succ, pred, [-(st[i] + dur[i]) for i in range(n + 1)]), succ, dur, engs)
+        bk = back(st)
         return forth([-(bk[i] + dur[i]) for i in range(n + 1)])
 
     now = forth(key)
@@ -480,90 +509,56 @@ def schedule(ops, par, C):
             now = st
         if now[n] < best[n]:
             best = now
-    for _ in range(par["sweeps"]):
-        t0 = 0.0
-        while t0 < best[n]:
-            bk = place(n + 1, topo_order(n + 1, succ, pred, [-(best[i] + dur[i]) for i in range(n + 1)]), succ, dur, engs)
-            ids = [i for i in range(n) if t0 - 3000.0 <= best[i] < t0 + par["win"]]
-            pos = {i: j for j, i in enumerate(ids)}
-            m = len(ids)
-            fixed = [best[i] < t0 for i in ids]
-            rel = [max([best[d] + dur[d] + lag for d, lag in pred[i] if d not in pos] + [best[i] if fixed[j] else t0])
-                   for j, i in enumerate(ids)]
-            sp = [[(pos[d], lag) for d, lag in pred[i] if d in pos] + [(m, rel[j])] for j, i in enumerate(ids)] + [[]]
-            sd, se = [dur[i] for i in ids] + [0.0], [engs[i] for i in ids] + ["start"]
-            edge, half = t0 + par["win"] - 2500.0, t0 + par["win"] / 2
-            tail = np.array([max([lag + dur[i] + bk[j] + dur[j] for j, lag in succ[i] if j not in pos]
-                                 + [bk[i] + dur[i] if best[i] > edge else -1e9]) if best[i] > half else -1e9 for i in ids] + [-1e9])
-            fx = np.array(fixed + [True])
-
-            def value(st):
-                v = np.sort(np.array(st) + tail)
-                return float(v[-1] + 0.5 * np.mean(np.maximum(v[-12:], v[-1] - 5000.0)))
-
-            cur = np.array([best[i] for i in ids] + [-1e9])
-            cv = value(place(m + 1, topo_order(m + 1, sp, None, cur.tolist()), sp, sd, se))
-            bv, top, tope = cv, cur, list(se)
-            free = [j for j, i in enumerate(ids) if ops[i]["free"] and not fixed[j]]
-
-            def flip(j):
-                se[j] = "act" if se[j] == "dve" else "dve"
-                sd[j] = cost(ops[ids[j]], se[j], C)[0]
-                for a, b in [(d, j) for d, _ in sp[j][:-1]] + [(j, pos[k]) for k, _ in succ[ids[j]] if k in pos]:
-                    if not ops[ids[a]]["sem"]:
-                        sp[b] = [(d, C["same" if se[a] == se[b] else "hop"] if d == a else lag) for d, lag in sp[b]]
-
-            for it in range(par["tries"]):
-                at = t0 + rng.random() * par["win"]
-                flips = []
-                if free and rng.random() < par["flip"]:
-                    flips = [free[int(rng.random() * len(free))]]
-                    at = cur[flips[0]]
-                    other = [j for j in free if se[j] != se[flips[0]] and abs(cur[j] - at) < 6000.0]
-                    if other and rng.random() < 0.5:
-                        flips.append(other[int(rng.random() * len(other))])
-                for j in flips:
-                    flip(j)
-                near = (np.abs(cur - at) < 5000.0 * rng.random()) & ~fx
-                key = cur + near * rng.random(m + 1) * par["amp"] * rng.random() - fx * 1e6
-                st = place(m + 1, topo_order(m + 1, sp, None, key.tolist()), sp, sd, se)
-                v = value(st)
-                if v <= cv + par["temp"] * (1.0 - it / par["tries"]) * rng.random():
-                    cv, cur = v, np.array(st[:m] + [-1e9])
-                    if cv < bv:
-                        bv, top, tope = cv, cur, list(se)
-                else:
-                    for j in flips:
-                        flip(j)
-            key, was = list(best), (list(engs), list(dur))
-            for j, i in enumerate(ids):
-                key[i], engs[i] = float(top[j]), tope[j]
-                dur[i] = cost(ops[i], engs[i], C)[0]
-            edges()
-            st = forth(key)
-            st2 = again(st)
-            st = st2 if st2[n] < st[n] else st
-            if st[n] < best[n]:
-                best = st
-            else:
-                engs[:], dur[:] = was
-                edges()
-            t0 += par["win"] * (0.3 + 0.3 * rng.random())
-    best = polish(n + 1, [[(d, dur[d] + lag) for d, lag in p] for p in pred],
-                  [[(j, dur[i] + lag) for j, lag in p] for i, p in enumerate(succ)], dur, engs, best, par, rng)
+    best, seq = polish(ops, n + 1, pred, succ, dur, engs, best, par, C, rng)
     order = {e: [] for e in ("pe", "dve", "act", "pool", "sp")}
-    for i in sorted(range(n), key=lambda i: (best[i], i)):
-        order[engs[i]].append(i)
-    return order, engs[:n], best
+    for i in seq[:-1]:
+        if dur[i]:
+            order[engs[i]].append(i)
+    return order, engs[:n], best, seq[:-1]
 
 
-def polish(n, pred, succ, dur, engs, start, par, rng):
+def polish(ops, n, pred, succ, dur, engs, start, par, C, rng):
+    pred = [[[d, dur[d] + lag] for d, lag in p] for p in pred]
+    succ = [[[j, dur[i] + lag] for j, lag in p] for i, p in enumerate(succ)]
+    other = {"act": "dve", "dve": "act"}
+    alt = [cost(ops[i], other[engs[i]], C)[0] if i < n - 1 and ops[i]["free"] else 0.0 for i in range(n)]
+    for i in range(n - 1):
+        if "only" in ops[i]:
+            alt[i] = cost(ops[i], "pe", C)[0] - dur[i]
     order = sorted(range(n), key=lambda i: (start[i], i))
-    mp, ms, last = [-1] * n, [-1] * n, {}
-    for i in order:
-        if engs[i] in last:
-            mp[i], ms[last[engs[i]]] = last[engs[i]], i
-        last[engs[i]] = i
+    mp, ms = [-1] * n, [-1] * n
+
+    def queues():
+        last = {}
+        for i in order:
+            mp[i], ms[i] = last.get(engs[i], -1), -1
+            if mp[i] >= 0:
+                ms[mp[i]] = i
+            last[engs[i]] = i
+
+    def turn(d, e):
+        return (C["hop"] - C["same"]) * (1 if d == e else -1) if d in other else 0.0
+
+    def shift(a, b, x):
+        for e in succ[a]:
+            if e[0] == b:
+                e[1] += x
+        for e in pred[b]:
+            if e[0] == a:
+                e[1] += x
+
+    def flip(u):
+        for d, _ in pred[u]:
+            shift(d, u, turn(engs[d], engs[u]))
+        for j, _ in succ[u]:
+            shift(u, j, turn(engs[j], engs[u]) + alt[u] - dur[u])
+        engs[u] = other[engs[u]]
+        dur[u], alt[u] = alt[u], dur[u]
+        for v in ops[u].get("link", ()):
+            for j, _ in succ[v]:
+                shift(v, j, alt[v] - dur[v])
+            dur[v], alt[v] = alt[v], dur[v]
+
     head, tail, jh, jt, pos = [0.0] * n, [0.0] * n, [0.0] * n, [0.0] * n, [0] * n
 
     def heads(seq):
@@ -630,12 +625,26 @@ def polish(n, pred, succ, dur, engs, start, par, rng):
         for k, i in enumerate(win):
             pos[i] = k
         mk = best = max(head[i] + tail[i] for i in win)
-        keep = (list(win), [mp[i] for i in win], [ms[i] for i in win])
+        keep = (list(win), [engs[i] for i in win])
         tabu, idle, reach = {}, 0, par["reach"]
         for it in range(par["moves"]):
             lim = mk - 0.01
-            runs, seen = [], set()
+            runs, seen, top = [], set(), None
             for i in win:
+                if alt[i] and head[i] + tail[i] > lim and engs[i] in other and tabu.get(i, -1) <= it and rng.random() < par["flip"]:
+                    e2, k = other[engs[i]], pos[i] - 1
+                    while k >= 0 and engs[win[k]] != e2:
+                        k -= 1
+                    if k >= 0:
+                        p = win[k]
+                        q = ms[p]
+                        e = max([head[d] + w + turn(engs[d], engs[i]) for d, w in pred[i]] + [head[p] + dur[p]]) + alt[i] + max(
+                            [tail[j] + w - dur[i] + turn(engs[j], engs[i]) for j, w in succ[i]] + [tail[q] if q >= 0 else 0.0])
+                        for v in ops[i].get("link", ()):
+                            e = max(e, head[v] + tail[v] + alt[v] - dur[v])
+                        e += par["toll"] * (alt[i] if e2 == "dve" else -dur[i])
+                        if top is None or e < top[0]:
+                            top = (e, 2, i, p, q)
                 if head[i] + tail[i] > lim and i not in seen:
                     run, j = [i], ms[i]
                     while j in inside and head[j] + tail[j] > lim and head[j] < head[run[-1]] + dur[run[-1]] + 0.01:
@@ -644,7 +653,6 @@ def polish(n, pred, succ, dur, engs, start, par, rng):
                         j = ms[j]
                     if len(run) > 1:
                         runs.append(run)
-            top = None
             for run in runs:
                 k = len(run)
                 for x, y in sorted({(0, j) for j in range(1, min(k, reach))} | {(j, k - 1) for j in range(max(0, k - reach), k - 1)}):
@@ -668,11 +676,23 @@ def polish(n, pred, succ, dur, engs, start, par, rng):
             if top is None:
                 break
             _, late, u, v, seq = top
-            link(seq, mp[u], ms[v])
             ten = it + par["ten"] + int(rng.random() * par["ten"])
-            lo, hi = pos[u], pos[v] + 1
+            if late == 2:
+                if mp[u] >= 0:
+                    ms[mp[u]] = ms[u]
+                if ms[u] >= 0:
+                    mp[ms[u]] = mp[u]
+                link([u], v, seq)
+                flip(u)
+                tabu[u] = ten + par["ten"]
+                lo, hi = 0, len(win)
+            else:
+                link(seq, mp[u], ms[v])
+                lo, hi = pos[u], pos[v] + 1
             seg = win[lo:hi]
-            if late:
+            if late == 2:
+                pass
+            elif late:
                 tabu.update({(u, w): ten for w in seq[:-1]})
                 mark = {u}
                 for i in seg:
@@ -695,13 +715,16 @@ def polish(n, pred, succ, dur, engs, start, par, rng):
             idle += 1
             if mk < best - 0.01:
                 best, idle = mk, 0
-                keep = (list(win), [mp[i] for i in win], [ms[i] for i in win])
+                keep = (list(win), [engs[i] for i in win])
             if idle > par["idle"]:
                 break
         order[a:b] = keep[0]
-        for i, p, q in zip(*keep):
-            link([i], p, q)
+        for i, e in zip(*keep):
+            if engs[i] != e:
+                flip(i)
+        queues()
 
+    queues()
     for _ in range(par["passes"]):
         a = 0
         while a < n - 20:
@@ -711,31 +734,12 @@ def polish(n, pred, succ, dur, engs, start, par, rng):
             window(a, min(n, a + par["span"]))
             a += int(par["span"] * (0.3 + 0.4 * rng.random()))
     heads(order)
-    return head
-
-
-def topo_order(n, pred, succ, key):
-    rank = sorted(range(n), key=lambda i: (key[i], i))
-    seq, done = [], [False] * n
-    for i in rank:
-        stack = [i]
-        while stack:
-            j = stack[-1]
-            if done[j]:
-                stack.pop()
-                continue
-            todo = [d for d, _ in pred[j] if not done[d]]
-            if todo:
-                stack.extend(sorted(todo, key=lambda d: -key[d]))
-            else:
-                done[j] = True
-                seq.append(j)
-                stack.pop()
-    return seq
+    order.sort(key=lambda i: head[i])
+    return head, order
 
 
 OPS = build(PARAMS)
-ORDER, ENGS, _T = schedule(OPS, PARAMS, COST)
+ORDER, ENGS, _T, SEQ = schedule(OPS, PARAMS, COST)
 SEMAPHORES = ["pe", "dve", "act", "pool", "sent"] + [o["sem"] for o in OPS if o["sem"]]
 
 
@@ -755,9 +759,10 @@ def rank_program(g, core, T, topo):
     def engines(o, src_rank):
         return len(topo.engines(T.cores[src_rank % NR], T.cores[(src_rank + o["peer"]) % NR]))
 
-    needed = set()
-    for i, o in enumerate(OPS):
-        needed.update(d for d in o["deps"] if not (ENGS[d] == "pe" and ENGS[i] == "pe"))
+    live = {i for l in ORDER.values() for i in l}
+    deps = {i: [d for d in OPS[i]["deps"] if d in live and not (ENGS[d] == "pe" and ENGS[i] == "pe")] for i in live}
+    needed = {d for l in deps.values() for d in l}
+    place_of = {i: k for k, i in enumerate(SEQ)}
     mark, total = {}, {}
     for e, l in ORDER.items():
         for i in l:
@@ -770,11 +775,11 @@ def rank_program(g, core, T, topo):
                 total[e] = total.get(e, 0) + 1
                 mark[i] = (e, total[e])
     seen, knew, waits = {e: {} for e in ORDER}, {}, {}
-    for i in sorted(range(len(OPS)), key=lambda i: (_T[i], i)):
+    for i in sorted(live, key=place_of.get):
         e = ENGS[i]
         waits[i] = []
-        for d in sorted(OPS[i]["deps"], key=lambda d: (-_T[d], -d)):
-            if not (e == "pe" and ENGS[d] == "pe") and seen[e].get(mark[d][0], 0) < mark[d][1]:
+        for d in sorted(deps[i], key=lambda d: -place_of[d]):
+            if seen[e].get(mark[d][0], 0) < mark[d][1]:
                 waits[i].append(mark[d])
                 for sm, n in knew[d].items():
                     seen[e][sm] = max(seen[e].get(sm, 0), n)
@@ -798,10 +803,22 @@ def rank_program(g, core, T, topo):
                     r = g.vector.tensor_copy(*x)
                 elif k == "gat":
                     r = g.scalar.activation(x[0], x[1], ACT.Copy)
+                elif k == "gy" and e == "act":
+                    r = g.scalar.activation(x[0], x[1], ACT.Copy)
+                elif k == "gy":
+                    r = g.vector.tensor_tensor(x[0], x[1], x[2], ALU.subtract)
+                elif k == "ab":
+                    r = g.scalar.activation(x[0], x[2 if ENGS[x[3]] == "act" else 1], ACT.Abs)
+                elif k == "nl" and e == "act":
+                    r = g.scalar.activation(x[0], x[1], ACT.Abs)
+                elif k == "nl":
+                    r = g.vector.tensor_scalar(x[0], x[1], 0.0, 2.0, ALU.max, ALU.mult)
+                elif k == "mt" and e == "act":
+                    r = g.scalar.activation(x[0], x[1], ACT.Sigmoid, bias=x[2], scale=-256.0)
+                elif k == "mt":
+                    r = g.vector.tensor_scalar(x[0], x[1], x[3], None, ALU.is_lt)
                 elif k == "cv" and e == "act":
-                    r = g.scalar.activation(x[0], x[1], ACT.Relu if x[4] else ACT.Identity, bias=x[2], scale=x[3])
-                elif k == "cv" and x[4]:
-                    r = g.vector.tensor_scalar(x[0], x[1], x[2], 0.0, ALU.add, ALU.max)
+                    r = g.scalar.activation(x[0], x[1], ACT.Identity, bias=x[2], scale=x[3])
                 elif k == "cv" and x[2:4] == [0.0, 1.0]:
                     r = g.vector.tensor_copy(x[0], x[1])
                 elif k == "cv":

@@ -1,34 +1,39 @@
 import numpy as np
+from concourse.bass import DstId, RemoteDMATransfer
 from concourse.mybir import AluOpType as ALU, ActivationFunctionType as ACT
 
 NR, NV, NS = 4, 5, 3
 F32, BF, I32, U16, F16 = "float32", "bfloat16", "int32", "uint16", "float16"
-M16 = ("P0", "P5", "P6", "P10", "P15", "P4", "La", "Lb", "nI", "nX", "B", "nB", "B2k",
-       "Da", "Db", "Dc", "nP15", "nP4", "Q15", "Q4")
-MBF = ("KN", "KL", "nKN", "nKL", "K5", "K10", "nK0", "nK6", "nK11", "X4", "K16", "nK16", "Ib", "nIb", "Bb",
-       "KB", "nKB", "KO", "nKO", "KE", "nKE", "c64", "cP", "cN", "c512", "cm16", "cm8")
+PAD, SLOT, HALF = 64, 4160, 1600
+M16 = ("nB", "nP1", "nP13", "nP0", "B", "P1", "P13", "P0", "P11", "P6", "D1", "D2", "P5", "P2", "La0", "Lb", "B2k", "nX", "nBx", "nOf",
+       "nBl", "nLa1", "nLa0", "Bl", "La1", "La5")
+MBF = ("KO", "KS", "KR", "nKO", "nKS", "nKR", "KN", "nKN", "KB", "nKB", "X11", "X6", "K5", "K10", "T", "Ib", "Q0", "Odd", "Even",
+       "Xa", "Xb", "Xc", "Xd", "cP", "cN", "ch", "c512", "cm16", "cm64")
 SB = {
-    "XT": (8208, BF), "HN": (256, I32), "GT": (256, I32), "ZS": (256, I32), "QS": (1024, I32), "TH": (4, I32),
-    "HO": (5 * 272, F16), "HI": (4 * 256, F16), "THS": (16, F32), "GI": (5 * 768, F16), "OUT": (5 * 1536, F16),
-    "BK": (5 * 768, F16), "GL": (256, F32), "ZF": (256, F32), "W": (1024, F16), "WF": (1024, F32),
+    "XT": (NR * SLOT, BF), "HB": (SLOT, BF), "HN": (256, I32), "GT": (256, I32), "ZS": (256, I32), "QS": (1024, I32), "TH": (4, I32),
+    "HO": (272, F16), "HT": (512, F32), "THS": (16, F32), "ZZ": (6 * 256, F16), "E": (1536, F16), "OUT": (5 * 1280, F16),
+    "BK": (4 * 1024, F16), "WU": (5 * 1024, F16), "WB": (3 * 1024, F16), "GL": (256, F32), "ZF": (256, F32), "WF": (1024, F32),
     "X": (4096, BF), "D": (4096, BF), "AB": (4096, BF), "OX": (256, U16), "OY": (256, U16), "OM": (256, U16),
-    "IA": (512, I32), "IB": (256, I32), "IC": (512, I32), "M": (768, BF), "F2": (512, F16), "DD": (512, BF), "AC": (512, F32),
-    "PAR": (5 * 256, BF), "U": (512, F32),
-    "VP": (8, I32), "VR": (32, I32), "PC": (16, F32), "SC": (48, F32), "TAB": (440, BF),
-    "C16": (128 * len(M16), F16), "CB": (128 * len(MBF), BF), "C32": (128, F32), "T": (5 * 128, BF), "TS": (5 * 128, BF),
-    "ORD": (144, BF), "BT": (8, F32), "Z1": (112, BF), "RS": (1024, BF), "ZO1": (384, BF), "CN": (128, F16),
+    "IX": (512, I32), "IY": (512, I32), "IC": (512, I32), "IB": (256, I32), "IG": (256, I32), "IA": (1024, I32), "AC": (1024, I32),
+    "M": (768, BF), "F2": (512, F16), "DD": (512, BF), "PAR": (5 * 256, BF), "U": (512, F32),
+    "VP": (8, I32), "VR": (32, I32), "PC": (16, F32), "SC": (48, F32), "TAB": (568, BF),
+    "C16": (128 * len(M16), F16), "CB": (128 * len(MBF), BF), "Z1": (112, BF), "RS": (1024, BF), "ZO1": (384, BF),
+    "HI": (8, BF),
 }
 SCRATCH = {k: ("sbuf", [128, n], d) for k, (n, d) in SB.items()}
 for _b in range(8):
     SCRATCH["P%d" % _b] = ("psum", [128, 512], F32)
-BIG, HUGE = 8192.0, 2.0 ** 40
-REG = dict(c=(0, 0), D=(0, 0), u=(0, 2), lin=(0, 0), cu=(0, 0), ft=(0, 0), xa=(0, 0), par=(0, 0),
-           P2=(1, 0), mc=(1, 2), N=(1, 0), pd=(1, 0), pz=(1, 0), mg=(1, 0))
+BIG, HUGE = 8192.0, 2.0 ** 50
+REG = dict(c=(0, 0), D=(0, 0), u=(0, 2), mc=(0, 2), ft=(0, 0), pz=(0, 0), par=(0, 0), P2=(1, 0), N=(1, 0), mg=(1, 0))
 
-PARAMS = dict(lanes=(64, 64, 64, 64), modes=[[("a", 32), ("a", 32)]] * 3, xs=(32, 32), ts=(32, 32), sch=32, relu=False, pool=(),
-              dve=("GO",), lead=(0, 2500, 5000, 7500), seed=4, iters=100, flip=0.15, toll=0.5,
-              passes=12, span=200, moves=2000, idle=500, ten=8, reach=6)
-COST = dict(f=1.1, gc=1.56, pe=0.5, ov=60.0, hop=200.0, same=110.0, net=4000.0, iss=800.0, bw=200.0)
+PARAMS = dict(lanes=(64, 64, 64, 64), ys=(32, 32), xs=(32, 32), ts=(32, 32), sch=64, rdve=((0, 32),), pool=(1, 0, ()), plin=(), soon=(0,), dve=("GO", "wide"),
+              early=2, eq=1, late=2,
+              lead=((2000, 2500, 0.15), (2500, 2000, 0.12), (2200, 2200, 0.15), (2800, 1800, 0.12)),
+              seed=4, iters=4, heats=2, trial=2, rounds=36, suits=7, both=2, mid=1, slack=1.002,
+              flip=0.15, toll=0.6, span=130, moves=500, idle=170, ten=8, reach=6)
+COST = dict(f=1.1, gc=1.56, pe=0.49, ov=60.0, hop=200.0, same=110.0, net=4000.0, iss=800.0, bw=260.0, link=70.0, once=2200.0, dge=200.0)
+SPREAD = dict(gc=(1.04, 2.08, 1), f=(1.0, 1.4, 3), hop=(120.0, 260.0, 2), same=(60.0, 130.0, 2), pe=(0.42, 0.56, 5), ov=(45.0, 75.0, 4),
+              iss=(500.0, 1300.0, 6), net=(2500.0, 5000.0, 4), bw=(160.0, 360.0, 5), link=(35.0, 100.0, 3))
 
 
 def A(name, a, n, step=1, ind=None):
@@ -47,6 +52,10 @@ def width(ap):
     return 16 * (ap[4][2] - ap[4][1]) if ap[4] else (ap[2] - ap[1] - 1) // ap[3] + 1
 
 
+def size(ap):
+    return 2 if ap[0] in SB and SB[ap[0]][1] in (BF, U16, F16) else 4
+
+
 def build(par):
     ops = []
     hist = {}
@@ -55,9 +64,9 @@ def build(par):
     lanes = par["lanes"]
     first_lane = [sum(lanes[:s]) for s in range(len(lanes))]
 
-    def add(eng, ins, reads, writes, sem=None, peer=0, nbytes=0, free=False):
+    def add(eng, ins, reads, writes, sem=None, far=None, nbytes=0, free=False, after=()):
         i = len(ops)
-        deps, order = set(), set()
+        deps, order = set(), set(after)
         rd = [r for r in reads if is_ap(r)]
         rd += [r[4] for r in rd + writes if r[4]]
         who = i if free else eng
@@ -83,160 +92,182 @@ def build(par):
                     hit = e[1] < ap[2] and ap[1] < e[2]
                     if hit and (w or e[3]):
                         deps.add(e[0])
-                    if not (w and ap[3] == 1 and ap[1] <= e[1] and e[2] <= ap[2]):
+                    if not (w and ap[1] <= e[1] and e[2] <= ap[2]):
                         keep.append(e)
                 keep.append((i, ap[1], ap[2], w))
                 hist[nm] = keep
         deps.discard(i)
         order.discard(i)
-        ops.append(dict(eng=eng, ins=ins, deps=deps, order=order - deps, sem=sem, peer=peer, nbytes=nbytes, st=cur[0], free=free))
+        ops.append(dict(eng=eng, ins=ins, deps=deps, order=order - deps, sem=sem, far=far, nbytes=nbytes, st=cur[0], free=free))
+        return i
 
     def tt(o, a, b, op): add("dve", [("tt", o, a, b, op)], [a, b], [o])
     def ts(o, a, s1, op0, s2=None, op1=None): add("dve", [("ts", o, a, s1, s2, op0, op1)], [a, s1, s2], [o])
     def cp(o, a): add("dve", [("cp", o, a)], [a], [o])
     def ms(o, c): add("dve", [("ms", o, c)], [], [o])
     def scan(o, a, b, op0, op1): add("dve", [("scan", o, a, b, op0, op1)], [a, b], [o])
-    def act(o, a, fn, bias=0.0, scale=1.0): add("act", [("act", o, a, fn, bias, scale)], [a, bias, scale], [o])
-    def iota(o, pat, base, cm): add("pool", [("iota", o, pat, base, cm)], [], [o])
+    def iota(o, pat, base, cm): return add("pool", [("iota", o, pat, base, cm)], [], [o])
     def sel(o, a, pat, op, fill, base, cm): add("pool", [("sel", o, a, pat, op, fill, base, cm)], [a], [o])
-    def dma(o, a, sem, nbytes, eng="sp"): add(eng, [("dma", o, a)], [a], [o], sem=sem, nbytes=nbytes)
-    def send(o, a, sem, peer): add("pool", [("send", o, a)], [a], [o], sem=sem, peer=peer)
+    def dma(o, a, sem, nbytes, eng="sp", after=()): add(eng, [("dma", o, a)], [a], [o], sem=sem, nbytes=nbytes, after=after)
+
+    def send(moves, by="pool", after=()):
+        ins = [("send",) + m for m in moves]
+        i = add(by, ins, [m[1] for m in moves], [moves[0][0]], sem=moves[0][2], far=(moves[0][3], len(moves), by), after=after)
+        for m in moves[1:]:
+            j = add("nil", [("land", m[0])], [], [m[0]], sem=m[2], far=(m[3], len(moves), by))
+            ops[j]["deps"].add(i)
+        return i
 
     def mm(terms, first=False):
         ins = [("mm", o, l, r, first and j == 0, False) for j, (o, l, r) in enumerate(terms)]
-        add("pe", ins, [x for t in terms for x in t[1:]], [t[0] for t in terms])
+        return add("pe", ins, [x for t in terms for x in t[1:]], [t[0] for t in terms])
 
-    def either(tag, ins, reads, writes): add("dve" if tag in par["dve"] else "act", [ins], reads, writes, free=True)
-
-    def only(i, eng, *js):
-        ops[i]["link"] = js
-        for j in js:
-            ops[j]["only"] = (i, eng)
+    def either(tag, ins, reads, writes): return add("dve" if tag in par["dve"] else "act", [ins], reads, writes, free=True)
 
     def conv(o, a, tag, bias=0.0, scale=1.0):
-        either(tag, ("cv", o, a, bias, scale), [a], [o])
+        either(tag, ("cv", o, a, bias, scale), [a, bias], [o])
 
-    def index(o, tmp, b, a, lin):
-        tt(tmp, b, a, ALU.mult)
-        tt(tmp, tmp, lin, ALU.add)
-        ts(tmp, tmp, 5, ALU.arith_shift_right, 4095, ALU.bitwise_and)
-        if o[0] in par["pool"]:
-            sel(o, tmp, [[0, width(o)]], ALU.is_ge, 0.0, 0, 0)
+    def cast(o, a, pool):
+        if pool:
+            sel(o, a, [[0, width(o)]], ALU.is_ge, 0.0, 0, 0)
         else:
-            conv(o, tmp, o[0])
+            conv(o, a, o[0])
+
+    def index(o, whole, pairs, zb, al, pool):
+        scan(pairs, zb, al, ALU.mult, ALU.add)
+        ts(whole, both(pairs)[1], 5, ALU.arith_shift_right, 4095, ALU.bitwise_and)
+        cast(o, whole, pool)
 
     def drop(o, name, mask):
         return [(o, C[name], mask), (o, C["n" + name], mask)]
 
     def both(o): return [part(o, hf, width(o) // 2, 2) for hf in range(2)]
+    def halves(o): return [part(o, hf * width(o) // 2, width(o) // 2) for hf in range(2)]
 
     def load(src, s):
         l0, n = (0, 0) if src == "xt" else (first_lane[s], lanes[s])
         if src == "qs":
             for b in range(2):
-                dma(A("QS", 4 * l0 + 2 * n * b, 2 * n), A("qs", 512 * b + 2 * l0, 2 * n), "lq%d%d" % (s, b), 1024 * n)
+                dma(A("QS", 4 * l0 + 2 * n * b, 2 * n), A("qs", 512 * b + 2 * l0, 2 * n), "lq%d%d" % (s, b), 1024 * n,
+                    "act" if s < par["eq"] else "sp")
         elif src == "xt":
-            dma(A("XT", 4096 * s, 4096), A("xt", 0, 4096), "lx%d" % s, 1 << 20)
+            a, n = (0, HALF - PAD) if s else (HALF - PAD, SLOT - HALF)
+            dma(A("XT", PAD + a, n), A("xt", a, n), "lx%d" % s, 256 * n)
         else:
-            n = 256 - l0 if s else n
+            l0, n = cuts[s]
             dma(A(src.upper(), l0, n), A(src, l0, n), "l%s%d" % (src, s), 512 * n)
 
-    for src, s in ([("zs", 0), ("hn", 0), ("gt", 0), ("qs", 0), ("xt", 0), ("zs", 1), ("hn", 1), ("gt", 1)]
-                   + [("qs", s) for s in range(1, len(lanes))] + [("xt", 1)]):
+    early = par["early"]
+    cuts = [(0, sum(lanes[:early])), (sum(lanes[:early]), sum(lanes[early:]))][:1 + (early < len(lanes))]
+    for src, s in ([("zs", 0), ("hn", 0), ("gt", 0)] + [("qs", s) for s in range(par["eq"])] + [("xt", 0), ("xt", 1)]
+                   + [(src, 1) for src in ("zs", "hn", "gt") if len(cuts) > 1] + [("qs", s) for s in range(par["eq"], len(lanes))]):
         load(src, s)
-    iota(A("VP", 0, 1), [[0, 1]], 0, 1)
-    iota(A("VP", 1, 1), [[0, 1]], 0, 16)
-    iota(A("VR", 0, 16), [[-1, 16]], 16, 1)
-    iota(A("VR", 16, 16), [[-1, 16]], 16, 0)
-    COL, CG, CX = (A("TAB", 128 * j, 128) for j in range(3))
-    iota(COL, [[1, 128]], 0, 0)
-    iota(CG, [[16, 8], [0, 16]], 0, 0)
-    iota(A("ZO1", 0, 128), [[0, 128]], 0, 0)
-    ms(A("ZO1", 128, 128), 1.0)
+    COL, CG, CX, C8 = (A("TAB", 128 * j, 128) for j in range(4))
+    ZERO = A("ZO1", 0, 128)
+    soon = [iota(A("VP", 0, 1), [[0, 1]], 0, 1), iota(A("VP", 1, 1), [[0, 1]], 0, 16), iota(A("VR", 0, 16), [[-1, 16]], 16, 1),
+            iota(A("VR", 16, 16), [[-1, 16]], 16, 0), iota(CG, [[16, 8], [0, 16]], 0, 0), iota(COL, [[1, 128]], 0, 0)]
+    dma(A("TH", 0, 1), A("th", 0, 1), "lth", 0, "pool", soon)
+    iota(ZERO, [[0, 128]], 0, 0)
+    ms(A("ZO1", 128, 256), 1.0)
     iota(CX, [[16, 128]], 0, 0)
-    iota(A("TAB", 384, 56), [[16, 56]], -384, 0)
-    iota(A("ORD", 0, 144), [[0, 9], [1, 16]], 0, 0)
-    dma(A("TH", 0, 1), A("th", 0, 1), "lth", 0, eng="pool")
+    iota(C8, [[0, 16], [1, 8]], 0, 0)
+    iota(A("TAB", 512, 56), [[16, 56]], -384, 0)
     C = {k: A("C16", 128 * j, 128) for j, k in enumerate(M16)}
     C.update({k: A("CB", 128 * j, 128) for j, k in enumerate(MBF)})
-    I32m = A("C32", 0, 128)
-    for j, (src, n, op) in enumerate(((0, 15, ALU.bitwise_and), (0, 112, ALU.bitwise_and), (0, 3, ALU.arith_shift_right),
-                                      (0, 7, ALU.bitwise_and), (1, 112, ALU.bitwise_and))):
-        ts(A("VP", 2 + j, 1), A("VP", src, 1), n, op)
+    for j, n, src, c, op in ((2, 1, 0, 15, ALU.bitwise_and), (3, 2, 0, 112, ALU.bitwise_and), (5, 1, 0, 3, ALU.arith_shift_right),
+                             (6, 1, 0, 7, ALU.bitwise_and)):
+        ts(A("VP", j, n), A("VP", src, n), c, op)
     cp(A("PC", 0, 5), A("VP", 2, 5))
-    K, G16, K8, G8, E16 = (A("PC", j, 1) for j in range(5))
+    K, G16, E16, K8, G8 = (A("PC", j, 1) for j in range(5))
     ts(A("PC", 5, 1), K, 128.0, ALU.mult, G16, ALU.add)
-    ts(A("PC", 6, 1), A("PC", 5, 1), -1024.0, ALU.add)
-    ts(A("PC", 7, 1), K, 8.0, ALU.is_ge)
+    add("act", [("step", A("HI", 0, 1), K)], [K], [A("HI", 0, 1)])
+    OFF, NOFF, ZB = (A("PC", j, 1) for j in (6, 7, 8))
+    ts(A("PC", 9, 1), K, 8.0, ALU.is_ge, -2308.0, ALU.mult)
+    for o, c, d in ((OFF, 1.0, 1028.0), (NOFF, -1.0, -1028.0), (ZB, 0.5, 513.75)):
+        conv(o, A("PC", 9, 1), "const", d, c)
     ts(A("VR", 16, 16), A("VR", 16, 16), K8, ALU.add)
     ts(A("VR", 0, 32), A("VR", 0, 32), 15, ALU.bitwise_and)
     ts(A("SC", 0, 16), A("VR", 0, 16), G16, ALU.add)
-    ts(A("SC", 16, 16), A("VR", 16, 16), E16, ALU.add)
-    ts(A("SC", 32, 16), A("VR", 16, 16), 8.0, ALU.mult, G8, ALU.add)
-    ts(A("BT", 0, 5), A("VR", 16, 5), -256.0, ALU.mult)
+    ts(A("SC", 16, 16), A("VR", 16, 16), 8.0, ALU.mult, G8, ALU.add)
 
     def where(o, tab, s, c):
         ts(o, tab, s, ALU.is_equal, c, ALU.mult)
 
+    ms(A("E", 0, 768, 2), 0.0)
     where(C["B"], CG, G16, 1.0)
     where(C["KO"], CG, A("PC", 5, 1), HUGE)
-    for k, c in (("cP", 2.0 ** 17), ("cN", -2.0 ** 17), ("c64", 64.0), ("c512", 512.0), ("cm16", -16.0), ("cm8", -8.0)):
-        ms(C[k], c)
-    for k, j, c in (("P0", 0, 1.0), ("La", 0, 2080.0), ("Lb", 0, 3232.0), ("P5", 5, 1.0), ("P6", 6, 1.0), ("P10", 10, 1.0),
-                    ("P15", 15, 1.0), ("P4", 4, 1.0), ("K16", 16, 2 * BIG), ("nK6", 22, -BIG), ("nK11", 27, -BIG),
-                    ("KN", 31, HUGE), ("KL", 20, HUGE), ("K5", 37, BIG), ("K10", 42, BIG)):
+    for k, c in (("ch", -2.0 ** -8), ("cP", 3 * 2.0 ** 16), ("cN", -3 * 2.0 ** 16)):
+        conv(C[k], A("ZO1", 128, 128), "const", 0.0, c)
+    for k, j, c in (("P0", 0, 1.0), ("P5", 5, 1.0), ("P1", 1, 1.0), ("P6", 6, 1.0), ("P11", 11, 1.0), ("P13", 13, 1.0), ("P2", 2, 1.0),
+                    ("KR", 12, HUGE), ("K5", 21, BIG), ("K10", 26, BIG)):
         where(C[k], COL, A("SC", j, 1), c)
     where(C["nX"], CX, A("PC", 5, 1), -1.0)
-    where(C["KE"], CG, A("PC", 6, 1), HUGE)
-    where(C["Bb"], CG, E16, 1.0)
-    where(A("Z1", 0, 56), A("TAB", 384, 56), G16, 1.0)
-    where(A("Z1", 56, 56), A("TAB", 384, 56), G16, -1.0)
-    PBK = A("P7", 0, 128)
-    where(PBK, CG, E16, -BIG)
-    tt(PBK, C["K16"], PBK, ALU.add)
-    for t in range(NV):
-        act(A("TS", 128 * t, 128), A("ORD", 16 - t, 128), ACT.Sigmoid, bias=A("BT", t, 1), scale=256.0)
-        tt(A("T", 128 * t, 128), A("TS", 128 * t, 128), PBK, ALU.mult)
-    for k, a, c in (("nB", "B", -1.0), ("nKO", "KO", -1.0), ("nI", "P0", -1.0), ("nK0", "K16", -0.5), ("X4", "K16", 0.25),
-                    ("nK16", "K16", -1.0), ("B2k", "B", 2048.0), ("nKN", "KN", -1.0), ("nKL", "KL", -1.0), ("nKE", "KE", -1.0),
-                    ("nP15", "P15", -1.0), ("nP4", "P4", -1.0), ("Q15", "P15", 32.0), ("Q4", "P4", 32.0)):
+    where(C["nBx"], C8, G8, -1.0)
+    where(C["KS"], CG, E16, HUGE)
+    where(A("Z1", 0, 56), A("TAB", 512, 56), G16, 1.0)
+    conv(A("Z1", 56, 56), A("Z1", 0, 56), "const", 0.0, -1.0)
+    conv(A("C16", 0, 512), A("C16", 512, 512), "wide", 0.0, -1.0)
+    conv(A("CB", 384, 384), A("CB", 0, 384), "wide", 0.0, -1.0)
+    for k, a, c in (("La0", "P0", 2080.0), ("Lb", "P0", 3232.0), ("T", "KS", -BIG / HUGE), ("B2k", "B", 2048.0)):
         conv(C[k], C[a], "const", 0.0, c)
-    conv(I32m, C["P0"], "const")
-    for k, a, b in (("Da", "P10", "P5"), ("Db", "P15", "P10"), ("Dc", "P4", "P15")):
-        tt(C[k], C[a], C[b], ALU.subtract)
-    ms(A("CN", 0, 128), -1086.0)
-    for k, c in (("Ib", 1.0), ("KB", HUGE), ("nKB", -HUGE), ("nIb", -1.0)):
-        sel(C[k], A("ZO1", 0, 128), [[-1, 128]], ALU.not_equal, c, 0, 1)
+    if par["plin"]:
+        conv(A("C16", C["nBl"][1], 256), A("C16", C["nB"][1], 256), "wide", 0.0, 2080.0)
+        conv(A("C16", C["nLa0"][1], 384), A("C16", C["nP0"][1], 384), "wide", 0.0, 2080.0)
+        conv(C["La5"], C["P5"], "const", 0.0, 2080.0)
+    tt(A("C16", C["D1"][1], 256), A("C16", C["P0"][1], 256), A("C16", C["P11"][1], 256), ALU.subtract)
+    where(C["nOf"], COL, A("SC", 0, 1), NOFF)
+    back = [[1, 8], [8, 16]]
+    sel(C["T"], C["T"], back, ALU.is_gt, 0.0, 0, -1)
+    sel(C["T"], C["T"], back, ALU.not_equal, BIG / 2, 0, -1)
+    iota(A("XT", 0, PAD), [[0, PAD]], 0, 0)
+    for k, c in (("KB", HUGE), ("nKB", -HUGE), ("Ib", 1.0), ("Q0", 32.0)):
+        sel(C[k], ZERO, [[-1, 128]], ALU.not_equal, c, 0, 1)
     for k in ("K5", "K10"):
         sel(C[k], C[k], [[-1, 128]], ALU.not_equal, BIG, 0, 1)
-    iota(A("XT", 8192, 16), [[0, 16]], 0, 0)
+    for k, c in (("KN", HUGE), ("nKN", -HUGE), ("Xa", BIG + 4096), ("Xb", BIG), ("Xc", BIG - 4096 + PAD), ("Xd", BIG + PAD)):
+        sel(C[k], ZERO, back, ALU.not_equal, c, 0, -1)
+    for k, r in (("X11", 11), ("X6", 6)):
+        sel(C[k], ZERO, back, ALU.not_equal, BIG, 8 * r, -1)
+        sel(C[k], C[k], back, ALU.not_equal, BIG, 8 * r - 128, -1)
+    for k, r in (("Odd", 0), ("Even", 8)):
+        sel(C[k], ZERO, [[16, 8], [0, 16]], ALU.not_equal, 1.0, r, -1)
+    for k, c in (("cm64", -64), ("c512", 512), ("cm16", -16)):
+        iota(C[k], [[0, 128]], c, 0)
     iota(A("RS", 0, 16 * par["sch"]), [[0, par["sch"]], [256, 16]], 0, 0)
-    iota(A("U", 0, 512), [[0, 512]], 0, 0)
-    XW, XZ = ("XT", 0, 4096, 1), ("XT", 0, 8208, 1)
+    iota(A("U", 0, 256, 2), [[0, 256]], 0, 0)
+    iota(A("IA", 3, 256, 4), [[0, 256]], 0, 0)
 
     ts(A("HO", 256, 1), A("TH", 0, 1), -2048.0, ALU.add)
-    for l0, n in zip(first_lane, lanes):
+    for l0, n in cuts:
+        conv(A("ZZ", l0, n), A("ZS", l0, n), "const", OFF)
+        conv(A("E", 1025 + 2 * l0, n, 2), A("GT", l0, n), "const", -2048.0)
+        conv(A("HT", 2 * l0, n, 2), A("HN", l0, n), "const", 1184.0)
+        conv(A("HT", 2 * l0 + 1, n, 2), A("HN", l0, n), "const", -2048.0 * 2080.0, 2080.0)
         conv(A("HO", l0, n), A("HN", l0, n), "const", -2048.0)
-        conv(A("GI", 3 * l0, n), A("ZS", l0, n), "const", 1024.0)
-        conv(A("GI", 3 * l0 + n, n), A("GT", l0, n), "const", -2048.0)
-        conv(A("W", 4 * l0, 4 * n), A("QS", 4 * l0, 4 * n), "const", -2048.0)
-
-    def thresholds(a, n, o):
-        mm([(o, C["nX"], A("HO", 272 * a + 256, n, 272))], True)
-        ts(A("THS", a, n), o, -256.0, ALU.mult, 2048 * 256.0 - 128.0, ALU.add)
-        ts(A("THS", 8 + a, n), o, -1.0, ALU.mult, 2048.0, ALU.add)
-
-    def turn_names(d, o):
-        mm([(o, C["P15"], A("HO", 272 * (d - 1), 257))], True)
-        conv(A("HO", 272 * d, 257), o, "turn")
-        if d < NR:
-            send(A("HI", 256 * d, 256), A("HO", 272 * d, 256), "h%d" % d, d)
-        else:
-            thresholds(1, NV - 1, part(o, 0, NV - 1))
-
-    thresholds(0, 1, A("P6", 0, 1))
+    for l0, n in zip(first_lane, lanes):
+        conv(A("WU", 4 * l0, 4 * n), A("QS", 4 * l0, 4 * n), "const", -2048.0)
+    o = A("P6", 0, 1)
+    mm([(o, C["nX"], A("HO", 256, 1))], True)
+    ts(A("THS", 0, 1), o, -256.0, ALU.mult, 2048 * 256.0 - 128.0, ALU.add)
+    ts(A("THS", 1, 1), o, -1.0, ALU.mult, 2048.0, ALU.add)
+    rest = SLOT - HALF
+    n = 4 * lanes[0]
+    i = send([(A("WU", 1024, n), A("WU", 0, n), "w0", NR - 1)])
+    ops[i]["once"] = True
+    i = send([(A("HB", HALF, rest), A("XT", HALF, rest), "hb", None)], after=[i])
+    i = send([(A("XT", SLOT, HALF), A("XT", 0, HALF), "xa1", NR - 1)], after=[i])
+    i = send([(A("HB", 0, HALF), A("XT", 0, HALF), "ha", None)], after=[i])
+    i = send([(A("WU", 1024 + n, 1024 - n), A("WU", n, 1024 - n), "w1", NR - 1)], after=[i])
+    i = send([(A("THS", 4 * d, 2), A("THS", 0, 2), "th%d" % d, NR - d) for d in range(1, NR)], after=[i])
+    send([(A("WB", 0, 1024), A("WU", 0, 1024), "v1", NR - 2)], after=[i])
+    i = send([(A("XT", SLOT + HALF, rest), A("HB", HALF, rest), "xb1", NR - 1)], "help")
+    for d in (2, 3):
+        i = send([(A("XT", SLOT * d, SLOT), A("HB", 0, SLOT), "x%d" % d, NR - d)], "help", after=[i])
 
     for t in range(NV):
+        x0 = SLOT * (t % NR)
+        XW, XZ = ("XT", x0 + PAD, x0 + SLOT, 1), ("XT", x0, x0 + SLOT, 1)
+        more = t < NV - 1
         for s, (l0, LN) in enumerate(zip(first_lane, lanes)):
             cur[0] = s
             c0 = 16 * l0
@@ -250,95 +281,107 @@ def build(par):
                 return [(sum(ws[:j]), w) for j, w in enumerate(ws)]
 
             ONE = A("ZO1", 128, LN)
-            H = A("HI", 256 * t + l0, LN) if t % NR else A("HO", 272 * t + l0, LN)
-            i0, o0 = 768 * t + 3 * l0, 1536 * t + 6 * l0
-            Z, G, CNT = (A("GI", i0 + LN * j, LN) for j in range(3))
-            ZO, GO, CO, USED = (A("OUT", o0 + LN * j, LN) for j in range(4))
-            RF = A("OUT", o0 + 4 * LN, 2 * LN)
-            R, F = both(RF)
+            H, Z, ZO = A("HO", l0, LN), A("ZZ", 256 * t + l0, LN), A("ZZ", 256 * (t + 1) + l0, LN)
+            ZG = A("E", 1024 + 2 * l0, 2 * LN)
+            G = both(ZG)[1]
+            o0 = 1280 * t + 5 * l0
+            CO = A("OUT", o0, LN)
+            RF = A("E", 4 * l0 + 1, 2 * LN, 2)
+            R, F = halves(RF)
             Ms = [A("M", 3 * l0 + LN * k, LN) for k in range(NS)]
-            ACs = [A("AC", 2 * l0 + LN * k, LN) for k in range(NS - 1)]
-            IB, IC = A("IB", l0, LN), A("IC", 2 * l0, 2 * LN)
-            Q = [A("W", 4 * l0 + 2 * LN * b, 2 * LN) for b in range(2)]
+            W = A("WU", 1024 * t + 4 * l0, 4 * LN)
+            Q = [both(q) for q in halves(W)]
             PAR, U = A("PAR", 256 * t + l0, LN), A("U", 2 * l0, 2 * LN)
-            N, Dr = pr("N", 0, 2 * LN), pr("D", 0, 2 * LN)
-            mm([(pr("xa"), C["P0"], H), (pr("xa"), C["Lb"], ONE), (pr("xa", LN), C["La"], H)], True)
-            index(A("OX", l0, LN), IB, G, pr("xa"), pr("xa", LN))
+            N = pr("N", 0, 2 * LN, 2)
+            index(A("OX", l0, LN), A("IB", l0, LN), A("IX", 2 * l0, 2 * LN), ZG, A("HT", 2 * l0, 2 * LN), t >= par["pool"][0])
             for a, n in pieces(par["xs"]):
                 w = XW + (A("OX", l0 + a, n),)
                 either("x", ("gat", A("X", c0 + 16 * a, 16 * n), w), [w], [A("X", c0 + 16 * a, 16 * n)])
-            p = pr("par")
-            mm([(N, C["P0"], Q[0]), (N, C["nI"], Q[1])], True)
-            mm([(p, C["B"], Z), (p, C["cP"], ONE), (p, C["cN"], ONE), (p, C["nB"], Z)], True)
-            ts(PAR, p, 0.0, ALU.is_equal, A("PC", 7, 1), ALU.is_equal)
-            mm([x for o in both(N) for x in drop(o, "KO", PAR)] + [(N, C["P0"], Q[1])])
+            p, r = pr("par"), "P%d" % min(t, 1)
+            plin, LIN, la = par["plin"], pr("N", 1, LN, 2), "La%d" % min(t, 1)
+            lift = [(N, C["Lb"], A("ZO1", 128, 2 * LN))]
+            mm([(o, C[w + r], Q[b][j]) for j, o in enumerate(halves(N)) for b, w in enumerate(("", "n"))]
+               + [(LIN, C[w + la], Q[b][0]) for b, w in enumerate(("", "n")) if 0 in plin], True)
+            mm([(p, C["ch"], ONE), (p, C["B"], Z), (p, C["cP"], ONE), (p, C["cN"], ONE), (p, C["nB"], Z)], True)
+            conv(PAR, p, "PAR", A("HI", 0, 1))
+            mm([x for o in halves(N) for x in drop(o, "KO", PAR)] + [(o, C[r], Q[1][j]) for j, o in enumerate(halves(N))]
+               + (drop(LIN, "KO", PAR) + [(LIN, C[la], Q[1][0])] + lift if 0 in plin else []))
             for k in range(NS):
-                lin, c, mc, P2, IA = pr("lin"), pr("c"), pr("mc"), pr("P2", 0, 2 * LN), A("IA", 2 * l0 + LN * (k % 2), LN)
-                conv(RF, N, "RF")
-                mm([(lin, C["La"], R), (lin, C["Lb"], F)], True)
-                index(A("OY", l0, LN), IA, F, both(N)[0], lin)
-                if t == s == 0 and k < 2:
-                    for d in (1, 2):
-                        turn_names(d + 2 * k, A("P1", 0, 257))
-                rot = C["P5" if k < NS - 1 else "P0"]
-                mm(([(c, C["nX"], CNT if t else A("ZO1", 0, LN))] if t or not k else [])
+                c, P2, Dr, last = pr("c"), pr("P2", 0, 2 * LN), pr("D", 0, 2 * LN), k == NS - 1
+                rot = C["P0" if last else "P5"]
+                conv(RF, N, "RF", -3232.0 if k in plin else 0.0)
+                if k not in plin:
+                    mm([(LIN, C["La0"], R), (LIN, C["Lb"], F)], True)
+                index(A("OY", l0, LN), A("IA", 4 * l0 + k, LN, 4), A("IY", 2 * l0, 2 * LN), A("E", 4 * l0 + 2 * LN, 2 * LN),
+                      pr("N", 0, 2 * LN), t > 0 and k in par["pool"][2])
+                mm(([(c, C["nBx"], A("OUT", o0 - 1280, LN))] if t else [] if k else [(c, C["B"], A("ZO1", 0, LN))])
                    + [(c, C["K%d" % (5 * (k - j))], Ms[j]) for j in range(k)], True)
-                ways = par["modes"][k]
-                for (mode, _), (a, n) in zip(ways, pieces([w for _, w in ways])):
+                for a, n in pieces(par["ys"]):
                     x, d, ab = (A(nm, c0 + 16 * a, 16 * n) for nm in ("X", "D", "AB"))
-                    y, pd = XW + (A("OY", l0 + a, n),), pr("pd", 0, 16 * n)
-                    if mode in "dD":
-                        add("act" if mode == "d" else "dve", [("gy", d, y, x)], [y, x], [d], free=True)
-                        i = len(ops) - 1
-                        mm([(pd, C["nIb"], x)], True)
-                        mm([(pd, C["Ib"], d)])
-                        only(i, "act", i + 1, i + 2)
-                        add("act", [("ab", ab, d, pd, i)], [d, pd], [ab])
-                    else:
-                        tt(d, y, x, ALU.subtract)
-                        add("act" if mode == "a" else "dve", [("nl", ab, d)], [d], [ab], free=par["relu"])
-                    for src, z in ([] if mode in "dD" else [(d, 56)]) + [(ab, 0)]:
-                        mm([(pr("c", a, n) + (32 * (j // 4),), A("Z1", z + 24 - 8 * (j % 4), 32), part(src, j, n, 16)) for j in range(16)])
-                    if mode in "ar":
-                        only(len(ops) - 3, "dve", len(ops) - 2)
-                mm([(pr("P2"), C["P0"], H), (pr("P2", LN), C["P0"], R)]
-                   + ([(mc, I32m, ACs[k - 1]), (mc, C["X4"], Ms[k - 1])] if k else [(mc, C["c64"], ONE)]), True)
-                M, Tt = Ms[k], A("T", 128 * t, 128)
-                either("M", ("mt", M, c, A("THS", t, 1), A("THS", 8 + t, 1)), [c, A("THS", t, 1), A("THS", 8 + t, 1)], [M])
-                mm([(pr("P2", LN * hf), Tt, M) for hf in range(2)] + [(mc, C["nK16"], M)])
-                mm([(Dr, rot, RF)] + ([] if k else [(pr("u"), C["B"], Z)]), True)
-                fH, fR = A("F2", 2 * l0, LN), A("F2", 2 * l0 + LN, LN)
+                    tt(d, XW + (A("OY", l0 + a, n),), x, ALU.subtract)
+                    i = add("dve" if (k, a) in par["rdve"] else "act", [("nl", ab, d)], [d], [ab], free=True)
+                    for src, z in ((d, 56), (ab, 0)):
+                        j = mm([(pr("c", a, n) + (32 * (j // 4),), A("Z1", z + 24 - 8 * (j % 4), 32), part(src, j, n, 16))
+                                for j in range(16)])
+                        if z:
+                            ops[i]["link"], ops[j]["only"] = (j,), (i, "dve")
+                mm([(o, C["P0"], m) for o, m in zip(halves(P2), (H, R))], True)
+                M, th = Ms[k], [A("THS", 4 * (t % NR) + j, 1) for j in range(2)]
+                either("M", ("mt", M, c, th[0], th[1]), [c] + th, [M])
+                mm([(o, C["T"], M) for o in halves(P2)])
+                soon = t in par["soon"]
+
+                def matched():
+                    AC = A("AC", 4 * l0, 4 * LN)
+                    scan(AC, pr("mc", 0, 4 * LN), A("IA", 4 * l0, 4 * LN), ALU.add, ALU.max)
+                    cast(A("OM", l0, LN), part(AC, 3, LN, 4), t >= par["pool"][1])
+
+                if not (last and soon):
+                    mm([(Dr, rot, RF)] + ([] if k else [(pr("u"), C["B"], Z)]), True)
+                if last:
+                    mm([(pr("mc", 0, 4 * LN), C["cm64"], A("ZO1", 128, 4 * LN))]
+                       + [(pr("mc", j, LN, 4), C["X" + w], Ms[i])
+                          for j, w, i in ((1, "a", 0), (2, "b", 0), (2, "a", 1), (3, "c", 0), (3, "c", 1), (3, "d", 2))], soon)
+                    if soon:
+                        matched()
+                        mm([(Dr, rot, RF)], True)
+                fH, fR = halves(A("F2", 2 * l0, 2 * LN))
                 ts(A("F2", 2 * l0, 2 * LN), P2, -4096.0, ALU.add, -2048.0, ALU.max)
-                tt(ACs[k] if k < NS - 1 else A("OM", l0, LN), IA, mc, ALU.max)
-                mm([(o, C["nB"], fR) for o in both(Dr)])
-                mm([(o, w, m) for w, m in ((C["B"], fH), (C["nB"], fR)) for o in both(N)], True)
+                mm([(o, C["nB"], fR) for o in halves(Dr)])
+                nz = 3 if t else 1
+                if last:
+                    N = pr("N", nz * LN, 2 * LN)
+                mm([(o, w, m) for w, m in ((C["B"], fH), (C["nB"], fR)) for o in halves(N)]
+                   + ([(LIN, C["Bl"], fH), (LIN, C["nBl"], fR)] if k + 1 in plin else []), True)
+                if last:
+                    before = A("PAR", 256 * (t - 1) + l0, LN)
+                    mm([(pr("N"), C["Ib"], m) for m in Ms]
+                       + [(pr("N", LN * (1 + b)), C[w], m) for b in range(nz - 1)
+                          for w, m in zip(("Xb", "X11", "X6", ("Odd", "Even")[b]), Ms + [before])])
                 DD = A("DD", 2 * l0, 2 * LN)
                 conv(DD, Dr, "DD", -30720.0)
                 if k == 0:
-                    conv(both(U)[1], pr("u"), "U", -16352.0)
-                if k == NS - 1:
-                    mm([(pr("cu"), C["Bb"], m) for m in Ms]
-                       + ([(pr("cu", LN), C[nk], m) for nk, m in zip(("nK0", "nK11", "nK6"), Ms)] if t else []), True)
-                mm(drop(N, "KB", DD) + [(N, rot, RF)])
-            conv(RF, N, "RF")
-            more = t < NV - 1
-            nz = 2 * LN if t else LN
-            conv(A("OUT", CO[1], nz), pr("cu", 0, nz), "CU")
+                    conv(both(U)[1], pr("u"), "U", 2048.0)
+                if last and not soon:
+                    matched()
+                mm(drop(N, "KB", DD) + [(N, rot, RF)]
+                   + (drop(LIN, "KB", halves(DD)[0]) + [(LIN, C["La5"], R)] + lift if k + 1 in plin else []))
+            conv(A("OUT", o0, (nz + 2) * LN), pr("N", 0, (nz + 2) * LN), "CU")
+            R, F = halves(A("OUT", o0 + nz * LN, 2 * LN))
             if t > 0:
-                BK = A("BK", i0, 3 * LN)
-                send(BK, A("OUT", USED[1], 3 * LN), "b%d%d" % (t, s), NR - 1)
+                BK = A("BK", 1024 * (t - 1) + 4 * l0, 4 * LN)
+                send([(BK, A("OUT", o0 + LN, 4 * LN), "b%d%d" % (t, s), NR - 2 if more else NR - 1)])
             fs, fl = both(pr("ft", 0, 2 * LN))
-            kn, turn = ("KN", ("Q15", "nP15", "Db", "Da", "P5")) if more else ("KL", ("Q4", "nP4", "Dc", "Db", "P10"))
-            mm([(fl, C[turn[0]], G), (fl, C["c512"], ONE)] + [x for m in Ms for x in drop(fl, kn, m)]
-               + [(fl, C["B2k"], Z), (fl, C["B2k"], A("CN", 0, LN)), (fs, C["cm16"], ONE)], True)
-            mm([x for w, m in zip(turn[1:], Ms[::-1]) for x in [(fs, C[w], F)] + drop(fs, kn, m)] + [(fs, C[turn[4]], F)])
+            mm([(fl, C["Q0"], G), (fl, C["c512"], ONE)] + drop(fl, "KN", CO)
+               + [(fl, C["B2k"], Z), (fs, C["cm16"], ONE)], True)
+            mm([x for w, m in zip(("nP0", "D1", "D2"), Ms[::-1]) for x in [(fs, C[w], F)] + drop(fs, "KN", m)] + [(fs, C["P6"], F)])
+            IC, IG = A("IC", 2 * l0, 2 * LN), A("IG", l0, LN)
             scan(IC, U, pr("ft", 0, 2 * LN), ALU.mult, ALU.add)
-            ts(IB, both(IC)[1], 5, ALU.arith_shift_right, 4095, ALU.bitwise_and)
+            ts(IG, both(IC)[1], 5, ALU.arith_shift_right, 4095, ALU.bitwise_and)
             if more:
-                conv(GO, IB, "GO", -2048.0)
-                send(A("GI", G[1] + 768, 2 * LN), A("OUT", GO[1], 2 * LN), "g%d%d" % (t, s), 1)
+                conv(G, IG, "GO", -2048.0)
             else:
-                conv(A("GL", l0, LN), IB, "GO")
+                conv(A("GL", l0, LN), IG, "GO")
                 dma(A("yg", l0, LN), A("GL", l0, LN), "sg%d" % s, 512 * LN)
             for a, n in pieces(par["ts"]):
                 w = XZ + (A("OM", l0 + a, n),)
@@ -347,27 +390,29 @@ def build(par):
                 n = 16 * min(par["sch"], LN - a)
                 scan(A("AB", c0 + 16 * a, n), A("RS", 0, n), A("D", c0 + 16 * a, n), ALU.min, ALU.max)
             pz = pr("pz")
-            mm([(pz, C["P0"], Z), (pz, C["cm8"], ONE)] + drop(pz, "KB", CO) + [(pz, C["P0"], Z)], True)
+            mm([(pz, C["P0"], Z), (pz, C["nOf"], ONE)] + drop(pz, "KS", CO) + [(pz, C["P0"], Z)], True)
             mm([(pz, C["Ib"], A("AB", c0 + 15, LN, 16))])
-            conv(ZO, pz, "ZO", 511.75, 0.5)
-            if more:
-                send(A("GI", Z[1] + 768, LN), ZO, "z%d%d" % (t, s), 1)
-            else:
-                conv(A("ZF", l0, LN), ZO, "ZF", -1024.0)
+            conv(ZO, pz, "ZO", ZB, 0.5)
+            if not more:
+                conv(A("ZF", l0, LN), ZO, "ZF", NOFF)
                 dma(A("yz", l0, LN), A("ZF", l0, LN), "sz%d" % s, 512 * LN)
             if t > 0:
-                before, mg = A("PAR", 256 * (t - 1) + l0, LN), [pr("mg", 2 * LN * b, 2 * LN) for b in range(2)]
-                mm([(o, C["nI"], q) for o, q in zip(mg, Q)], True)
-                for o, q, kp in zip(mg, Q, ("KO", "KE")):
-                    mm([(o, C["P6"], part(BK, LN, 2 * LN))]
-                       + [x for h in both(o) for x in drop(h, kp, before) + drop(h, "KB", part(BK, 0, LN))]
-                       + ([] if more else [(o, C["P0"], q)]))
+                base = A("WB", 1024 * (t - 1) + 4 * l0, 4 * LN) if more else W
+                pw, pn, kd = ("P1", "P6", "KB") if more else ("P13", "P2", "KR")
+                mg = pr("mg", 0, 4 * LN)
+                mm([(mg, C["n" + pw], base)], True)
+                for b, (o, q) in enumerate(zip(halves(mg), halves(base))):
+                    mm([(h, C[pn], part(BK, LN * (2 + j), LN)) for j, h in enumerate(both(o))]
+                       + [x for h in both(o) for x in drop(h, kd, part(BK, LN * b, LN))] + [(o, C[pw], q)])
                 if more:
-                    tt(A("W", 4 * l0, 4 * LN), A("W", 4 * l0, 4 * LN), pr("mg", 0, 4 * LN), ALU.add)
+                    conv(A("WU", 1024 * (t + 1) + 4 * l0, 4 * LN), mg, "W")
+                    if t < NV - 2 and s == len(lanes) - 1:
+                        send([(A("WB", 1024 * t, 1024), A("WU", 1024 * (t + 1), 1024), "v%d" % (t + 1), NR - 1)])
                 else:
-                    conv(A("WF", 4 * l0, 4 * LN), pr("mg", 0, 4 * LN), "W", 2048.0)
+                    conv(A("WF", 4 * l0, 4 * LN), mg, "W", 2048.0)
                     for b in range(2):
-                        dma(A("yq", 512 * b + 2 * l0, 2 * LN), A("WF", 4 * l0 + 2 * LN * b, 2 * LN), "sq%d%d" % (s, b), 1024 * LN)
+                        dma(A("yq", 512 * b + 2 * l0, 2 * LN), A("WF", 4 * l0 + 2 * LN * b, 2 * LN), "sq%d%d" % (s, b), 1024 * LN,
+                            "act" if b and s >= par["late"] else "sp")
     closed = set()
     for o in reversed(ops):
         if o["eng"] == "pe":
@@ -379,22 +424,21 @@ def build(par):
     return ops
 
 
-def size(ap):
-    return 2 if ap[0] in SB and SB[ap[0]][1] in (BF, U16, F16) else 4
-
-
 def cost(op, eng, C):
     cy, i = 0.83 * C["f"], op["ins"][0]
     k = i[0]
     if k == "mm":
-        return sum(max(min(64, width(j[2])), width(j[3])) * (4 if size(j[3]) == 4 else 1) for j in op["ins"]) * C["pe"] * C["f"] + 20, 0
+        return sum(max(min(64, width(j[2])), width(j[3])) * (4 if size(j[3]) == 4 else 1) for j in op["ins"]) * C["pe"] * C["f"] + 15, 0
     if k == "dma":
-        return (100 if eng == "sp" else 1500), 2000
+        return (C["once"] if eng == "pool" else C["dge"]), 2000
     if k == "send":
-        return C["iss"], C["net"]
+        way = sum(128 * width(j[1]) * size(j[1]) for j in op["ins"]) / C["link" if i[4] else "bw"]
+        return (C["iss"] + way, C["net"]) if eng == "help" else (C["iss"] * len(op["ins"]) + C["once"] * ("once" in op), C["net"] + way)
+    if k in ("land", "step"):
+        return (1.0 if k == "land" else 1500.0), 0
     n = width(i[1])
     if k in ("iota", "sel"):
-        return 150 + 2 * n * cy, 0
+        return 200 + 2 * n * cy, 0
     aps = [x for x in i[1:] if is_ap(x) and (x[4] or width(x) > 1 or n == 1)]
     if any(x[4] for x in aps):
         return (50 if eng == "dve" else 65) + C["gc"] * n * cy, 0
@@ -453,80 +497,123 @@ def topo_order(n, pred, key):
 
 def schedule(ops, par, C):
     n = len(ops)
-    engs = [o["eng"] for o in ops]
-    dur, lat, cum = [0.0] * n, [0.0] * n, 0.0
+    need, last, done = [], {}, []
     for i, o in enumerate(ops):
-        dur[i], lat[i] = cost(o, engs[i], C)
-        if "only" in o and engs[o["only"][0]] != o["only"][1]:
-            dur[i] = 0.0
-        if o["ins"][0][0] == "dma":
-            cum = (cum if o["st"] < 0 else 0.0) + o["nbytes"] / C["bw"]
-            lat[i] += cum if o["nbytes"] else 0.0
-    pred, succ = [], []
+        firm = o["deps"] | {d for d in o["order"] if not ops[d]["sem"]}
+        below = 0
+        for d in firm:
+            below |= done[d]
+        done.append(below | sum(1 << d for d in firm))
+        need.append(([d for d in o["deps"] if not below >> d & 1], [d for d in o["order"] if not below >> d & 1]))
+        if o["nbytes"] and o["st"] < 0:
+            need[i][1].extend(last.get(o["eng"], []))
+            last[o["eng"]] = [i]
+    known = {}
 
-    def edges():
-        pred[:], succ[:] = [[] for _ in range(n + 1)], [[] for _ in range(n + 1)]
-        last = None
+    def graph(engs, j):
+        C = suits[j]
+        dur, lat, cum = [0.0] * n + [1.0], [0.0] * n, 0.0
+        pred, succ = [[] for _ in range(n + 1)], [[] for _ in range(n + 1)]
         for i, o in enumerate(ops):
-            e = [(d, lat[d] + (C["hop"] if ops[d]["sem"] or engs[d] != engs[i] else 0 if engs[i] == "pe" else C["same"])) for d in o["deps"]]
-            e += [(d, 0.0) for d in o["order"]]
-            if engs[i] == "sp" and o["st"] < 0:
-                e += [(last, 0.0)] if last is not None else []
-                last = i
+            if (i, engs[i], j) not in known:
+                known[i, engs[i], j] = cost(o, engs[i], C)
+            dur[i], lat[i] = known[i, engs[i], j]
+            if "only" in o and engs[o["only"][0]] != o["only"][1]:
+                dur[i] = 0.0
+            if o["nbytes"]:
+                cum = (cum if o["st"] < 0 else 0.0) + o["nbytes"] / C["bw"]
+                lat[i] += cum
+            e = [(d, lat[d] + (C["hop"] if ops[d]["sem"] or engs[d] != engs[i] else 0 if engs[i] == "pe" else C["same"]))
+                 for d in need[i][0]] + [(d, 0.0) for d in need[i][1]]
             for d, lag in e:
                 pred[i].append((d, lag))
                 succ[d].append((i, lag))
-            pred[n].append((i, lat[i]))
-            succ[i].append((n, lat[i]))
+        for i in range(n):
+            if lat[i] or not succ[i]:
+                pred[n].append((i, lat[i]))
+                succ[i].append((n, lat[i]))
+        return dur, pred, succ
 
-    edges()
-    dur, engs = dur + [1.0], engs + ["end"]
+    def worth(seq, engs):
+        total = 0.0
+        for j in list(range(par["suits"])) + [-1] * par["mid"]:
+            dur, pred, _ = graph(engs, j)
+            st, free = [0.0] * (n + 1), {}
+            for i in seq:
+                st[i] = max([st[d] + dur[d] + lag for d, lag in pred[i]] + [free.get(engs[i], 0.0)])
+                free[engs[i]] = st[i] + dur[i]
+            total += st[n] / suits[j]["f"]
+        return total
+
     rng = np.random.default_rng(par["seed"])
-    pr = [0.0] * (n + 1)
-    for i in range(n - 1, -1, -1):
-        pr[i] = dur[i] + max(pr[j] + lag for j, lag in succ[i])
-    key = [-pr[i] + (par["lead"][max(ops[i]["st"], 0)] if i < n else 0) for i in range(n + 1)]
+    suits = [dict(C, **{k: lo + (hi - lo) * ((j * step) % par["suits"] + 0.5) / par["suits"] for k, (lo, hi, step) in SPREAD.items()})
+             for j in range(par["suits"])] + [C]
 
-    def forth(key):
-        return place(n + 1, topo_order(n + 1, pred, key), pred, dur, engs)
+    def start(lead):
+        engs = [o["eng"] for o in ops] + ["end"]
+        dur, pred, succ = graph(engs, -1)
 
-    def back(st):
-        return place(n + 1, topo_order(n + 1, succ, [-(st[i] + dur[i]) for i in range(n + 1)]), succ, dur, engs)
+        def forth(key):
+            return place(n + 1, topo_order(n + 1, pred, key), pred, dur, engs)
 
-    def again(st):
-        bk = back(st)
-        return forth([-(bk[i] + dur[i]) for i in range(n + 1)])
+        def again(st):
+            bk = place(n + 1, topo_order(n + 1, succ, [-(st[i] + dur[i]) for i in range(n + 1)]), succ, dur, engs)
+            return forth([-(bk[i] + dur[i]) for i in range(n + 1)])
 
-    now = forth(key)
-    for _ in range(4):
-        now = again(now)
-    best = now
-    for _ in range(par["iters"]):
-        a = np.array(now)
-        near = np.abs(a - rng.random() * now[n]) < 20000.0
-        st = again(forth((a + near * rng.random(n + 1) * 3000.0 * rng.random()).tolist()))
-        if st[n] <= now[n] + 300.0 * rng.random():
-            now = st
-        if now[n] < best[n]:
-            best = now
-    best, seq = polish(ops, n + 1, pred, succ, dur, engs, best, par, C, rng)
-    order = {e: [] for e in ("pe", "dve", "act", "pool", "sp")}
+        pr = [0.0] * (n + 1)
+        for i in range(n - 1, -1, -1):
+            pr[i] = dur[i] + max(pr[j] + lag for j, lag in succ[i])
+        top = max(pr)
+        now = forth([-pr[i] + ((lead[0] + lead[1] * min(1.0, pr[i] / top / lead[2], (1.0 - pr[i] / top) / lead[2]))
+                               * max(ops[i]["st"], 0) if i < n else 0) for i in range(n + 1)])
+        for _ in range(4):
+            now = again(now)
+        best = now
+        for _ in range(par["iters"]):
+            a = np.array(now)
+            near = np.abs(a - rng.random() * now[n]) < 20000.0
+            st = again(forth((a + near * rng.random(n + 1) * 3000.0 * rng.random()).tolist()))
+            if st[n] <= now[n] + 300.0 * rng.random():
+                now = st
+            if now[n] < best[n]:
+                best = now
+        return better(engs, sorted(range(n + 1), key=lambda i: (best[i], i)), [-1])
+
+    def better(engs, seq, js):
+        st, seq = polish(ops, n + 1, [(suits[j], C["f"] / suits[j]["f"]) + graph(engs, j) for j in js], engs, seq, par, rng)
+        return worth(seq, engs), engs, st, seq
+
+    def improve(best, rounds):
+        now = best
+        for _ in range(rounds):
+            new = better(list(now[1]), list(now[3]), [-1] * (par["mid"] > 0) + rng.permutation(par["suits"])[:par["both"]].tolist())
+            if new[0] < now[0] * par["slack"]:
+                now = new
+            best = min(best, now)
+        return best
+
+    heats = sorted(start(lead) for lead in par["lead"])[:par["heats"]]
+    _, engs, st, seq = improve(min(improve(h, par["trial"]) for h in heats), par["rounds"])
+    order = {e: [] for e in ("pe", "dve", "act", "pool", "sp", "help", "nil")}
     for i in seq[:-1]:
-        if dur[i]:
+        if "only" not in ops[i] or engs[ops[i]["only"][0]] == ops[i]["only"][1]:
             order[engs[i]].append(i)
-    return order, engs[:n], best, seq[:-1]
+    return order, engs[:n], st, seq[:-1]
 
 
-def polish(ops, n, pred, succ, dur, engs, start, par, C, rng):
-    pred = [[[d, dur[d] + lag] for d, lag in p] for p in pred]
-    succ = [[[j, dur[i] + lag] for j, lag in p] for i, p in enumerate(succ)]
+def polish(ops, n, graphs, engs, order, par, rng):
     other = {"act": "dve", "dve": "act"}
-    alt = [cost(ops[i], other[engs[i]], C)[0] if i < n - 1 and ops[i]["free"] else 0.0 for i in range(n)]
-    for i in range(n - 1):
-        if "only" in ops[i]:
-            alt[i] = cost(ops[i], "pe", C)[0] - dur[i]
-    order = sorted(range(n), key=lambda i: (start[i], i))
-    mp, ms = [-1] * n, [-1] * n
+    views = []
+    for C, weight, dur, pred, succ in graphs:
+        alt = [cost(ops[i], other[engs[i]], C)[0] if i < n - 1 and ops[i]["free"] else 0.0 for i in range(n)]
+        for i in range(n - 1):
+            if "only" in ops[i]:
+                alt[i] = cost(ops[i], "pe", C)[0] - dur[i]
+        pred = [[[d, dur[d] + lag] for d, lag in p] for p in pred]
+        succ = [[[j, dur[i] + lag] for j, lag in p] for i, p in enumerate(succ)]
+        views.append((pred, succ, dur, alt, [0.0] * n, [0.0] * n, [0.0] * n, [0.0] * n, C["hop"] - C["same"], weight))
+    mp, ms, pos = [-1] * n, [-1] * n, [0] * n
+    pred0, succ0 = views[0][:2]
 
     def queues():
         last = {}
@@ -537,77 +624,78 @@ def polish(ops, n, pred, succ, dur, engs, start, par, C, rng):
             last[engs[i]] = i
 
     def turn(d, e):
-        return (C["hop"] - C["same"]) * (1 if d == e else -1) if d in other else 0.0
-
-    def shift(a, b, x):
-        for e in succ[a]:
-            if e[0] == b:
-                e[1] += x
-        for e in pred[b]:
-            if e[0] == a:
-                e[1] += x
+        return (1 if d == e else -1) if d in other else 0
 
     def flip(u):
-        for d, _ in pred[u]:
-            shift(d, u, turn(engs[d], engs[u]))
-        for j, _ in succ[u]:
-            shift(u, j, turn(engs[j], engs[u]) + alt[u] - dur[u])
+        for pred, succ, dur, alt, _, _, _, _, gap, _ in views:
+            moves = [(d, u, gap * turn(engs[d], engs[u])) for d, _ in pred[u]]
+            moves += [(u, j, gap * turn(engs[j], engs[u]) + alt[u] - dur[u]) for j, _ in succ[u]]
+            for v in ops[u].get("link", ()):
+                moves += [(v, j, alt[v] - dur[v]) for j, _ in succ[v]]
+                dur[v], alt[v] = alt[v], dur[v]
+            dur[u], alt[u] = alt[u], dur[u]
+            for a, b, x in moves:
+                for e in succ[a]:
+                    if e[0] == b:
+                        e[1] += x
+                for e in pred[b]:
+                    if e[0] == a:
+                        e[1] += x
         engs[u] = other[engs[u]]
-        dur[u], alt[u] = alt[u], dur[u]
-        for v in ops[u].get("link", ()):
-            for j, _ in succ[v]:
-                shift(v, j, alt[v] - dur[v])
-            dur[v], alt[v] = alt[v], dur[v]
-
-    head, tail, jh, jt, pos = [0.0] * n, [0.0] * n, [0.0] * n, [0.0] * n, [0] * n
 
     def heads(seq):
-        for i in seq:
-            t = 0.0
-            for d, w in pred[i]:
-                x = head[d] + w
-                if x > t:
-                    t = x
-            jh[i] = t
-            d = mp[i]
-            if d >= 0:
-                x = head[d] + dur[d]
-                if x > t:
-                    t = x
-            head[i] = t
+        for pred, _, dur, _, head, _, jh, _, _, _ in views:
+            for i in seq:
+                t = 0.0
+                for d, w in pred[i]:
+                    x = head[d] + w
+                    if x > t:
+                        t = x
+                jh[i] = t
+                d = mp[i]
+                if d >= 0:
+                    x = head[d] + dur[d]
+                    if x > t:
+                        t = x
+                head[i] = t
 
     def tails(seq):
-        for i in seq:
-            t = 0.0
-            for d, w in succ[i]:
-                x = tail[d] + w
-                if x > t:
-                    t = x
-            jt[i] = t
-            d = ms[i]
-            if d >= 0:
-                x = tail[d] + dur[i]
-                if x > t:
-                    t = x
-            tail[i] = t
+        for _, succ, dur, _, _, tail, _, jt, _, _ in views:
+            for i in seq:
+                t = 0.0
+                for d, w in succ[i]:
+                    x = tail[d] + w
+                    if x > t:
+                        t = x
+                jt[i] = t
+                d = ms[i]
+                if d >= 0:
+                    x = tail[d] + dur[i]
+                    if x > t:
+                        t = x
+                tail[i] = t
 
-    def guess(seq, a, b):
-        t = head[a] + dur[a] if a >= 0 else 0.0
-        hs = []
-        for i in seq:
-            if jh[i] > t:
-                t = jh[i]
-            hs.append(t)
-            t += dur[i]
-        t, top = tail[b] if b >= 0 else 0.0, 0.0
-        for k in range(len(seq) - 1, -1, -1):
-            i = seq[k]
-            t += dur[i]
-            if jt[i] > t:
-                t = jt[i]
-            if t + hs[k] > top:
-                top = t + hs[k]
-        return top
+    def guess(seq, a, b, u, v, mks):
+        total = 0.0
+        for (_, _, dur, _, head, tail, jh, jt, _, weight), mk in zip(views, mks):
+            t = head[a] + dur[a] if a >= 0 else 0.0
+            hs = []
+            for i in seq:
+                if jh[i] > t:
+                    t = jh[i]
+                hs.append(t)
+                t += dur[i]
+            t = tail[b] if b >= 0 else 0.0
+            top = 0.0 if head[u] + tail[u] > mk - 0.01 or head[v] + tail[v] > mk - 0.01 else mk
+            for k in range(len(seq) - 1, -1, -1):
+                i = seq[k]
+                t += dur[i]
+                if jt[i] > t:
+                    t = jt[i]
+                if t + hs[k] > top:
+                    top = t + hs[k]
+            total += weight * top
+        return total
 
     def link(seq, p, q):
         for i in seq:
@@ -624,28 +712,41 @@ def polish(ops, n, pred, succ, dur, engs, start, par, C, rng):
         inside = set(win)
         for k, i in enumerate(win):
             pos[i] = k
-        mk = best = max(head[i] + tail[i] for i in win)
+
+        def spans():
+            mks = [max([w[4][i] + w[5][i] for i in win]) for w in views]
+            return mks, sum(m * w[9] for m, w in zip(mks, views))
+
+        mks, best = spans()
         keep = (list(win), [engs[i] for i in win])
         tabu, idle, reach = {}, 0, par["reach"]
         for it in range(par["moves"]):
-            lim = mk - 0.01
-            runs, seen, top = [], set(), None
+            top = None
+            _, _, dur, alt, head, tail, _, _, _, _ = views[it % len(views)]
+            lim = mks[it % len(views)] - 0.01
+            runs, seen = [], set()
             for i in win:
-                if alt[i] and head[i] + tail[i] > lim and engs[i] in other and tabu.get(i, -1) <= it and rng.random() < par["flip"]:
+                if head[i] + tail[i] <= lim:
+                    continue
+                if alt[i] and engs[i] in other and tabu.get(i, -1) <= it and rng.random() < par["flip"]:
                     e2, k = other[engs[i]], pos[i] - 1
                     while k >= 0 and engs[win[k]] != e2:
                         k -= 1
                     if k >= 0:
                         p = win[k]
                         q = ms[p]
-                        e = max([head[d] + w + turn(engs[d], engs[i]) for d, w in pred[i]] + [head[p] + dur[p]]) + alt[i] + max(
-                            [tail[j] + w - dur[i] + turn(engs[j], engs[i]) for j, w in succ[i]] + [tail[q] if q >= 0 else 0.0])
-                        for v in ops[i].get("link", ()):
-                            e = max(e, head[v] + tail[v] + alt[v] - dur[v])
-                        e += par["toll"] * (alt[i] if e2 == "dve" else -dur[i])
+                        e = 0.0
+                        for (pred, succ, du, al, he, ta, _, _, gap, weight), mk in zip(views, mks):
+                            x = max([he[d] + w + gap * turn(engs[d], engs[i]) for d, w in pred[i]] + [he[p] + du[p]]) + al[i] + max(
+                                [ta[j] + w - du[i] + gap * turn(engs[j], engs[i]) for j, w in succ[i]] + [ta[q] if q >= 0 else 0.0])
+                            for v in ops[i].get("link", ()):
+                                x = max(x, he[v] + ta[v] + al[v] - du[v])
+                            if he[i] + ta[i] < mk - 0.01:
+                                x = max(x, mk)
+                            e += weight * (x + par["toll"] * (al[i] if e2 == "dve" else -du[i]))
                         if top is None or e < top[0]:
                             top = (e, 2, i, p, q)
-                if head[i] + tail[i] > lim and i not in seen:
+                if i not in seen:
                     run, j = [i], ms[i]
                     while j in inside and head[j] + tail[j] > lim and head[j] < head[run[-1]] + dur[run[-1]] + 0.01:
                         run.append(j)
@@ -659,22 +760,25 @@ def polish(ops, n, pred, succ, dur, engs, start, par, C, rng):
                     u, v = run[x], run[y]
                     for late in ((0,) if y == x + 1 else (0, 1)):
                         if late:
-                            if any(d == v or tail[d] > tail[v] for d, _ in succ[u]):
+                            if any(d == v or tail[d] > tail[v] for d, _ in succ0[u]):
                                 continue
                             seq = run[x + 1:y + 1] + [u]
                             bad = any(tabu.get((w, u), -1) > it for w in seq)
                         else:
-                            if any(d == u or head[d] >= head[u] + dur[u] for d, _ in pred[v]):
+                            if any(d == u or head[d] >= head[u] + dur[u] for d, _ in pred0[v]):
                                 continue
                             seq = [v] + run[x:y]
                             bad = any(tabu.get((v, w), -1) > it for w in seq)
-                        e = guess(seq, mp[u], ms[v])
+                        e = guess(seq, mp[u], ms[v], u, v, mks)
                         if bad and e >= best - 0.01:
                             e += 1e6
                         if top is None or e < top[0]:
                             top = (e, late, u, v, seq)
             if top is None:
-                break
+                idle += 50
+                if idle > par["idle"]:
+                    break
+                continue
             _, late, u, v, seq = top
             ten = it + par["ten"] + int(rng.random() * par["ten"])
             if late == 2:
@@ -696,14 +800,14 @@ def polish(ops, n, pred, succ, dur, engs, start, par, C, rng):
                 tabu.update({(u, w): ten for w in seq[:-1]})
                 mark = {u}
                 for i in seg:
-                    if mp[i] in mark or any(d in mark for d, _ in pred[i]):
+                    if mp[i] in mark or any(d in mark for d, _ in pred0[i]):
                         mark.add(i)
                 seg = [i for i in seg if i not in mark] + [i for i in seg if i in mark]
             else:
                 tabu.update({(w, v): ten for w in seq[1:]})
                 mark = {v}
                 for i in reversed(seg):
-                    if ms[i] in mark or any(d in mark for d, _ in succ[i]):
+                    if ms[i] in mark or any(d in mark for d, _ in succ0[i]):
                         mark.add(i)
                 seg = [i for i in seg if i in mark] + [i for i in seg if i not in mark]
             win[lo:hi] = seg
@@ -711,10 +815,10 @@ def polish(ops, n, pred, succ, dur, engs, start, par, C, rng):
                 pos[win[k]] = k
             heads(win[lo:])
             tails(win[hi - 1::-1])
-            mk = max(head[i] + tail[i] for i in win)
+            mks, now = spans()
             idle += 1
-            if mk < best - 0.01:
-                best, idle = mk, 0
+            if now < best - 0.01:
+                best, idle = now, 0
                 keep = (list(win), [engs[i] for i in win])
             if idle > par["idle"]:
                 break
@@ -725,14 +829,14 @@ def polish(ops, n, pred, succ, dur, engs, start, par, C, rng):
         queues()
 
     queues()
-    for _ in range(par["passes"]):
-        a = 0
-        while a < n - 20:
-            heads(order)
-            order.sort(key=lambda i: head[i])
-            tails(order[::-1])
-            window(a, min(n, a + par["span"]))
-            a += int(par["span"] * (0.3 + 0.4 * rng.random()))
+    head = views[0][4]
+    a = 0
+    while a < n - 20:
+        heads(order)
+        order.sort(key=lambda i: head[i])
+        tails(order[::-1])
+        window(a, min(n, a + par["span"]))
+        a += int(par["span"] * (0.3 + 0.4 * rng.random()))
     heads(order)
     order.sort(key=lambda i: head[i])
     return head, order
@@ -744,10 +848,21 @@ SEMAPHORES = ["pe", "dve", "act", "pool", "sent"] + [o["sem"] for o in OPS if o[
 
 
 def rank_program(g, core, T, topo):
-    rank = T.rank_of(core)
-    if rank is None:
-        return
-    q = dict(pe=g.tensor, dve=g.vector, act=g.scalar, pool=g, sp=g.sync)
+    def helper(r):
+        c = T.cores[r]
+        return [h for h in topo.cores_of(c) if topo.die(h) != topo.die(c) and T.rank_of(h) is None
+                and all(topo.may_write(h, d) for d in T.cores if d != c)][0]
+
+    def way(far, r, j=0):
+        peer, moves, by = far
+        src = T.cores[r] if by == "pool" else helper(r)
+        if peer is None:
+            out = topo.engines(src, T.cores[(r + 1) % NR])
+            return src, helper(r), [e for e in topo.engines(src, helper(r)) if e not in out]
+        dst = T.cores[(r + peer) % NR]
+        es = topo.engines(src, dst)
+        n = 1 << (len(es) // moves).bit_length() - 1
+        return src, dst, es[n * j:n * (j + 1)]
 
     def ap(x):
         if not is_ap(x):
@@ -756,21 +871,45 @@ def rank_program(g, core, T, topo):
         v = T[x[0]][rows, x[1]:x[2]:x[3]] if x[3] > 1 else T[x[0]][rows, x[1]:x[2]]
         return v.indirect(ap(x[4])) if x[4] else v
 
-    def engines(o, src_rank):
-        return len(topo.engines(T.cores[src_rank % NR], T.cores[(src_rank + o["peer"]) % NR]))
+    def remote(o, r):
+        moves = []
+        for j, (_, out, src, sem, peer) in enumerate(o["ins"]):
+            _, dst, es = way((peer,) + o["far"][1:], r, j)
+            moves.append((ap(out), ap(src), T.sem[sem], topo.addr(dst), sum(1 << e for e in es), len(es)))
+        if len(moves) == 1:
+            out, src, sem, (rid, pid, _), mask, _ = moves[0]
+            g.remote_dma(out, src, sem, T.sem["sent"], pid, rid, mask)
+        else:
+            g.remote_dma_fused([RemoteDMATransfer(dst_ids=[DstId(rid=rid, pnc=pid)], dma_engine_mask=mask, remote_sem=sem, src=src, dst=out)
+                                for out, src, sem, (rid, pid, _), mask, _ in moves], local_sem=T.sem["sent"])
+        return sum(m[5] for m in moves)
 
+    rank = T.rank_of(core)
+    if rank is None:
+        for r in range(NR):
+            if core == helper(r):
+                sent = 0
+                for i in ORDER["help"]:
+                    for d in sorted(OPS[i]["deps"]):
+                        g.wait_ge(T.sem[OPS[d]["sem"]], len(way(OPS[d]["far"], r)[2]))
+                    sent += remote(OPS[i], r)
+                    g.wait_ge(T.sem["sent"], sent)
+        return
+    q = dict(pe=g.tensor, dve=g.vector, act=g.scalar, pool=g, sp=g.sync)
     live = {i for l in ORDER.values() for i in l}
     deps = {i: [d for d in OPS[i]["deps"] if d in live and not (ENGS[d] == "pe" and ENGS[i] == "pe")] for i in live}
-    needed = {d for l in deps.values() for d in l}
+    needed = {d for i, l in deps.items() for d in l if ENGS[i] in q}
     place_of = {i: k for k, i in enumerate(SEQ)}
     mark, total = {}, {}
     for e, l in ORDER.items():
         for i in l:
             o = OPS[i]
             if o["sem"]:
-                n = engines(o, rank - o["peer"]) if o["peer"] else 16
+                far = o["far"]
+                n = len(way(far, (rank - (far[0] or 0)) % NR)[2]) if far else 16
                 mark[i] = (o["sem"], n)
-                total[o["sem"]] = n
+                if not far or far[0]:
+                    total[o["sem"]] = n
             elif i in needed:
                 total[e] = total.get(e, 0) + 1
                 mark[i] = (e, total[e])
@@ -778,19 +917,22 @@ def rank_program(g, core, T, topo):
     for i in sorted(live, key=place_of.get):
         e = ENGS[i]
         waits[i] = []
-        for d in sorted(deps[i], key=lambda d: -place_of[d]):
+        for d in sorted(deps[i] if e in q else [], key=lambda d: -place_of[d]):
             if seen[e].get(mark[d][0], 0) < mark[d][1]:
                 waits[i].append(mark[d])
                 for sm, n in knew[d].items():
                     seen[e][sm] = max(seen[e].get(sm, 0), n)
         if i in mark:
-            knew[i] = dict({} if OPS[i]["peer"] else seen[e], **{mark[i][0]: mark[i][1]})
+            knew[i] = dict({} if OPS[i]["far"] else seen[e], **{mark[i][0]: mark[i][1]})
     sent = 0
-    for e, l in ORDER.items():
-        for i in l:
+    for e in q:
+        for i in ORDER[e]:
             o = OPS[i]
             for sm, n in waits[i]:
                 q[e].wait_ge(T.sem[sm], n)
+            if o["far"]:
+                sent += remote(o, rank)
+                continue
             for j in o["ins"]:
                 k, x = j[0], [ap(y) for y in j[1:]]
                 if k == "mm":
@@ -803,23 +945,19 @@ def rank_program(g, core, T, topo):
                     r = g.vector.tensor_copy(*x)
                 elif k == "gat":
                     r = g.scalar.activation(x[0], x[1], ACT.Copy)
-                elif k == "gy" and e == "act":
-                    r = g.scalar.activation(x[0], x[1], ACT.Copy)
-                elif k == "gy":
-                    r = g.vector.tensor_tensor(x[0], x[1], x[2], ALU.subtract)
-                elif k == "ab":
-                    r = g.scalar.activation(x[0], x[2 if ENGS[x[3]] == "act" else 1], ACT.Abs)
                 elif k == "nl" and e == "act":
                     r = g.scalar.activation(x[0], x[1], ACT.Abs)
                 elif k == "nl":
                     r = g.vector.tensor_scalar(x[0], x[1], 0.0, 2.0, ALU.max, ALU.mult)
+                elif k == "step":
+                    r = g.scalar.activation(x[0], x[1], ACT.Sigmoid, bias=-7.5 * 256.0, scale=256.0)
                 elif k == "mt" and e == "act":
                     r = g.scalar.activation(x[0], x[1], ACT.Sigmoid, bias=x[2], scale=-256.0)
                 elif k == "mt":
                     r = g.vector.tensor_scalar(x[0], x[1], x[3], None, ALU.is_lt)
                 elif k == "cv" and e == "act":
                     r = g.scalar.activation(x[0], x[1], ACT.Identity, bias=x[2], scale=x[3])
-                elif k == "cv" and x[2:4] == [0.0, 1.0]:
+                elif k == "cv" and j[3:5] == (0.0, 1.0):
                     r = g.vector.tensor_copy(x[0], x[1])
                 elif k == "cv":
                     r = g.vector.tensor_scalar(x[0], x[1], x[3], x[2], ALU.mult, ALU.add)
@@ -827,13 +965,6 @@ def rank_program(g, core, T, topo):
                     r = g.vector.memset(*x)
                 elif k == "scan":
                     r = g.vector.tensor_tensor_scan(x[0], x[1], x[2], 0.0, x[3], x[4])
-                elif k == "act":
-                    kw = {}
-                    if j[4] != 0.0:
-                        kw["bias"] = x[3]
-                    if j[5] != 1.0:
-                        kw["scale"] = x[4]
-                    r = g.scalar.activation(x[0], x[1], x[2], **kw)
                 elif k == "iota":
                     if SB[j[1][0]][1] == I32:
                         r = g.iota(*x)
@@ -841,18 +972,11 @@ def rank_program(g, core, T, topo):
                         r = g.iota(*x, allow_small_or_imprecise_dtypes=True)
                 elif k == "sel":
                     r = g.affine_select(*x)
-                elif k == "dma":
-                    if e == "pool":
-                        r = g.dma_start(x[0], T.th[:], allow_slow_non_contiguous=True)
-                    else:
-                        r = q[e].dma_start(x[0], x[1])
+                elif e == "pool":
+                    r = g.dma_start(x[0], T.th[:], allow_slow_non_contiguous=True)
                 else:
-                    dst = T.cores[(rank + o["peer"]) % NR]
-                    rid, pid = topo.addr(dst)[:2]
-                    g.remote_dma(x[0], x[1], T.sem[o["sem"]], T.sem["sent"], pid, rid, topo.mask(core, dst))
-                    sent += engines(o, rank)
-                    r = None
-            if r is not None and i in mark:
+                    r = q[e].dma_start(x[0], x[1])
+            if i in mark:
                 r.then_inc(T.sem[mark[i][0]], 16 if o["sem"] else 1)
     total["sent"] = sent
     for sm in sorted(total):

import numpy as np
from concourse.bass import DstId, RemoteDMATransfer
from concourse.mybir import AluOpType as ALU, ActivationFunctionType as ACT

NR, NV, NS = 4, 5, 3
F32, BF, I32, U16, F16 = "float32", "bfloat16", "int32", "uint16", "float16"
PAD, SLOT, HALF = 64, 4160, 1600
M16 = ("nB", "nP1", "nP13", "nP0", "B", "P1", "P13", "P0", "P11", "P6", "D1", "D2", "P5", "P2", "La0", "Lb", "B2k", "nX", "nBx", "nOf",
       "nBl", "nLa1", "nLa0", "Bl", "La1", "La5")
MBF = ("KO", "KS", "KR", "nKO", "nKS", "nKR", "KN", "nKN", "KB", "nKB", "X11", "X6", "K5", "K10", "T", "Ib", "Q0", "Odd", "Even",
       "Xa", "Xb", "Xc", "Xd", "cP", "cN", "ch", "c512", "cm16", "cm64")
SB = {
    "XT": (NR * SLOT, BF), "HB": (SLOT, BF), "HN": (256, I32), "GT": (256, I32), "ZS": (256, I32), "QS": (1024, I32), "TH": (4, I32),
    "HO": (272, F16), "HT": (512, F32), "THS": (16, F32), "ZZ": (6 * 256, F16), "E": (1536, F16), "OUT": (5 * 1280, F16),
    "BK": (4 * 1024, F16), "WU": (5 * 1024, F16), "WB": (3 * 1024, F16), "GL": (256, F32), "ZF": (256, F32), "WF": (1024, F32),
    "X": (4096, BF), "D": (4096, BF), "AB": (4096, BF), "OX": (256, U16), "OY": (256, U16), "OM": (256, U16),
    "IX": (512, I32), "IY": (512, I32), "IC": (512, I32), "IB": (256, I32), "IG": (256, I32), "IA": (1024, I32), "AC": (1024, I32),
    "M": (768, BF), "F2": (512, F16), "DD": (512, BF), "PAR": (5 * 256, BF), "U": (512, F32),
    "VP": (8, I32), "VR": (32, I32), "PC": (16, F32), "SC": (48, F32), "TAB": (568, BF),
    "C16": (128 * len(M16), F16), "CB": (128 * len(MBF), BF), "Z1": (112, BF), "RS": (1024, BF), "ZO1": (384, BF),
    "HI": (8, BF),
}
SCRATCH = {k: ("sbuf", [128, n], d) for k, (n, d) in SB.items()}
for _b in range(8):
    SCRATCH["P%d" % _b] = ("psum", [128, 512], F32)
BIG, HUGE = 8192.0, 2.0 ** 50
REG = dict(c=(0, 0), D=(0, 0), u=(0, 2), mc=(0, 2), ft=(0, 0), pz=(0, 0), par=(0, 0), P2=(1, 0), N=(1, 0), mg=(1, 0))

PARAMS = dict(lanes=(64, 64, 64, 64), ys=(32, 32), xs=(32, 32), ts=(32, 32), sch=64, rdve=((0, 32),), pool=(1, 0, ()), plin=(), soon=(0,), dve=("GO", "wide"),
              early=2, eq=1, late=2,
              lead=((2000, 2500, 0.15), (2500, 2000, 0.12), (2200, 2200, 0.15), (2800, 1800, 0.12)),
              seed=4, iters=4, heats=2, trial=2, rounds=36, suits=7, both=2, mid=1, slack=1.002,
              flip=0.15, toll=0.6, span=130, moves=500, idle=170, ten=8, reach=6)
COST = dict(f=1.1, gc=1.56, pe=0.49, ov=60.0, hop=200.0, same=110.0, net=4000.0, iss=800.0, bw=260.0, link=70.0, once=2200.0, dge=200.0)
SPREAD = dict(gc=(1.04, 2.08, 1), f=(1.0, 1.4, 3), hop=(120.0, 260.0, 2), same=(60.0, 130.0, 2), pe=(0.42, 0.56, 5), ov=(45.0, 75.0, 4),
              iss=(500.0, 1300.0, 6), net=(2500.0, 5000.0, 4), bw=(160.0, 360.0, 5), link=(35.0, 100.0, 3))


def A(name, a, n, step=1, ind=None):
    return (name, a, a + (n - 1) * step + 1, step, ind)


def part(ap, a, n, step=1):
    return A(ap[0], ap[1] + a * ap[3], n, ap[3] * step)


def is_ap(x):
    return isinstance(x, tuple)


def width(ap):
    return 16 * (ap[4][2] - ap[4][1]) if ap[4] else (ap[2] - ap[1] - 1) // ap[3] + 1


def size(ap):
    return 2 if ap[0] in SB and SB[ap[0]][1] in (BF, U16, F16) else 4


def build(par):
    ops = []
    hist = {}
    bank = {}
    cur = [-1]
    lanes = par["lanes"]
    first_lane = [sum(lanes[:s]) for s in range(len(lanes))]

    def add(eng, ins, reads, writes, sem=None, far=None, nbytes=0, free=False, after=()):
        i = len(ops)
        deps, order = set(), set(after)
        rd = [r for r in reads if is_ap(r)]
        rd += [r[4] for r in rd + writes if r[4]]
        who = i if free else eng
        for lst, w in ((rd, False), (writes, True)):
            for ap in lst:
                nm = ap[0]
                if nm not in SB:
                    if nm[0] != "P":
                        continue
                    st = bank.setdefault(nm, [None, [], []])
                    if st[0] != who:
                        st[0], st[1], st[2] = who, [], st[1]
                    deps.update(st[2])
                    if eng == "pe":
                        order.update(st[1][-1:])
                    if i not in st[1]:
                        st[1].append(i)
                    if eng == "pe":
                        continue
                h = hist.setdefault(nm, [])
                keep = []
                for e in h:
                    hit = e[1] < ap[2] and ap[1] < e[2]
                    if hit and (w or e[3]):
                        deps.add(e[0])
                    if not (w and ap[1] <= e[1] and e[2] <= ap[2]):
                        keep.append(e)
                keep.append((i, ap[1], ap[2], w))
                hist[nm] = keep
        deps.discard(i)
        order.discard(i)
        ops.append(dict(eng=eng, ins=ins, deps=deps, order=order - deps, sem=sem, far=far, nbytes=nbytes, st=cur[0], free=free))
        return i

    def tt(o, a, b, op): add("dve", [("tt", o, a, b, op)], [a, b], [o])
    def ts(o, a, s1, op0, s2=None, op1=None): add("dve", [("ts", o, a, s1, s2, op0, op1)], [a, s1, s2], [o])
    def cp(o, a): add("dve", [("cp", o, a)], [a], [o])
    def ms(o, c): add("dve", [("ms", o, c)], [], [o])
    def scan(o, a, b, op0, op1): add("dve", [("scan", o, a, b, op0, op1)], [a, b], [o])
    def iota(o, pat, base, cm): return add("pool", [("iota", o, pat, base, cm)], [], [o])
    def sel(o, a, pat, op, fill, base, cm): add("pool", [("sel", o, a, pat, op, fill, base, cm)], [a], [o])
    def dma(o, a, sem, nbytes, eng="sp", after=()): add(eng, [("dma", o, a)], [a], [o], sem=sem, nbytes=nbytes, after=after)

    def send(moves, by="pool", after=()):
        ins = [("send",) + m for m in moves]
        i = add(by, ins, [m[1] for m in moves], [moves[0][0]], sem=moves[0][2], far=(moves[0][3], len(moves), by), after=after)
        for m in moves[1:]:
            j = add("nil", [("land", m[0])], [], [m[0]], sem=m[2], far=(m[3], len(moves), by))
            ops[j]["deps"].add(i)
        return i

    def mm(terms, first=False):
        ins = [("mm", o, l, r, first and j == 0, False) for j, (o, l, r) in enumerate(terms)]
        return add("pe", ins, [x for t in terms for x in t[1:]], [t[0] for t in terms])

    def either(tag, ins, reads, writes): return add("dve" if tag in par["dve"] else "act", [ins], reads, writes, free=True)

    def conv(o, a, tag, bias=0.0, scale=1.0):
        either(tag, ("cv", o, a, bias, scale), [a, bias], [o])

    def cast(o, a, pool):
        if pool:
            sel(o, a, [[0, width(o)]], ALU.is_ge, 0.0, 0, 0)
        else:
            conv(o, a, o[0])

    def index(o, whole, pairs, zb, al, pool):
        scan(pairs, zb, al, ALU.mult, ALU.add)
        ts(whole, both(pairs)[1], 5, ALU.arith_shift_right, 4095, ALU.bitwise_and)
        cast(o, whole, pool)

    def drop(o, name, mask):
        return [(o, C[name], mask), (o, C["n" + name], mask)]

    def both(o): return [part(o, hf, width(o) // 2, 2) for hf in range(2)]
    def halves(o): return [part(o, hf * width(o) // 2, width(o) // 2) for hf in range(2)]

    def load(src, s):
        l0, n = (0, 0) if src == "xt" else (first_lane[s], lanes[s])
        if src == "qs":
            for b in range(2):
                dma(A("QS", 4 * l0 + 2 * n * b, 2 * n), A("qs", 512 * b + 2 * l0, 2 * n), "lq%d%d" % (s, b), 1024 * n,
                    "act" if s < par["eq"] else "sp")
        elif src == "xt":
            a, n = (0, HALF - PAD) if s else (HALF - PAD, SLOT - HALF)
            dma(A("XT", PAD + a, n), A("xt", a, n), "lx%d" % s, 256 * n)
        else:
            l0, n = cuts[s]
            dma(A(src.upper(), l0, n), A(src, l0, n), "l%s%d" % (src, s), 512 * n)

    early = par["early"]
    cuts = [(0, sum(lanes[:early])), (sum(lanes[:early]), sum(lanes[early:]))][:1 + (early < len(lanes))]
    for src, s in ([("zs", 0), ("hn", 0), ("gt", 0)] + [("qs", s) for s in range(par["eq"])] + [("xt", 0), ("xt", 1)]
                   + [(src, 1) for src in ("zs", "hn", "gt") if len(cuts) > 1] + [("qs", s) for s in range(par["eq"], len(lanes))]):
        load(src, s)
    COL, CG, CX, C8 = (A("TAB", 128 * j, 128) for j in range(4))
    ZERO = A("ZO1", 0, 128)
    soon = [iota(A("VP", 0, 1), [[0, 1]], 0, 1), iota(A("VP", 1, 1), [[0, 1]], 0, 16), iota(A("VR", 0, 16), [[-1, 16]], 16, 1),
            iota(A("VR", 16, 16), [[-1, 16]], 16, 0), iota(CG, [[16, 8], [0, 16]], 0, 0), iota(COL, [[1, 128]], 0, 0)]
    dma(A("TH", 0, 1), A("th", 0, 1), "lth", 0, "pool", soon)
    iota(ZERO, [[0, 128]], 0, 0)
    ms(A("ZO1", 128, 256), 1.0)
    iota(CX, [[16, 128]], 0, 0)
    iota(C8, [[0, 16], [1, 8]], 0, 0)
    iota(A("TAB", 512, 56), [[16, 56]], -384, 0)
    C = {k: A("C16", 128 * j, 128) for j, k in enumerate(M16)}
    C.update({k: A("CB", 128 * j, 128) for j, k in enumerate(MBF)})
    for j, n, src, c, op in ((2, 1, 0, 15, ALU.bitwise_and), (3, 2, 0, 112, ALU.bitwise_and), (5, 1, 0, 3, ALU.arith_shift_right),
                             (6, 1, 0, 7, ALU.bitwise_and)):
        ts(A("VP", j, n), A("VP", src, n), c, op)
    cp(A("PC", 0, 5), A("VP", 2, 5))
    K, G16, E16, K8, G8 = (A("PC", j, 1) for j in range(5))
    ts(A("PC", 5, 1), K, 128.0, ALU.mult, G16, ALU.add)
    add("act", [("step", A("HI", 0, 1), K)], [K], [A("HI", 0, 1)])
    OFF, NOFF, ZB = (A("PC", j, 1) for j in (6, 7, 8))
    ts(A("PC", 9, 1), K, 8.0, ALU.is_ge, -2308.0, ALU.mult)
    for o, c, d in ((OFF, 1.0, 1028.0), (NOFF, -1.0, -1028.0), (ZB, 0.5, 513.75)):
        conv(o, A("PC", 9, 1), "const", d, c)
    ts(A("VR", 16, 16), A("VR", 16, 16), K8, ALU.add)
    ts(A("VR", 0, 32), A("VR", 0, 32), 15, ALU.bitwise_and)
    ts(A("SC", 0, 16), A("VR", 0, 16), G16, ALU.add)
    ts(A("SC", 16, 16), A("VR", 16, 16), 8.0, ALU.mult, G8, ALU.add)

    def where(o, tab, s, c):
        ts(o, tab, s, ALU.is_equal, c, ALU.mult)

    ms(A("E", 0, 768, 2), 0.0)
    where(C["B"], CG, G16, 1.0)
    where(C["KO"], CG, A("PC", 5, 1), HUGE)
    for k, c in (("ch", -2.0 ** -8), ("cP", 3 * 2.0 ** 16), ("cN", -3 * 2.0 ** 16)):
        conv(C[k], A("ZO1", 128, 128), "const", 0.0, c)
    for k, j, c in (("P0", 0, 1.0), ("P5", 5, 1.0), ("P1", 1, 1.0), ("P6", 6, 1.0), ("P11", 11, 1.0), ("P13", 13, 1.0), ("P2", 2, 1.0),
                    ("KR", 12, HUGE), ("K5", 21, BIG), ("K10", 26, BIG)):
        where(C[k], COL, A("SC", j, 1), c)
    where(C["nX"], CX, A("PC", 5, 1), -1.0)
    where(C["nBx"], C8, G8, -1.0)
    where(C["KS"], CG, E16, HUGE)
    where(A("Z1", 0, 56), A("TAB", 512, 56), G16, 1.0)
    conv(A("Z1", 56, 56), A("Z1", 0, 56), "const", 0.0, -1.0)
    conv(A("C16", 0, 512), A("C16", 512, 512), "wide", 0.0, -1.0)
    conv(A("CB", 384, 384), A("CB", 0, 384), "wide", 0.0, -1.0)
    for k, a, c in (("La0", "P0", 2080.0), ("Lb", "P0", 3232.0), ("T", "KS", -BIG / HUGE), ("B2k", "B", 2048.0)):
        conv(C[k], C[a], "const", 0.0, c)
    if par["plin"]:
        conv(A("C16", C["nBl"][1], 256), A("C16", C["nB"][1], 256), "wide", 0.0, 2080.0)
        conv(A("C16", C["nLa0"][1], 384), A("C16", C["nP0"][1], 384), "wide", 0.0, 2080.0)
        conv(C["La5"], C["P5"], "const", 0.0, 2080.0)
    tt(A("C16", C["D1"][1], 256), A("C16", C["P0"][1], 256), A("C16", C["P11"][1], 256), ALU.subtract)
    where(C["nOf"], COL, A("SC", 0, 1), NOFF)
    back = [[1, 8], [8, 16]]
    sel(C["T"], C["T"], back, ALU.is_gt, 0.0, 0, -1)
    sel(C["T"], C["T"], back, ALU.not_equal, BIG / 2, 0, -1)
    iota(A("XT", 0, PAD), [[0, PAD]], 0, 0)
    for k, c in (("KB", HUGE), ("nKB", -HUGE), ("Ib", 1.0), ("Q0", 32.0)):
        sel(C[k], ZERO, [[-1, 128]], ALU.not_equal, c, 0, 1)
    for k in ("K5", "K10"):
        sel(C[k], C[k], [[-1, 128]], ALU.not_equal, BIG, 0, 1)
    for k, c in (("KN", HUGE), ("nKN", -HUGE), ("Xa", BIG + 4096), ("Xb", BIG), ("Xc", BIG - 4096 + PAD), ("Xd", BIG + PAD)):
        sel(C[k], ZERO, back, ALU.not_equal, c, 0, -1)
    for k, r in (("X11", 11), ("X6", 6)):
        sel(C[k], ZERO, back, ALU.not_equal, BIG, 8 * r, -1)
        sel(C[k], C[k], back, ALU.not_equal, BIG, 8 * r - 128, -1)
    for k, r in (("Odd", 0), ("Even", 8)):
        sel(C[k], ZERO, [[16, 8], [0, 16]], ALU.not_equal, 1.0, r, -1)
    for k, c in (("cm64", -64), ("c512", 512), ("cm16", -16)):
        iota(C[k], [[0, 128]], c, 0)
    iota(A("RS", 0, 16 * par["sch"]), [[0, par["sch"]], [256, 16]], 0, 0)
    iota(A("U", 0, 256, 2), [[0, 256]], 0, 0)
    iota(A("IA", 3, 256, 4), [[0, 256]], 0, 0)

    ts(A("HO", 256, 1), A("TH", 0, 1), -2048.0, ALU.add)
    for l0, n in cuts:
        conv(A("ZZ", l0, n), A("ZS", l0, n), "const", OFF)
        conv(A("E", 1025 + 2 * l0, n, 2), A("GT", l0, n), "const", -2048.0)
        conv(A("HT", 2 * l0, n, 2), A("HN", l0, n), "const", 1184.0)
        conv(A("HT", 2 * l0 + 1, n, 2), A("HN", l0, n), "const", -2048.0 * 2080.0, 2080.0)
        conv(A("HO", l0, n), A("HN", l0, n), "const", -2048.0)
    for l0, n in zip(first_lane, lanes):
        conv(A("WU", 4 * l0, 4 * n), A("QS", 4 * l0, 4 * n), "const", -2048.0)
    o = A("P6", 0, 1)
    mm([(o, C["nX"], A("HO", 256, 1))], True)
    ts(A("THS", 0, 1), o, -256.0, ALU.mult, 2048 * 256.0 - 128.0, ALU.add)
    ts(A("THS", 1, 1), o, -1.0, ALU.mult, 2048.0, ALU.add)
    rest = SLOT - HALF
    n = 4 * lanes[0]
    i = send([(A("WU", 1024, n), A("WU", 0, n), "w0", NR - 1)])
    ops[i]["once"] = True
    i = send([(A("HB", HALF, rest), A("XT", HALF, rest), "hb", None)], after=[i])
    i = send([(A("XT", SLOT, HALF), A("XT", 0, HALF), "xa1", NR - 1)], after=[i])
    i = send([(A("HB", 0, HALF), A("XT", 0, HALF), "ha", None)], after=[i])
    i = send([(A("WU", 1024 + n, 1024 - n), A("WU", n, 1024 - n), "w1", NR - 1)], after=[i])
    i = send([(A("THS", 4 * d, 2), A("THS", 0, 2), "th%d" % d, NR - d) for d in range(1, NR)], after=[i])
    send([(A("WB", 0, 1024), A("WU", 0, 1024), "v1", NR - 2)], after=[i])
    i = send([(A("XT", SLOT + HALF, rest), A("HB", HALF, rest), "xb1", NR - 1)], "help")
    for d in (2, 3):
        i = send([(A("XT", SLOT * d, SLOT), A("HB", 0, SLOT), "x%d" % d, NR - d)], "help", after=[i])

    for t in range(NV):
        x0 = SLOT * (t % NR)
        XW, XZ = ("XT", x0 + PAD, x0 + SLOT, 1), ("XT", x0, x0 + SLOT, 1)
        more = t < NV - 1
        for s, (l0, LN) in enumerate(zip(first_lane, lanes)):
            cur[0] = s
            c0 = 16 * l0

            def pr(name, off=0, n=LN, step=1):
                bk, col = REG[name]
                return A("P%d" % (2 * s + bk), col * LN + off, n, step)

            def pieces(ws):
                ws = [w * LN // sum(ws) for w in ws]
                return [(sum(ws[:j]), w) for j, w in enumerate(ws)]

            ONE = A("ZO1", 128, LN)
            H, Z, ZO = A("HO", l0, LN), A("ZZ", 256 * t + l0, LN), A("ZZ", 256 * (t + 1) + l0, LN)
            ZG = A("E", 1024 + 2 * l0, 2 * LN)
            G = both(ZG)[1]
            o0 = 1280 * t + 5 * l0
            CO = A("OUT", o0, LN)
            RF = A("E", 4 * l0 + 1, 2 * LN, 2)
            R, F = halves(RF)
            Ms = [A("M", 3 * l0 + LN * k, LN) for k in range(NS)]
            W = A("WU", 1024 * t + 4 * l0, 4 * LN)
            Q = [both(q) for q in halves(W)]
            PAR, U = A("PAR", 256 * t + l0, LN), A("U", 2 * l0, 2 * LN)
            N = pr("N", 0, 2 * LN, 2)
            index(A("OX", l0, LN), A("IB", l0, LN), A("IX", 2 * l0, 2 * LN), ZG, A("HT", 2 * l0, 2 * LN), t >= par["pool"][0])
            for a, n in pieces(par["xs"]):
                w = XW + (A("OX", l0 + a, n),)
                either("x", ("gat", A("X", c0 + 16 * a, 16 * n), w), [w], [A("X", c0 + 16 * a, 16 * n)])
            p, r = pr("par"), "P%d" % min(t, 1)
            plin, LIN, la = par["plin"], pr("N", 1, LN, 2), "La%d" % min(t, 1)
            lift = [(N, C["Lb"], A("ZO1", 128, 2 * LN))]
            mm([(o, C[w + r], Q[b][j]) for j, o in enumerate(halves(N)) for b, w in enumerate(("", "n"))]
               + [(LIN, C[w + la], Q[b][0]) for b, w in enumerate(("", "n")) if 0 in plin], True)
            mm([(p, C["ch"], ONE), (p, C["B"], Z), (p, C["cP"], ONE), (p, C["cN"], ONE), (p, C["nB"], Z)], True)
            conv(PAR, p, "PAR", A("HI", 0, 1))
            mm([x for o in halves(N) for x in drop(o, "KO", PAR)] + [(o, C[r], Q[1][j]) for j, o in enumerate(halves(N))]
               + (drop(LIN, "KO", PAR) + [(LIN, C[la], Q[1][0])] + lift if 0 in plin else []))
            for k in range(NS):
                c, P2, Dr, last = pr("c"), pr("P2", 0, 2 * LN), pr("D", 0, 2 * LN), k == NS - 1
                rot = C["P0" if last else "P5"]
                conv(RF, N, "RF", -3232.0 if k in plin else 0.0)
                if k not in plin:
                    mm([(LIN, C["La0"], R), (LIN, C["Lb"], F)], True)
                index(A("OY", l0, LN), A("IA", 4 * l0 + k, LN, 4), A("IY", 2 * l0, 2 * LN), A("E", 4 * l0 + 2 * LN, 2 * LN),
                      pr("N", 0, 2 * LN), t > 0 and k in par["pool"][2])
                mm(([(c, C["nBx"], A("OUT", o0 - 1280, LN))] if t else [] if k else [(c, C["B"], A("ZO1", 0, LN))])
                   + [(c, C["K%d" % (5 * (k - j))], Ms[j]) for j in range(k)], True)
                for a, n in pieces(par["ys"]):
                    x, d, ab = (A(nm, c0 + 16 * a, 16 * n) for nm in ("X", "D", "AB"))
                    tt(d, XW + (A("OY", l0 + a, n),), x, ALU.subtract)
                    i = add("dve" if (k, a) in par["rdve"] else "act", [("nl", ab, d)], [d], [ab], free=True)
                    for src, z in ((d, 56), (ab, 0)):
                        j = mm([(pr("c", a, n) + (32 * (j // 4),), A("Z1", z + 24 - 8 * (j % 4), 32), part(src, j, n, 16))
                                for j in range(16)])
                        if z:
                            ops[i]["link"], ops[j]["only"] = (j,), (i, "dve")
                mm([(o, C["P0"], m) for o, m in zip(halves(P2), (H, R))], True)
                M, th = Ms[k], [A("THS", 4 * (t % NR) + j, 1) for j in range(2)]
                either("M", ("mt", M, c, th[0], th[1]), [c] + th, [M])
                mm([(o, C["T"], M) for o in halves(P2)])
                soon = t in par["soon"]

                def matched():
                    AC = A("AC", 4 * l0, 4 * LN)
                    scan(AC, pr("mc", 0, 4 * LN), A("IA", 4 * l0, 4 * LN), ALU.add, ALU.max)
                    cast(A("OM", l0, LN), part(AC, 3, LN, 4), t >= par["pool"][1])

                if not (last and soon):
                    mm([(Dr, rot, RF)] + ([] if k else [(pr("u"), C["B"], Z)]), True)
                if last:
                    mm([(pr("mc", 0, 4 * LN), C["cm64"], A("ZO1", 128, 4 * LN))]
                       + [(pr("mc", j, LN, 4), C["X" + w], Ms[i])
                          for j, w, i in ((1, "a", 0), (2, "b", 0), (2, "a", 1), (3, "c", 0), (3, "c", 1), (3, "d", 2))], soon)
                    if soon:
                        matched()
                        mm([(Dr, rot, RF)], True)
                fH, fR = halves(A("F2", 2 * l0, 2 * LN))
                ts(A("F2", 2 * l0, 2 * LN), P2, -4096.0, ALU.add, -2048.0, ALU.max)
                mm([(o, C["nB"], fR) for o in halves(Dr)])
                nz = 3 if t else 1
                if last:
                    N = pr("N", nz * LN, 2 * LN)
                mm([(o, w, m) for w, m in ((C["B"], fH), (C["nB"], fR)) for o in halves(N)]
                   + ([(LIN, C["Bl"], fH), (LIN, C["nBl"], fR)] if k + 1 in plin else []), True)
                if last:
                    before = A("PAR", 256 * (t - 1) + l0, LN)
                    mm([(pr("N"), C["Ib"], m) for m in Ms]
                       + [(pr("N", LN * (1 + b)), C[w], m) for b in range(nz - 1)
                          for w, m in zip(("Xb", "X11", "X6", ("Odd", "Even")[b]), Ms + [before])])
                DD = A("DD", 2 * l0, 2 * LN)
                conv(DD, Dr, "DD", -30720.0)
                if k == 0:
                    conv(both(U)[1], pr("u"), "U", 2048.0)
                if last and not soon:
                    matched()
                mm(drop(N, "KB", DD) + [(N, rot, RF)]
                   + (drop(LIN, "KB", halves(DD)[0]) + [(LIN, C["La5"], R)] + lift if k + 1 in plin else []))
            conv(A("OUT", o0, (nz + 2) * LN), pr("N", 0, (nz + 2) * LN), "CU")
            R, F = halves(A("OUT", o0 + nz * LN, 2 * LN))
            if t > 0:
                BK = A("BK", 1024 * (t - 1) + 4 * l0, 4 * LN)
                send([(BK, A("OUT", o0 + LN, 4 * LN), "b%d%d" % (t, s), NR - 2 if more else NR - 1)])
            fs, fl = both(pr("ft", 0, 2 * LN))
            mm([(fl, C["Q0"], G), (fl, C["c512"], ONE)] + drop(fl, "KN", CO)
               + [(fl, C["B2k"], Z), (fs, C["cm16"], ONE)], True)
            mm([x for w, m in zip(("nP0", "D1", "D2"), Ms[::-1]) for x in [(fs, C[w], F)] + drop(fs, "KN", m)] + [(fs, C["P6"], F)])
            IC, IG = A("IC", 2 * l0, 2 * LN), A("IG", l0, LN)
            scan(IC, U, pr("ft", 0, 2 * LN), ALU.mult, ALU.add)
            ts(IG, both(IC)[1], 5, ALU.arith_shift_right, 4095, ALU.bitwise_and)
            if more:
                conv(G, IG, "GO", -2048.0)
            else:
                conv(A("GL", l0, LN), IG, "GO")
                dma(A("yg", l0, LN), A("GL", l0, LN), "sg%d" % s, 512 * LN)
            for a, n in pieces(par["ts"]):
                w = XZ + (A("OM", l0 + a, n),)
                either("m", ("gat", A("D", c0 + 16 * a, 16 * n), w), [w], [A("D", c0 + 16 * a, 16 * n)])
            for a in range(0, LN, par["sch"]):
                n = 16 * min(par["sch"], LN - a)
                scan(A("AB", c0 + 16 * a, n), A("RS", 0, n), A("D", c0 + 16 * a, n), ALU.min, ALU.max)
            pz = pr("pz")
            mm([(pz, C["P0"], Z), (pz, C["nOf"], ONE)] + drop(pz, "KS", CO) + [(pz, C["P0"], Z)], True)
            mm([(pz, C["Ib"], A("AB", c0 + 15, LN, 16))])
            conv(ZO, pz, "ZO", ZB, 0.5)
            if not more:
                conv(A("ZF", l0, LN), ZO, "ZF", NOFF)
                dma(A("yz", l0, LN), A("ZF", l0, LN), "sz%d" % s, 512 * LN)
            if t > 0:
                base = A("WB", 1024 * (t - 1) + 4 * l0, 4 * LN) if more else W
                pw, pn, kd = ("P1", "P6", "KB") if more else ("P13", "P2", "KR")
                mg = pr("mg", 0, 4 * LN)
                mm([(mg, C["n" + pw], base)], True)
                for b, (o, q) in enumerate(zip(halves(mg), halves(base))):
                    mm([(h, C[pn], part(BK, LN * (2 + j), LN)) for j, h in enumerate(both(o))]
                       + [x for h in both(o) for x in drop(h, kd, part(BK, LN * b, LN))] + [(o, C[pw], q)])
                if more:
                    conv(A("WU", 1024 * (t + 1) + 4 * l0, 4 * LN), mg, "W")
                    if t < NV - 2 and s == len(lanes) - 1:
                        send([(A("WB", 1024 * t, 1024), A("WU", 1024 * (t + 1), 1024), "v%d" % (t + 1), NR - 1)])
                else:
                    conv(A("WF", 4 * l0, 4 * LN), mg, "W", 2048.0)
                    for b in range(2):
                        dma(A("yq", 512 * b + 2 * l0, 2 * LN), A("WF", 4 * l0 + 2 * LN * b, 2 * LN), "sq%d%d" % (s, b), 1024 * LN,
                            "act" if b and s >= par["late"] else "sp")
    closed = set()
    for o in reversed(ops):
        if o["eng"] == "pe":
            for j in range(len(o["ins"]) - 1, -1, -1):
                x = o["ins"][j]
                rows = {(x[1][0], r) for r in x[1][5:] or (0, 32, 64, 96)}
                o["ins"][j] = x[:5] + (not rows & closed,)
                closed = closed - rows if x[4] else closed | rows
    return ops


def cost(op, eng, C):
    cy, i = 0.83 * C["f"], op["ins"][0]
    k = i[0]
    if k == "mm":
        return sum(max(min(64, width(j[2])), width(j[3])) * (4 if size(j[3]) == 4 else 1) for j in op["ins"]) * C["pe"] * C["f"] + 15, 0
    if k == "dma":
        return (C["once"] if eng == "pool" else C["dge"]), 2000
    if k == "send":
        way = sum(128 * width(j[1]) * size(j[1]) for j in op["ins"]) / C["link" if i[4] else "bw"]
        return (C["iss"] + way, C["net"]) if eng == "help" else (C["iss"] * len(op["ins"]) + C["once"] * ("once" in op), C["net"] + way)
    if k in ("land", "step"):
        return (1.0 if k == "land" else 1500.0), 0
    n = width(i[1])
    if k in ("iota", "sel"):
        return 200 + 2 * n * cy, 0
    aps = [x for x in i[1:] if is_ap(x) and (x[4] or width(x) > 1 or n == 1)]
    if any(x[4] for x in aps):
        return (50 if eng == "dve" else 65) + C["gc"] * n * cy, 0
    if eng == "act":
        return C["ov"] + 15 + n * cy, 0
    c = 0.5 if all(size(x) == 2 for x in aps) else 1.0
    if k == "tt" and i[2][0] in SB and i[3][0] in SB:
        c = 2.0
    return C["ov"] + max(64, n * c) * cy, 0


def place(n, seq, pred, dur, engs):
    st = [0.0] * n
    line = {e: [] for e in set(engs)}
    for i in seq:
        t = 0.0
        for d, lag in pred[i]:
            x = st[d] + dur[d] + lag
            if x > t:
                t = x
        l = line[engs[i]]
        lo, hi = 0, len(l)
        while lo < hi:
            mid = (lo + hi) // 2
            if l[mid][1] <= t:
                lo = mid + 1
            else:
                hi = mid
        while lo < len(l) and l[lo][0] < t + dur[i]:
            t = max(t, l[lo][1])
            lo += 1
        l.insert(lo, (t, t + dur[i]))
        st[i] = t
    return st


def topo_order(n, pred, key):
    rank = sorted(range(n), key=lambda i: (key[i], i))
    seq, done = [], [False] * n
    for i in rank:
        stack = [i]
        while stack:
            j = stack[-1]
            if done[j]:
                stack.pop()
                continue
            todo = [d for d, _ in pred[j] if not done[d]]
            if todo:
                stack.extend(sorted(todo, key=lambda d: -key[d]))
            else:
                done[j] = True
                seq.append(j)
                stack.pop()
    return seq


def schedule(ops, par, C):
    n = len(ops)
    need, last, done = [], {}, []
    for i, o in enumerate(ops):
        firm = o["deps"] | {d for d in o["order"] if not ops[d]["sem"]}
        below = 0
        for d in firm:
            below |= done[d]
        done.append(below | sum(1 << d for d in firm))
        need.append(([d for d in o["deps"] if not below >> d & 1], [d for d in o["order"] if not below >> d & 1]))
        if o["nbytes"] and o["st"] < 0:
            need[i][1].extend(last.get(o["eng"], []))
            last[o["eng"]] = [i]
    known = {}

    def graph(engs, j):
        C = suits[j]
        dur, lat, cum = [0.0] * n + [1.0], [0.0] * n, 0.0
        pred, succ = [[] for _ in range(n + 1)], [[] for _ in range(n + 1)]
        for i, o in enumerate(ops):
            if (i, engs[i], j) not in known:
                known[i, engs[i], j] = cost(o, engs[i], C)
            dur[i], lat[i] = known[i, engs[i], j]
            if "only" in o and engs[o["only"][0]] != o["only"][1]:
                dur[i] = 0.0
            if o["nbytes"]:
                cum = (cum if o["st"] < 0 else 0.0) + o["nbytes"] / C["bw"]
                lat[i] += cum
            e = [(d, lat[d] + (C["hop"] if ops[d]["sem"] or engs[d] != engs[i] else 0 if engs[i] == "pe" else C["same"]))
                 for d in need[i][0]] + [(d, 0.0) for d in need[i][1]]
            for d, lag in e:
                pred[i].append((d, lag))
                succ[d].append((i, lag))
        for i in range(n):
            if lat[i] or not succ[i]:
                pred[n].append((i, lat[i]))
                succ[i].append((n, lat[i]))
        return dur, pred, succ

    def worth(seq, engs):
        total = 0.0
        for j in list(range(par["suits"])) + [-1] * par["mid"]:
            dur, pred, _ = graph(engs, j)
            st, free = [0.0] * (n + 1), {}
            for i in seq:
                st[i] = max([st[d] + dur[d] + lag for d, lag in pred[i]] + [free.get(engs[i], 0.0)])
                free[engs[i]] = st[i] + dur[i]
            total += st[n] / suits[j]["f"]
        return total

    rng = np.random.default_rng(par["seed"])
    suits = [dict(C, **{k: lo + (hi - lo) * ((j * step) % par["suits"] + 0.5) / par["suits"] for k, (lo, hi, step) in SPREAD.items()})
             for j in range(par["suits"])] + [C]

    def start(lead):
        engs = [o["eng"] for o in ops] + ["end"]
        dur, pred, succ = graph(engs, -1)

        def forth(key):
            return place(n + 1, topo_order(n + 1, pred, key), pred, dur, engs)

        def again(st):
            bk = place(n + 1, topo_order(n + 1, succ, [-(st[i] + dur[i]) for i in range(n + 1)]), succ, dur, engs)
            return forth([-(bk[i] + dur[i]) for i in range(n + 1)])

        pr = [0.0] * (n + 1)
        for i in range(n - 1, -1, -1):
            pr[i] = dur[i] + max(pr[j] + lag for j, lag in succ[i])
        top = max(pr)
        now = forth([-pr[i] + ((lead[0] + lead[1] * min(1.0, pr[i] / top / lead[2], (1.0 - pr[i] / top) / lead[2]))
                               * max(ops[i]["st"], 0) if i < n else 0) for i in range(n + 1)])
        for _ in range(4):
            now = again(now)
        best = now
        for _ in range(par["iters"]):
            a = np.array(now)
            near = np.abs(a - rng.random() * now[n]) < 20000.0
            st = again(forth((a + near * rng.random(n + 1) * 3000.0 * rng.random()).tolist()))
            if st[n] <= now[n] + 300.0 * rng.random():
                now = st
            if now[n] < best[n]:
                best = now
        return better(engs, sorted(range(n + 1), key=lambda i: (best[i], i)), [-1])

    def better(engs, seq, js):
        st, seq = polish(ops, n + 1, [(suits[j], C["f"] / suits[j]["f"]) + graph(engs, j) for j in js], engs, seq, par, rng)
        return worth(seq, engs), engs, st, seq

    def improve(best, rounds):
        now = best
        for _ in range(rounds):
            new = better(list(now[1]), list(now[3]), [-1] * (par["mid"] > 0) + rng.permutation(par["suits"])[:par["both"]].tolist())
            if new[0] < now[0] * par["slack"]:
                now = new
            best = min(best, now)
        return best

    heats = sorted(start(lead) for lead in par["lead"])[:par["heats"]]
    _, engs, st, seq = improve(min(improve(h, par["trial"]) for h in heats), par["rounds"])
    order = {e: [] for e in ("pe", "dve", "act", "pool", "sp", "help", "nil")}
    for i in seq[:-1]:
        if "only" not in ops[i] or engs[ops[i]["only"][0]] == ops[i]["only"][1]:
            order[engs[i]].append(i)
    return order, engs[:n], st, seq[:-1]


def polish(ops, n, graphs, engs, order, par, rng):
    other = {"act": "dve", "dve": "act"}
    views = []
    for C, weight, dur, pred, succ in graphs:
        alt = [cost(ops[i], other[engs[i]], C)[0] if i < n - 1 and ops[i]["free"] else 0.0 for i in range(n)]
        for i in range(n - 1):
            if "only" in ops[i]:
                alt[i] = cost(ops[i], "pe", C)[0] - dur[i]
        pred = [[[d, dur[d] + lag] for d, lag in p] for p in pred]
        succ = [[[j, dur[i] + lag] for j, lag in p] for i, p in enumerate(succ)]
        views.append((pred, succ, dur, alt, [0.0] * n, [0.0] * n, [0.0] * n, [0.0] * n, C["hop"] - C["same"], weight))
    mp, ms, pos = [-1] * n, [-1] * n, [0] * n
    pred0, succ0 = views[0][:2]

    def queues():
        last = {}
        for i in order:
            mp[i], ms[i] = last.get(engs[i], -1), -1
            if mp[i] >= 0:
                ms[mp[i]] = i
            last[engs[i]] = i

    def turn(d, e):
        return (1 if d == e else -1) if d in other else 0

    def flip(u):
        for pred, succ, dur, alt, _, _, _, _, gap, _ in views:
            moves = [(d, u, gap * turn(engs[d], engs[u])) for d, _ in pred[u]]
            moves += [(u, j, gap * turn(engs[j], engs[u]) + alt[u] - dur[u]) for j, _ in succ[u]]
            for v in ops[u].get("link", ()):
                moves += [(v, j, alt[v] - dur[v]) for j, _ in succ[v]]
                dur[v], alt[v] = alt[v], dur[v]
            dur[u], alt[u] = alt[u], dur[u]
            for a, b, x in moves:
                for e in succ[a]:
                    if e[0] == b:
                        e[1] += x
                for e in pred[b]:
                    if e[0] == a:
                        e[1] += x
        engs[u] = other[engs[u]]

    def heads(seq):
        for pred, _, dur, _, head, _, jh, _, _, _ in views:
            for i in seq:
                t = 0.0
                for d, w in pred[i]:
                    x = head[d] + w
                    if x > t:
                        t = x
                jh[i] = t
                d = mp[i]
                if d >= 0:
                    x = head[d] + dur[d]
                    if x > t:
                        t = x
                head[i] = t

    def tails(seq):
        for _, succ, dur, _, _, tail, _, jt, _, _ in views:
            for i in seq:
                t = 0.0
                for d, w in succ[i]:
                    x = tail[d] + w
                    if x > t:
                        t = x
                jt[i] = t
                d = ms[i]
                if d >= 0:
                    x = tail[d] + dur[i]
                    if x > t:
                        t = x
                tail[i] = t

    def guess(seq, a, b, u, v, mks):
        total = 0.0
        for (_, _, dur, _, head, tail, jh, jt, _, weight), mk in zip(views, mks):
            t = head[a] + dur[a] if a >= 0 else 0.0
            hs = []
            for i in seq:
                if jh[i] > t:
                    t = jh[i]
                hs.append(t)
                t += dur[i]
            t = tail[b] if b >= 0 else 0.0
            top = 0.0 if head[u] + tail[u] > mk - 0.01 or head[v] + tail[v] > mk - 0.01 else mk
            for k in range(len(seq) - 1, -1, -1):
                i = seq[k]
                t += dur[i]
                if jt[i] > t:
                    t = jt[i]
                if t + hs[k] > top:
                    top = t + hs[k]
            total += weight * top
        return total

    def link(seq, p, q):
        for i in seq:
            mp[i] = p
            if p >= 0:
                ms[p] = i
            p = i
        ms[p] = q
        if q >= 0:
            mp[q] = p

    def window(a, b):
        win = order[a:b]
        inside = set(win)
        for k, i in enumerate(win):
            pos[i] = k

        def spans():
            mks = [max([w[4][i] + w[5][i] for i in win]) for w in views]
            return mks, sum(m * w[9] for m, w in zip(mks, views))

        mks, best = spans()
        keep = (list(win), [engs[i] for i in win])
        tabu, idle, reach = {}, 0, par["reach"]
        for it in range(par["moves"]):
            top = None
            _, _, dur, alt, head, tail, _, _, _, _ = views[it % len(views)]
            lim = mks[it % len(views)] - 0.01
            runs, seen = [], set()
            for i in win:
                if head[i] + tail[i] <= lim:
                    continue
                if alt[i] and engs[i] in other and tabu.get(i, -1) <= it and rng.random() < par["flip"]:
                    e2, k = other[engs[i]], pos[i] - 1
                    while k >= 0 and engs[win[k]] != e2:
                        k -= 1
                    if k >= 0:
                        p = win[k]
                        q = ms[p]
                        e = 0.0
                        for (pred, succ, du, al, he, ta, _, _, gap, weight), mk in zip(views, mks):
                            x = max([he[d] + w + gap * turn(engs[d], engs[i]) for d, w in pred[i]] + [he[p] + du[p]]) + al[i] + max(
                                [ta[j] + w - du[i] + gap * turn(engs[j], engs[i]) for j, w in succ[i]] + [ta[q] if q >= 0 else 0.0])
                            for v in ops[i].get("link", ()):
                                x = max(x, he[v] + ta[v] + al[v] - du[v])
                            if he[i] + ta[i] < mk - 0.01:
                                x = max(x, mk)
                            e += weight * (x + par["toll"] * (al[i] if e2 == "dve" else -du[i]))
                        if top is None or e < top[0]:
                            top = (e, 2, i, p, q)
                if i not in seen:
                    run, j = [i], ms[i]
                    while j in inside and head[j] + tail[j] > lim and head[j] < head[run[-1]] + dur[run[-1]] + 0.01:
                        run.append(j)
                        seen.add(j)
                        j = ms[j]
                    if len(run) > 1:
                        runs.append(run)
            for run in runs:
                k = len(run)
                for x, y in sorted({(0, j) for j in range(1, min(k, reach))} | {(j, k - 1) for j in range(max(0, k - reach), k - 1)}):
                    u, v = run[x], run[y]
                    for late in ((0,) if y == x + 1 else (0, 1)):
                        if late:
                            if any(d == v or tail[d] > tail[v] for d, _ in succ0[u]):
                                continue
                            seq = run[x + 1:y + 1] + [u]
                            bad = any(tabu.get((w, u), -1) > it for w in seq)
                        else:
                            if any(d == u or head[d] >= head[u] + dur[u] for d, _ in pred0[v]):
                                continue
                            seq = [v] + run[x:y]
                            bad = any(tabu.get((v, w), -1) > it for w in seq)
                        e = guess(seq, mp[u], ms[v], u, v, mks)
                        if bad and e >= best - 0.01:
                            e += 1e6
                        if top is None or e < top[0]:
                            top = (e, late, u, v, seq)
            if top is None:
                idle += 50
                if idle > par["idle"]:
                    break
                continue
            _, late, u, v, seq = top
            ten = it + par["ten"] + int(rng.random() * par["ten"])
            if late == 2:
                if mp[u] >= 0:
                    ms[mp[u]] = ms[u]
                if ms[u] >= 0:
                    mp[ms[u]] = mp[u]
                link([u], v, seq)
                flip(u)
                tabu[u] = ten + par["ten"]
                lo, hi = 0, len(win)
            else:
                link(seq, mp[u], ms[v])
                lo, hi = pos[u], pos[v] + 1
            seg = win[lo:hi]
            if late == 2:
                pass
            elif late:
                tabu.update({(u, w): ten for w in seq[:-1]})
                mark = {u}
                for i in seg:
                    if mp[i] in mark or any(d in mark for d, _ in pred0[i]):
                        mark.add(i)
                seg = [i for i in seg if i not in mark] + [i for i in seg if i in mark]
            else:
                tabu.update({(w, v): ten for w in seq[1:]})
                mark = {v}
                for i in reversed(seg):
                    if ms[i] in mark or any(d in mark for d, _ in succ0[i]):
                        mark.add(i)
                seg = [i for i in seg if i in mark] + [i for i in seg if i not in mark]
            win[lo:hi] = seg
            for k in range(lo, hi):
                pos[win[k]] = k
            heads(win[lo:])
            tails(win[hi - 1::-1])
            mks, now = spans()
            idle += 1
            if now < best - 0.01:
                best, idle = now, 0
                keep = (list(win), [engs[i] for i in win])
            if idle > par["idle"]:
                break
        order[a:b] = keep[0]
        for i, e in zip(*keep):
            if engs[i] != e:
                flip(i)
        queues()

    queues()
    head = views[0][4]
    a = 0
    while a < n - 20:
        heads(order)
        order.sort(key=lambda i: head[i])
        tails(order[::-1])
        window(a, min(n, a + par["span"]))
        a += int(par["span"] * (0.3 + 0.4 * rng.random()))
    heads(order)
    order.sort(key=lambda i: head[i])
    return head, order


OPS = build(PARAMS)
ORDER, ENGS, _T, SEQ = schedule(OPS, PARAMS, COST)
SEMAPHORES = ["pe", "dve", "act", "pool", "sent"] + [o["sem"] for o in OPS if o["sem"]]


def rank_program(g, core, T, topo):
    def helper(r):
        c = T.cores[r]
        return [h for h in topo.cores_of(c) if topo.die(h) != topo.die(c) and T.rank_of(h) is None
                and all(topo.may_write(h, d) for d in T.cores if d != c)][0]

    def way(far, r, j=0):
        peer, moves, by = far
        src = T.cores[r] if by == "pool" else helper(r)
        if peer is None:
            out = topo.engines(src, T.cores[(r + 1) % NR])
            return src, helper(r), [e for e in topo.engines(src, helper(r)) if e not in out]
        dst = T.cores[(r + peer) % NR]
        es = topo.engines(src, dst)
        n = 1 << (len(es) // moves).bit_length() - 1
        return src, dst, es[n * j:n * (j + 1)]

    def ap(x):
        if not is_ap(x):
            return x
        rows = slice(x[5], x[5] + 32) if len(x) > 5 else slice(0, 128)
        v = T[x[0]][rows, x[1]:x[2]:x[3]] if x[3] > 1 else T[x[0]][rows, x[1]:x[2]]
        return v.indirect(ap(x[4])) if x[4] else v

    def remote(o, r):
        moves = []
        for j, (_, out, src, sem, peer) in enumerate(o["ins"]):
            _, dst, es = way((peer,) + o["far"][1:], r, j)
            moves.append((ap(out), ap(src), T.sem[sem], topo.addr(dst), sum(1 << e for e in es), len(es)))
        if len(moves) == 1:
            out, src, sem, (rid, pid, _), mask, _ = moves[0]
            g.remote_dma(out, src, sem, T.sem["sent"], pid, rid, mask)
        else:
            g.remote_dma_fused([RemoteDMATransfer(dst_ids=[DstId(rid=rid, pnc=pid)], dma_engine_mask=mask, remote_sem=sem, src=src, dst=out)
                                for out, src, sem, (rid, pid, _), mask, _ in moves], local_sem=T.sem["sent"])
        return sum(m[5] for m in moves)

    rank = T.rank_of(core)
    if rank is None:
        for r in range(NR):
            if core == helper(r):
                sent = 0
                for i in ORDER["help"]:
                    for d in sorted(OPS[i]["deps"]):
                        g.wait_ge(T.sem[OPS[d]["sem"]], len(way(OPS[d]["far"], r)[2]))
                    sent += remote(OPS[i], r)
                    g.wait_ge(T.sem["sent"], sent)
        return
    q = dict(pe=g.tensor, dve=g.vector, act=g.scalar, pool=g, sp=g.sync)
    live = {i for l in ORDER.values() for i in l}
    deps = {i: [d for d in OPS[i]["deps"] if d in live and not (ENGS[d] == "pe" and ENGS[i] == "pe")] for i in live}
    needed = {d for i, l in deps.items() for d in l if ENGS[i] in q}
    place_of = {i: k for k, i in enumerate(SEQ)}
    mark, total = {}, {}
    for e, l in ORDER.items():
        for i in l:
            o = OPS[i]
            if o["sem"]:
                far = o["far"]
                n = len(way(far, (rank - (far[0] or 0)) % NR)[2]) if far else 16
                mark[i] = (o["sem"], n)
                if not far or far[0]:
                    total[o["sem"]] = n
            elif i in needed:
                total[e] = total.get(e, 0) + 1
                mark[i] = (e, total[e])
    seen, knew, waits = {e: {} for e in ORDER}, {}, {}
    for i in sorted(live, key=place_of.get):
        e = ENGS[i]
        waits[i] = []
        for d in sorted(deps[i] if e in q else [], key=lambda d: -place_of[d]):
            if seen[e].get(mark[d][0], 0) < mark[d][1]:
                waits[i].append(mark[d])
                for sm, n in knew[d].items():
                    seen[e][sm] = max(seen[e].get(sm, 0), n)
        if i in mark:
            knew[i] = dict({} if OPS[i]["far"] else seen[e], **{mark[i][0]: mark[i][1]})
    sent = 0
    for e in q:
        for i in ORDER[e]:
            o = OPS[i]
            for sm, n in waits[i]:
                q[e].wait_ge(T.sem[sm], n)
            if o["far"]:
                sent += remote(o, rank)
                continue
            for j in o["ins"]:
                k, x = j[0], [ap(y) for y in j[1:]]
                if k == "mm":
                    r = g.tensor.matmul(*x)
                elif k == "tt":
                    r = g.vector.tensor_tensor(*x)
                elif k == "ts":
                    r = g.vector.tensor_scalar(*(x if x[5] is not None else x[:5]))
                elif k == "cp" or (k == "gat" and e == "dve"):
                    r = g.vector.tensor_copy(*x)
                elif k == "gat":
                    r = g.scalar.activation(x[0], x[1], ACT.Copy)
                elif k == "nl" and e == "act":
                    r = g.scalar.activation(x[0], x[1], ACT.Abs)
                elif k == "nl":
                    r = g.vector.tensor_scalar(x[0], x[1], 0.0, 2.0, ALU.max, ALU.mult)
                elif k == "step":
                    r = g.scalar.activation(x[0], x[1], ACT.Sigmoid, bias=-7.5 * 256.0, scale=256.0)
                elif k == "mt" and e == "act":
                    r = g.scalar.activation(x[0], x[1], ACT.Sigmoid, bias=x[2], scale=-256.0)
                elif k == "mt":
                    r = g.vector.tensor_scalar(x[0], x[1], x[3], None, ALU.is_lt)
                elif k == "cv" and e == "act":
                    r = g.scalar.activation(x[0], x[1], ACT.Identity, bias=x[2], scale=x[3])
                elif k == "cv" and j[3:5] == (0.0, 1.0):
                    r = g.vector.tensor_copy(x[0], x[1])
                elif k == "cv":
                    r = g.vector.tensor_scalar(x[0], x[1], x[3], x[2], ALU.mult, ALU.add)
                elif k == "ms":
                    r = g.vector.memset(*x)
                elif k == "scan":
                    r = g.vector.tensor_tensor_scan(x[0], x[1], x[2], 0.0, x[3], x[4])
                elif k == "iota":
                    if SB[j[1][0]][1] == I32:
                        r = g.iota(*x)
                    else:
                        r = g.iota(*x, allow_small_or_imprecise_dtypes=True)
                elif k == "sel":
                    r = g.affine_select(*x)
                elif e == "pool":
                    r = g.dma_start(x[0], T.th[:], allow_slow_non_contiguous=True)
                else:
                    r = q[e].dma_start(x[0], x[1])
            if i in mark:
                r.then_inc(T.sem[mark[i][0]], 16 if o["sem"] else 1)
    total["sent"] = sent
    for sm in sorted(total):
        g.wait_ge(T.sem[sm], total[sm])
